import numpy as np
import ml_dtypes


def mxq(x, axis, fmt="e4m3"):
    dtype, down = {"e4m3": (ml_dtypes.float8_e4m3fn, 7), "e5m2": (ml_dtypes.float8_e5m2, 14)}[fmt]
    v = np.moveaxis(np.asarray(x, np.float32).astype(ml_dtypes.bfloat16).astype(np.float64), axis, -1)
    blocks = v.reshape(v.shape[:-1] + (-1, 32))
    amax = np.abs(blocks).max(-1, keepdims=True)
    byte = np.maximum(np.where(amax > 0, np.frexp(amax)[1] - 1 + 127, 0) - down, 1)
    scale = np.exp2(byte - 127.0)
    codes = (blocks / scale).astype(np.float32).astype(dtype).astype(np.float64)
    return np.moveaxis((codes * scale).reshape(v.shape), -1, axis)


WIDE = False


def mx_kscale(k):
    if not WIDE:
        return np.ones(k)
    levels = np.array([10, -10, 5, -5, 0])
    if k % 512:
        return np.exp2(np.random.permutation(np.resize(levels, k // 32))).repeat(32)
    a = np.empty((k // 512, 16))
    for p in range(k // 512):
        a[p, :8] = np.random.permutation(np.resize(levels, 8))
        for g in range(8):
            far = levels[np.abs(levels - a[p, g]) >= 10]
            a[p, g + 8] = far[np.random.randint(len(far))]
    return np.exp2(a.ravel()).repeat(32)


BF16 = ml_dtypes.bfloat16


def bf(x):
    return np.asarray(x, np.float32).astype(BF16)


def f64(x):
    return np.asarray(x).astype(np.float64)


T, L, H, DK, DV = 2048, 512, 8, 128, 256


def draw0():
    s = mx_kscale(L)
    u = mx_kscale(T)
    r = 2.0 / T ** 0.25
    return {"c": bf(np.random.standard_normal((T, L)) * s),
            "wk": bf(np.random.standard_normal((L, H * DK)) / np.sqrt(L) / s[:, None]),
            "wv": bf(np.random.standard_normal((L, H * DV)) / np.sqrt(L) / s[:, None]),
            "keep": bf(np.random.uniform(0.5, 1.0, (T, H)) * r * u[:, None]),
            "write": bf(np.random.uniform(0.5, 1.5, (T, H)) * r / u[:, None])}


def core(c, wk, wv, keep, write):
    cq = mxq(f64(c), 1, "e4m3")
    k = np.maximum(cq @ mxq(f64(wk), 0, "e4m3"), 0.0)
    k = k.reshape(T, H, DK) * f64(keep)[:, :, None]
    v = cq @ mxq(f64(wv), 0, "e4m3")
    v = v.reshape(T, H, DV) * f64(write)[:, :, None]
    kq = mxq(k, 0, "e4m3").transpose(1, 2, 0)
    vq = mxq(v, 0, "e4m3").transpose(1, 0, 2)
    return kq @ vq


def e4m3fn_bytes(y):
    return np.clip(np.asarray(y, np.float64), -448.0, 448.0).astype(np.float32).astype(ml_dtypes.float8_e4m3fn).view(np.uint8)


def e4m3fn_values(b):
    return np.asarray(b, np.uint8).view(ml_dtypes.float8_e4m3fn).astype(np.float64)


def setup_inputs():
    d = draw0()
    x0 = np.asarray(d['wv']).astype(np.float64)
    s = (np.max(np.abs(x0), axis=(1,), keepdims=True) / 448.0).astype(np.float32)
    out = {}
    for k, v in d.items():
        if k == 'wv':
            out['wv_bytes'] = e4m3fn_bytes(x0 / s.astype(np.float64))
            out['wv_scale'] = s
        else:
            out[k] = v
    return out


def reference(c, wk, wv_bytes, wv_scale, keep, write):
    return core(c, wk, e4m3fn_values(wv_bytes) * wv_scale.astype(np.float64), keep, write)

@@ -1,0 +1,446 @@
+from contextlib import ExitStack
+
+import concourse.mybir as mybir
+from concourse.masks import make_identity
+
+F32 = mybir.dt.float32
+BF16 = mybir.dt.bfloat16
+U32 = mybir.dt.uint32
+U8 = mybir.dt.uint8
+FP8 = mybir.dt.float8_e4m3fn
+FP8X4 = mybir.dt.float8_e4m3fn_x4
+ALU = mybir.AluOpType
+COPY = mybir.ActivationFunctionType.Copy
+
+T, L, H, DK, DV = 2048, 512, 8, 128, 256
+P = 128
+G = 4
+FLOPS = 2 * T * L * H * (DK + DV) + 2 * T * H * DK * DV
+
+UNITS = H * G
+MODES = "GAGAAGGPPAPGAGPGGGGAGAPGPGPGPGAP"
+WK_ENG = "s"
+WV_ENG = "vs"
+ACC = 6
+SB = 6
+GROUPS = ((0, 1), (1, 2), (2, 4), (4, 6), (6, 8))
+WK0 = "v"
+LOADS = "v01 c0 k01 c1 c2 v12 k12 c3 v24 k24 v48 k48"
+WV0 = "v"
+C0FIRST = False
+PG = 0
+ACS = 0
+WID_ENG = "ssss"
+WID0 = "ssss"
+C0 = "sv"
+OB = 2
+WB = 1
+LW1 = 1
+LW2 = 2
+LQ = 2
+LF = 3
+LO = 1
+LI = 1
+HOLD = True
+WARM = 6
+HW = 2
+KKAA = False
+HEAD = ["wd:0:vsvs","iv:0:v","ik:0:s","t:0","t:1","qv:0","o:0:vs","qk:0","t:2","o:1:vs","q:0","q:1","p:0","cv:0","o:2:ss","p:1","a:0","k:0","s:1","t:3","q:2","s:0","p:2","o:3:ss","a:1","k:1","wd:1:ssss","g:0","k:2","ik:1:s","q:3","g:1","p:3","z:0","iv:1:vs","s:2","qk:1","qv:1","a:3","k:3","a:2","s:3"]
+LEAD = 4
+COUT = "sv"
+
+
+def tile_latent_kv_state_s7_kernel(tc, c, wk, wv_bytes, wv_scale, keep, write, out):
+    nc = tc.nc
+    with ExitStack() as ctx:
+        const = ctx.enter_context(tc.tile_pool(name="const", bufs=1))
+        stage = ctx.enter_context(tc.tile_pool(name="stage", bufs=SB))
+        psum = ctx.enter_context(tc.psum_pool(name="psum", bufs=1))
+
+        ident = const.tile([P, P], F32, name="ident")
+        ident_b = const.tile([P, P], BF16, name="ident_b")
+        c_sb = const.tile([P, G, 4, L], BF16, name="c_sb", align_bytes=64)
+        wk_raw = const.tile([P, 4, H * DK], BF16, name="wk_raw", align_bytes=64)
+        wv_raw = const.tile([P, 4, H * DV], U8, name="wv_raw", align_bytes=64)
+        wvs = const.tile([P, 4], F32, name="wvs")
+        kp_raw = const.tile([P, G, 32], BF16, name="kp_raw")
+        wr_raw = const.tile([P, G, 32], BF16, name="wr_raw")
+        kp = const.tile([P, G, H, 4], F32, name="kp")
+        wr = const.tile([P, G, H, 4], F32, name="wr")
+        c_cod = const.tile([P, G, 512], U32, name="c_cod", align_bytes=64)
+        c_scl = const.tile([P, G, 512], U8, name="c_scl", align_bytes=64)
+        wk_cod = const.tile([P, H, DK], U32, name="wk_cod", align_bytes=64)
+        wk_scl = const.tile([P, H, DK], U8, name="wk_scl", align_bytes=64)
+        wv_cod = const.tile([P, H, DV], U32, name="wv_cod", align_bytes=64)
+        wv_scl = const.tile([P, H, DV], U8, name="wv_scl", align_bytes=64)
+        warm = const.tile([P, 1], F32, name="warm")
+        zero = const.tile([P, 512], BF16, name="zero")
+
+        ctx.enter_context(tc.manual_schedule())
+
+        wv_view = wv_bytes.rearrange("(p j) w -> p j w", j=4)
+        wk_view = wk.rearrange("(p j) w -> p j w", j=4)
+        c_view = c.rearrange("(g p t) l -> g p t l", p=P, t=4)
+
+        nc.scalar.dma_start(out=wvs[:], in_=wv_scale.rearrange("(p j) o -> p (j o)", j=4))
+        nc.scalar.dma_start(out=wr_raw[:], in_=write.rearrange("(g p t) h -> p g (t h)", p=P, t=4))
+        nc.scalar.dma_start(out=kp_raw[:], in_=keep.rearrange("(g p t) h -> p g (t h)", p=P, t=4))
+
+        def load_wv(a, b):
+            nc.sync.dma_start(out=wv_raw[:, :, a * DV : b * DV], in_=wv_view[:, :, a * DV : b * DV])
+
+        def load_wk(a, b):
+            nc.sync.dma_start(out=wk_raw[:, :, a * DK : b * DK], in_=wk_view[:, :, a * DK : b * DK])
+
+        def load_c(g):
+            nc.sync.dma_start(out=c_sb[:, g, :, :], in_=c_view[g])
+
+        for item in LOADS.split():
+            if item[0] == "c":
+                load_c(int(item[1]))
+            elif item[0] == "k":
+                load_wk(int(item[1]), int(item[2]))
+            else:
+                load_wv(int(item[1]), int(item[2]))
+
+        make_identity(nc, ident[:])
+        nc.gpsimd.tensor_copy(out=ident_b[:], in_=ident[:])
+        nc.vector.memset(zero[:], 0.0)
+        nc.vector.memset(warm[:], 0.0)
+        nc.scalar.activation(out=warm[:], in_=warm[:], func=COPY)
+
+        def interleave(engine, dst, src):
+            d4 = dst.rearrange("p (c i) t -> p c t i", i=4)
+            s4 = src.rearrange("p t (c i) -> p c t i", i=4)
+            if engine == "g":
+                nc.gpsimd.tensor_scalar(out=dst, in0=src.rearrange("p t n -> p n t"), scalar1=1.0, scalar2=0.0, op0=ALU.mult, op1=ALU.add)
+            elif engine == "s":
+                nc.scalar.copy(out=d4, in_=s4)
+            else:
+                nc.vector.tensor_copy(out=d4, in_=s4)
+
+        wide = {}
+        vgrp = {}
+        kgrp = {}
+
+        def widen(a, b, js, engs):
+            if a not in wide:
+                w = stage.tile([P, 4, (b - a) * DV], BF16, name="wv_wide", bufs=2)
+                wide[a] = w
+            for j in js:
+                raw = wv_raw[:, j, a * DV : b * DV].bitcast(FP8)
+                if engs[j] == "s":
+                    nc.scalar.activation(out=wide[a][:, j, :], in_=raw, func=COPY, scale=wvs[:, j : j + 1])
+                else:
+                    nc.vector.tensor_scalar(out=wide[a][:, j, :], in0=raw, scalar1=wvs[:, j : j + 1], scalar2=None, op0=ALU.mult)
+
+        def group_wv(a, b, engs):
+            t = stage.tile([P, (b - a) * DV, 4], BF16, name="wv_grp", bufs=2, align_bytes=64)
+            vgrp[a] = t
+            n = (b - a) * DV // len(engs)
+            for i in range(len(engs)):
+                interleave(engs[i], t[:, i * n : (i + 1) * n, :], wide[a][:, :, i * n : (i + 1) * n])
+
+        def group_wk(a, b, engine):
+            t = stage.tile([P, (b - a) * DK, 4], BF16, name="wk_grp", bufs=2, align_bytes=64)
+            kgrp[a] = t
+            interleave(engine, t[:], wk_raw[:, :, a * DK : b * DK])
+
+        def quant_wv(a, b):
+            nc.vector.quantize_mx(
+                out=wv_cod[:, a:b, :].rearrange("p h n -> p (h n)").bitcast(FP8X4),
+                scales=wv_scl[:, a:b, :].rearrange("p h n -> p (h n)"),
+                in_=vgrp.pop(a)[:].rearrange("p n t -> p (n t)"),
+            )
+
+        def quant_wk(a, b):
+            nc.vector.quantize_mx(
+                out=wk_cod[:, a:b, :].rearrange("p h n -> p (h n)").bitcast(FP8X4),
+                scales=wk_scl[:, a:b, :].rearrange("p h n -> p (h n)"),
+                in_=kgrp.pop(a)[:].rearrange("p n t -> p (n t)"),
+            )
+
+        xt = {}
+        cgrp = {}
+
+        def transpose_c(g):
+            words = c_sb[:, g, :, :].bitcast(F32)
+            for b in range(2):
+                bank = psum.tile([P, 2, 2, P], F32, name="acc", bufs=ACC)
+                xt[g, b] = bank
+                for i in range(2):
+                    for u in range(2):
+                        nc.tensor.transpose(bank[:, i, u, :], words[:, 2 * b + i, u::2], ident[:])
+
+        def c_out(g, engines):
+            t = stage.tile([P, 2, 2, P, 4], BF16, name="c_grp", bufs=2, align_bytes=64)
+            cgrp[g] = t
+            for b in range(2):
+                dst = t[:, b, :, :, :].bitcast(F32)
+                src = xt.pop((g, b))[:].rearrange("q i u r -> q i r u")
+                if engines[b] == "s":
+                    nc.scalar.copy(out=dst, in_=src)
+                else:
+                    nc.vector.tensor_copy(out=dst, in_=src)
+
+        def quant_c(g):
+            nc.vector.quantize_mx(
+                out=c_cod[:, g, :].bitcast(FP8X4),
+                scales=c_scl[:, g, :],
+                in_=cgrp.pop(g)[:].rearrange("q b i r e -> q (b i r e)"),
+            )
+
+        kbank = {}
+        vbank = {}
+
+        def mm(out_ap, g, t, cod, scl):
+            nc.tensor.matmul_mx(
+                out=out_ap,
+                lhsT=c_cod[:, g, t * P : (t + 1) * P].bitcast(FP8X4),
+                lhsT_scale=c_scl[:, g, t * P : (t + 1) * P],
+                rhs=cod.bitcast(FP8X4),
+                rhs_scale=scl,
+                start=True,
+                stop=True,
+            )
+
+        def project(s):
+            h, g = s // G, s % G
+            bank = psum.tile([P, 4, P], F32, name="acc", bufs=ACC)
+            kbank[s] = bank
+            for t in range(4):
+                mm(bank[:, t, :], g, t, wk_cod[:, h, :], wk_scl[:, h, :])
+            if MODES[s] == "A":
+                for f in range(2):
+                    bank = psum.tile([P, 4, P], F32, name="acc", bufs=ACC)
+                    vbank[s, f] = bank
+                    for t in range(4):
+                        cols = slice(f * P, (f + 1) * P)
+                        mm(bank[:, t, :], g, t, wv_cod[:, h, cols], wv_scl[:, h, cols])
+            else:
+                for f in range(2):
+                    if ACS:
+                        bank = psum.tile([P, 2, DV], F32, name="acs", bufs=ACS)
+                    else:
+                        bank = psum.tile([P, 2, DV], F32, name="acc", bufs=ACC)
+                    vbank[s, f] = bank
+                    for i in range(2):
+                        mm(bank[:, i, :], g, 2 * f + i, wv_cod[:, h, :], wv_scl[:, h, :])
+
+        kin = {}
+        vin = {}
+        vt = {}
+        kcod = {}
+        vcod = {}
+
+        def ins(s):
+            if s // 2 not in kin:
+                k_in = stage.tile([P, 2, DK, 4], BF16, name="k_in", align_bytes=64)
+                v_in = stage.tile([P, 2, DV, 4], BF16, name="v_in", align_bytes=64)
+                kin[s // 2] = k_in
+                vin[s // 2] = v_in
+
+        def key(s):
+            h, g = s // G, s % G
+            ins(s)
+            nc.vector.scalar_tensor_tensor(
+                out=kin[s // 2][:, s % 2, :, :],
+                in0=kbank.pop(s)[:].rearrange("p t n -> p n t"),
+                scalar=0.0,
+                in1=kp[:, g, h, :].unsqueeze(1).to_broadcast([P, DK, 4]),
+                op0=ALU.max,
+                op1=ALU.mult,
+            )
+
+        def val_direct(s):
+            h, g = s // G, s % G
+            ins(s)
+            for f in range(2):
+                nc.vector.tensor_tensor(
+                    out=vin[s // 2][:, s % 2, f * P : (f + 1) * P, :],
+                    in0=vbank.pop((s, f))[:].rearrange("p t n -> p n t"),
+                    in1=wr[:, g, h, :].unsqueeze(1).to_broadcast([P, P, 4]),
+                    op=ALU.mult,
+                )
+
+        def val_scalar(s):
+            h, g = s // G, s % G
+            v_t = stage.tile([P, 4, DV], BF16, name="v_t", align_bytes=64)
+            vt[s] = v_t
+            for t in range(4):
+                nc.scalar.activation(
+                    out=v_t[:, t, :] if MODES[s] != "P" else v_t[:].rearrange("p t n -> p (t n)").rearrange("p (q n e) -> p q n e", q=2, e=2)[:, t // 2, :, t % 2],
+                    in_=vbank[s, t // 2][:, t % 2, :], func=COPY, scale=wr[:, g, h, t : t + 1]
+                )
+
+        def val_group(s):
+            ins(s)
+            if MODES[s] == "P":
+                src = vt.pop(s)[:].rearrange("p t n -> p (t n)").bitcast(F32).rearrange("p (q n) -> p n q", q=2)
+                dst = vin[s // 2][:, s % 2, :, :].bitcast(F32)
+                if PG and s % PG == 0:
+                    nc.gpsimd.tensor_scalar(out=dst, in0=src, scalar1=1.0, scalar2=0.0, op0=ALU.mult, op1=ALU.add)
+                else:
+                    nc.vector.tensor_copy(out=dst, in_=src)
+                return
+            interleave("g" if MODES[s] == "G" else "v", vin[s // 2][:, s % 2, :, :], vt.pop(s)[:])
+
+        wbank = {}
+
+        def weave(s):
+            bank = psum.tile([P, DV, 4], BF16, name="w_acc", bufs=WB)
+            wbank[s] = bank
+            src = vt.pop(s)[:]
+            dst = bank[:].rearrange("p n t -> p t n")
+            for f in range(2):
+                cols = slice(2 * f, 2 * f + 2)
+                nc.tensor.matmul(out=dst[:, cols, :], lhsT=ident_b[:], rhs=src[:, cols, :], start=True, stop=True)
+
+        def weave_out(s):
+            ins(s)
+            nc.scalar.copy(out=vin[s // 2][:, s % 2, :, :], in_=wbank.pop(s)[:])
+
+        def quant_kv(p):
+            kc = stage.tile([P, 2, DK], U32, name="k_cod", bufs=5, align_bytes=64)
+            ks = stage.tile([P, 2, DK], U8, name="k_scl", bufs=5, align_bytes=64)
+            vc = stage.tile([P, 2, DV], U32, name="v_cod", bufs=5, align_bytes=64)
+            vs = stage.tile([P, 2, DV], U8, name="v_scl", bufs=5, align_bytes=64)
+            kcod[p] = (kc, ks)
+            vcod[p] = (vc, vs)
+            nc.vector.quantize_mx(
+                out=kc[:].rearrange("p a n -> p (a n)").bitcast(FP8X4),
+                scales=ks[:].rearrange("p a n -> p (a n)"),
+                in_=kin.pop(p)[:].rearrange("p a n t -> p (a n t)"),
+            )
+            nc.vector.quantize_mx(
+                out=vc[:].rearrange("p a n -> p (a n)").bitcast(FP8X4),
+                scales=vs[:].rearrange("p a n -> p (a n)"),
+                in_=vin.pop(p)[:].rearrange("p a n t -> p (a n t)"),
+            )
+
+        obank = {}
+
+        def fold(h):
+            bank = psum.tile([P, DV], F32, name="o_acc", bufs=OB)
+            obank[h] = bank
+            for g in range(G):
+                (kc, ks), (vc, vs) = kcod[2 * h + g // 2], vcod[2 * h + g // 2]
+                nc.tensor.matmul_mx(
+                    out=bank[:],
+                    lhsT=kc[:, g % 2, :].bitcast(FP8X4),
+                    lhsT_scale=ks[:, g % 2, :],
+                    rhs=vc[:, g % 2, :].bitcast(FP8X4),
+                    rhs_scale=vs[:, g % 2, :],
+                    start=(g == 0),
+                    stop=(g == G - 1),
+                )
+
+        def store(h):
+            o = stage.tile([P, DV], F32, name="o_sb", bufs=2)
+            nc.scalar.copy(out=o[:], in_=obank.pop(h)[:])
+            nc.sync.dma_start(out=out[h], in_=o[:])
+
+        def hold(p):
+            mark = stage.tile([P, 1], U32, name="mark", bufs=2)
+            nc.gpsimd.tensor_copy(out=mark[:], in_=vcod[p][0][:, 1, DV - 1 : DV])
+
+        PAIRS = UNITS // 2
+        if WARM:
+            bank = psum.tile([P, 512], F32, name="o_acc", bufs=OB)
+            for i in range(WARM):
+                nc.tensor.matmul(out=bank[:], lhsT=zero[:, :P], rhs=zero[:], start=True, stop=True)
+
+        def scales():
+            nc.vector.tensor_copy(out=wr[:], in_=wr_raw[:].rearrange("p g (t h) -> p g h t", t=4))
+            nc.vector.tensor_copy(out=kp[:], in_=kp_raw[:].rearrange("p g (t h) -> p g h t", t=4))
+
+        for item in HEAD:
+            f = item.split(":")
+            i = int(f[1])
+            if f[0] == "wd":
+                widen(i, i + 1, range(4), f[2])
+            elif f[0] == "iv":
+                group_wv(i, i + 1, f[2])
+            elif f[0] == "ik":
+                group_wk(i, i + 1, f[2])
+            elif f[0] == "qv":
+                quant_wv(i, i + 1)
+            elif f[0] == "qk":
+                quant_wk(i, i + 1)
+            elif f[0] == "t":
+                transpose_c(i)
+            elif f[0] == "o":
+                c_out(i, f[2])
+            elif f[0] == "q":
+                quant_c(i)
+            elif f[0] == "cv":
+                scales()
+            elif f[0] == "p":
+                project(i)
+            elif f[0] == "s":
+                if MODES[i] != "A":
+                    val_scalar(i)
+            elif f[0] == "k":
+                key(i)
+            elif f[0] == "a":
+                if MODES[i] == "A":
+                    val_direct(i)
+            elif f[0] == "g":
+                if MODES[i] in "VPG":
+                    val_group(i)
+            elif f[0] == "z":
+                quant_kv(i)
+
+        for p in range(2, PAIRS + 8):
+            u = p - LF
+            if 0 <= u < PAIRS and u % 2 == 1:
+                fold(u // 2)
+            gjobs = []
+            if 1 <= p - LQ < PAIRS:
+                quant_kv(p - LQ)
+            for a in range(HW, H):
+                first = 2 * a - LEAD
+                b = a + 1
+                if p == max(2, first):
+                    widen(a, b, range(4), WID_ENG)
+                    group_wk(a, b, WK_ENG)
+                if p == max(2, first + 1):
+                    if WV_ENG == "g":
+                        gjobs.append((group_wv, a, b))
+                    else:
+                        group_wv(a, b, WV_ENG)
+                    quant_wk(a, b)
+                if p == max(2, first + 2):
+                    quant_wv(a, b)
+            if 1 <= p - 1 < PAIRS:
+                for s in (2 * (p - 1), 2 * (p - 1) + 1):
+                    if MODES[s] in "VP":
+                        val_group(s)
+                    elif MODES[s] == "G":
+                        gjobs.append((val_group, s))
+            if gjobs and 1 <= p - LQ < PAIRS:
+                hold(p - LQ)
+            for job in gjobs:
+                if job[0] is val_group:
+                    val_group(job[1])
+                else:
+                    job[0](job[1], job[2], "g")
+            if p < PAIRS:
+                for s in (2 * p, 2 * p + 1):
+                    project(s)
+                    if MODES[s] != "A":
+                        val_scalar(s)
+                if KKAA:
+                    key(2 * p)
+                    key(2 * p + 1)
+                    for s in (2 * p, 2 * p + 1):
+                        if MODES[s] == "A":
+                            val_direct(s)
+                else:
+                    for s in (2 * p, 2 * p + 1):
+                        key(s)
+                        if MODES[s] == "A":
+                            val_direct(s)
+            u = p - LF - LO
+            if 0 <= u < PAIRS and u % 2 == 1:
+                store(u // 2)

@@ -17,51 +17,19 @@ P = 128
 G = 4
 FLOPS = 2 * T * L * H * (DK + DV) + 2 * T * H * DK * DV
 
-UNITS = H * G
-MODES = "GAGAAGGPPAPGAGPGGGGAGAPGPGPGPGAP"
-WK_ENG = "s"
-WV_ENG = "vs"
-ACC = 6
-SB = 6
-GROUPS = ((0, 1), (1, 2), (2, 4), (4, 6), (6, 8))
-WK0 = "v"
-LOADS = "v01 c0 k01 c1 c2 v12 k12 c3 v24 k24 v48 k48"
-WV0 = "v"
-C0FIRST = False
-PG = 0
-ACS = 0
-WID_ENG = "ssss"
-WID0 = "ssss"
-C0 = "sv"
-OB = 2
-WB = 1
-LW1 = 1
-LW2 = 2
-LQ = 2
-LF = 3
-LO = 1
-LI = 1
-HOLD = True
-WARM = 6
-HW = 2
-KKAA = False
-HEAD = ["wd:0:vsvs","iv:0:v","ik:0:s","t:0","t:1","qv:0","o:0:vs","qk:0","t:2","o:1:vs","q:0","q:1","p:0","cv:0","o:2:ss","p:1","a:0","k:0","s:1","t:3","q:2","s:0","p:2","o:3:ss","a:1","k:1","wd:1:ssss","g:0","k:2","ik:1:s","q:3","g:1","p:3","z:0","iv:1:vs","s:2","qk:1","qv:1","a:3","k:3","a:2","s:3"]
-LEAD = 4
-COUT = "sv"
+NS = 5
+ND = 2 * G - NS
+W_LOADS = ((0, 2), (2, 4), (4, 8))
 
 
 def tile_latent_kv_state_s7_kernel(tc, c, wk, wv_bytes, wv_scale, keep, write, out):
     nc = tc.nc
     with ExitStack() as ctx:
         const = ctx.enter_context(tc.tile_pool(name="const", bufs=1))
-        stage = ctx.enter_context(tc.tile_pool(name="stage", bufs=SB))
+        stage = ctx.enter_context(tc.tile_pool(name="stage", bufs=2))
         psum = ctx.enter_context(tc.psum_pool(name="psum", bufs=1))
 
         ident = const.tile([P, P], F32, name="ident")
-        ident_b = const.tile([P, P], BF16, name="ident_b")
-        c_sb = const.tile([P, G, 4, L], BF16, name="c_sb", align_bytes=64)
-        wk_raw = const.tile([P, 4, H * DK], BF16, name="wk_raw", align_bytes=64)
-        wv_raw = const.tile([P, 4, H * DV], U8, name="wv_raw", align_bytes=64)
         wvs = const.tile([P, 4], F32, name="wvs")
         kp_raw = const.tile([P, G, 32], BF16, name="kp_raw")
         wr_raw = const.tile([P, G, 32], BF16, name="wr_raw")
@@ -73,374 +41,362 @@ def tile_latent_kv_state_s7_kernel(tc, c, wk, wv_bytes, wv_scale, keep, write, o
         wk_scl = const.tile([P, H, DK], U8, name="wk_scl", align_bytes=64)
         wv_cod = const.tile([P, H, DV], U32, name="wv_cod", align_bytes=64)
         wv_scl = const.tile([P, H, DV], U8, name="wv_scl", align_bytes=64)
-        warm = const.tile([P, 1], F32, name="warm")
-        zero = const.tile([P, 512], BF16, name="zero")
+        c_sb = {}
+        for g in range(G):
+            for b in range(2):
+                c_sb[g, b] = const.tile([P, 2, L], BF16, name="c_sb%d%d" % (g, b), align_bytes=64)
+        wv_raw = {}
+        wk_raw = {}
+        for a, b in W_LOADS:
+            tv = const.tile([P, 4, (b - a) * DV], U8, name="wv_raw%d" % a, align_bytes=64)
+            tk = const.tile([P, 4, (b - a) * DK], BF16, name="wk_raw%d" % a, align_bytes=64)
+            for h in range(a, b):
+                wv_raw[h] = (tv, h - a)
+                wk_raw[h] = (tk, h - a)
 
         ctx.enter_context(tc.manual_schedule())
 
         wv_view = wv_bytes.rearrange("(p j) w -> p j w", j=4)
         wk_view = wk.rearrange("(p j) w -> p j w", j=4)
-        c_view = c.rearrange("(g p t) l -> g p t l", p=P, t=4)
+        c_view = c.rearrange("(g p b i) l -> g b p i l", p=P, b=2, i=2)
 
-        nc.scalar.dma_start(out=wvs[:], in_=wv_scale.rearrange("(p j) o -> p (j o)", j=4))
-        nc.scalar.dma_start(out=wr_raw[:], in_=write.rearrange("(g p t) h -> p g (t h)", p=P, t=4))
-        nc.scalar.dma_start(out=kp_raw[:], in_=keep.rearrange("(g p t) h -> p g (t h)", p=P, t=4))
+        def load_c(g, b):
+            nc.sync.dma_start(out=c_sb[g, b][:], in_=c_view[g, b])
 
         def load_wv(a, b):
-            nc.sync.dma_start(out=wv_raw[:, :, a * DV : b * DV], in_=wv_view[:, :, a * DV : b * DV])
+            nc.sync.dma_start(out=wv_raw[a][0][:], in_=wv_view[:, :, a * DV : b * DV])
 
         def load_wk(a, b):
-            nc.sync.dma_start(out=wk_raw[:, :, a * DK : b * DK], in_=wk_view[:, :, a * DK : b * DK])
+            nc.sync.dma_start(out=wk_raw[a][0][:], in_=wk_view[:, :, a * DK : b * DK])
 
-        def load_c(g):
-            nc.sync.dma_start(out=c_sb[:, g, :, :], in_=c_view[g])
-
-        for item in LOADS.split():
-            if item[0] == "c":
-                load_c(int(item[1]))
-            elif item[0] == "k":
-                load_wk(int(item[1]), int(item[2]))
-            else:
-                load_wv(int(item[1]), int(item[2]))
+        nc.scalar.dma_start(out=wvs[:], in_=wv_scale.rearrange("(p j) o -> p (j o)", j=4))
+        load_c(0, 0)
+        load_wv(*W_LOADS[0])
+        load_c(0, 1)
+        load_wk(*W_LOADS[0])
+        load_c(1, 0)
+        load_c(1, 1)
+        nc.scalar.dma_start(out=kp_raw[:], in_=keep.rearrange("(g p t) h -> p g (t h)", p=P, t=4))
+        nc.sync.dma_start(out=wr_raw[:], in_=write.rearrange("(g p t) h -> p g (t h)", p=P, t=4))
+        for g in range(2, G):
+            load_c(g, 0)
+            load_c(g, 1)
+        for a, b in W_LOADS[1:]:
+            load_wv(a, b)
+            load_wk(a, b)
 
         make_identity(nc, ident[:])
-        nc.gpsimd.tensor_copy(out=ident_b[:], in_=ident[:])
-        nc.vector.memset(zero[:], 0.0)
-        nc.vector.memset(warm[:], 0.0)
-        nc.scalar.activation(out=warm[:], in_=warm[:], func=COPY)
+        nc.gpsimd.tensor_copy(out=kp[:], in_=kp_raw[:].rearrange("p g (t h) -> p g h t", t=4))
+        nc.gpsimd.tensor_copy(out=wr[:], in_=wr_raw[:].rearrange("p g (t h) -> p g h t", t=4))
 
         def interleave(engine, dst, src):
             d4 = dst.rearrange("p (c i) t -> p c t i", i=4)
             s4 = src.rearrange("p t (c i) -> p c t i", i=4)
-            if engine == "g":
-                nc.gpsimd.tensor_scalar(out=dst, in0=src.rearrange("p t n -> p n t"), scalar1=1.0, scalar2=0.0, op0=ALU.mult, op1=ALU.add)
-            elif engine == "s":
+            if engine == "s":
                 nc.scalar.copy(out=d4, in_=s4)
             else:
                 nc.vector.tensor_copy(out=d4, in_=s4)
 
-        wide = {}
-        vgrp = {}
-        kgrp = {}
+        def quantize(cod, scl, src):
+            nc.vector.quantize_mx(out=cod.bitcast(FP8X4), scales=scl, in_=src)
 
-        def widen(a, b, js, engs):
-            if a not in wide:
-                w = stage.tile([P, 4, (b - a) * DV], BF16, name="wv_wide", bufs=2)
-                wide[a] = w
-            for j in js:
-                raw = wv_raw[:, j, a * DV : b * DV].bitcast(FP8)
-                if engs[j] == "s":
-                    nc.scalar.activation(out=wide[a][:, j, :], in_=raw, func=COPY, scale=wvs[:, j : j + 1])
+        wide, wv_grp, wk_grp = {}, {}, {}
+
+        def widen(h, engines):
+            wide[h] = stage.tile([P, 4, DV], BF16, name="wv_wide", align_bytes=64)
+            raw, i = wv_raw[h]
+            for j in range(4):
+                src = raw[:, j, i * DV : (i + 1) * DV].bitcast(FP8)
+                if engines[j] == "s":
+                    nc.scalar.activation(out=wide[h][:, j, :], in_=src, func=COPY, scale=wvs[:, j : j + 1])
                 else:
-                    nc.vector.tensor_scalar(out=wide[a][:, j, :], in0=raw, scalar1=wvs[:, j : j + 1], scalar2=None, op0=ALU.mult)
+                    nc.vector.tensor_scalar(out=wide[h][:, j, :], in0=src, scalar1=wvs[:, j : j + 1], scalar2=None, op0=ALU.mult)
 
-        def group_wv(a, b, engs):
-            t = stage.tile([P, (b - a) * DV, 4], BF16, name="wv_grp", bufs=2, align_bytes=64)
-            vgrp[a] = t
-            n = (b - a) * DV // len(engs)
-            for i in range(len(engs)):
-                interleave(engs[i], t[:, i * n : (i + 1) * n, :], wide[a][:, :, i * n : (i + 1) * n])
+        def group_wv(h, engine):
+            wv_grp[h] = stage.tile([P, DV, 4], BF16, name="wv_grp", align_bytes=64)
+            interleave(engine, wv_grp[h][:], wide.pop(h)[:])
 
-        def group_wk(a, b, engine):
-            t = stage.tile([P, (b - a) * DK, 4], BF16, name="wk_grp", bufs=2, align_bytes=64)
-            kgrp[a] = t
-            interleave(engine, t[:], wk_raw[:, :, a * DK : b * DK])
+        def group_wk(h, engine):
+            wk_grp[h] = stage.tile([P, DK, 4], BF16, name="wk_grp", align_bytes=64)
+            raw, i = wk_raw[h]
+            interleave(engine, wk_grp[h][:], raw[:, :, i * DK : (i + 1) * DK])
 
-        def quant_wv(a, b):
-            nc.vector.quantize_mx(
-                out=wv_cod[:, a:b, :].rearrange("p h n -> p (h n)").bitcast(FP8X4),
-                scales=wv_scl[:, a:b, :].rearrange("p h n -> p (h n)"),
-                in_=vgrp.pop(a)[:].rearrange("p n t -> p (n t)"),
-            )
+        def quant_wk(h):
+            quantize(wk_cod[:, h, :], wk_scl[:, h, :], wk_grp.pop(h)[:].rearrange("p n t -> p (n t)"))
 
-        def quant_wk(a, b):
-            nc.vector.quantize_mx(
-                out=wk_cod[:, a:b, :].rearrange("p h n -> p (h n)").bitcast(FP8X4),
-                scales=wk_scl[:, a:b, :].rearrange("p h n -> p (h n)"),
-                in_=kgrp.pop(a)[:].rearrange("p n t -> p (n t)"),
-            )
+        def quant_wv(h):
+            quantize(wv_cod[:, h, :], wv_scl[:, h, :], wv_grp.pop(h)[:].rearrange("p n t -> p (n t)"))
 
-        xt = {}
-        cgrp = {}
+        def s_bank():
+            return psum.tile([P, 512], F32, name="s_bank", bufs=3)
 
-        def transpose_c(g):
-            words = c_sb[:, g, :, :].bitcast(F32)
-            for b in range(2):
-                bank = psum.tile([P, 2, 2, P], F32, name="acc", bufs=ACC)
-                xt[g, b] = bank
-                for i in range(2):
-                    for u in range(2):
-                        nc.tensor.transpose(bank[:, i, u, :], words[:, 2 * b + i, u::2], ident[:])
+        def v_bank():
+            return psum.tile([P, 4, P], F32, name="v_bank", bufs=4)
 
-        def c_out(g, engines):
-            t = stage.tile([P, 2, 2, P, 4], BF16, name="c_grp", bufs=2, align_bytes=64)
-            cgrp[g] = t
-            for b in range(2):
-                dst = t[:, b, :, :, :].bitcast(F32)
-                src = xt.pop((g, b))[:].rearrange("q i u r -> q i r u")
-                if engines[b] == "s":
-                    nc.scalar.copy(out=dst, in_=src)
-                else:
-                    nc.vector.tensor_copy(out=dst, in_=src)
+        xt, c_grp = {}, {}
 
-        def quant_c(g):
-            nc.vector.quantize_mx(
-                out=c_cod[:, g, :].bitcast(FP8X4),
-                scales=c_scl[:, g, :],
-                in_=cgrp.pop(g)[:].rearrange("q b i r e -> q (b i r e)"),
-            )
+        def transpose_c(g, b):
+            words = c_sb[g, b][:].bitcast(F32)
+            xt[g, b] = s_bank()
+            for i in range(2):
+                for u in range(2):
+                    col = (2 * i + u) * P
+                    nc.tensor.transpose(xt[g, b][:, col : col + P], words[:, i, u::2], ident[:])
 
-        kbank = {}
-        vbank = {}
+        def c_out(g, b, engine):
+            c_grp[g, b] = stage.tile([P, 2, P, 4], BF16, name="c_grp", bufs=4, align_bytes=64)
+            dst = c_grp[g, b][:].bitcast(F32)
+            src = xt.pop((g, b))[:].rearrange("q (i u r) -> q i r u", i=2, u=2)
+            if engine == "s":
+                nc.scalar.copy(out=dst, in_=src)
+            else:
+                nc.vector.tensor_copy(out=dst, in_=src)
 
-        def mm(out_ap, g, t, cod, scl):
+        def quant_c(g, b):
+            cols = slice(2 * b * P, 2 * (b + 1) * P)
+            quantize(c_cod[:, g, cols], c_scl[:, g, cols], c_grp.pop((g, b))[:].rearrange("q i r e -> q (i r e)"))
+
+        def mm(dst, g, t, cod, scl):
+            cols = slice(t * P, (t + 1) * P)
             nc.tensor.matmul_mx(
-                out=out_ap,
-                lhsT=c_cod[:, g, t * P : (t + 1) * P].bitcast(FP8X4),
-                lhsT_scale=c_scl[:, g, t * P : (t + 1) * P],
+                out=dst,
+                lhsT=c_cod[:, g, cols].bitcast(FP8X4),
+                lhsT_scale=c_scl[:, g, cols],
                 rhs=cod.bitcast(FP8X4),
                 rhs_scale=scl,
                 start=True,
                 stop=True,
             )
 
-        def project(s):
-            h, g = s // G, s % G
-            bank = psum.tile([P, 4, P], F32, name="acc", bufs=ACC)
-            kbank[s] = bank
+        kb, db, sb = {}, {}, {}
+
+        def mm_key(h, g):
+            kb[h, g] = v_bank()
             for t in range(4):
-                mm(bank[:, t, :], g, t, wk_cod[:, h, :], wk_scl[:, h, :])
-            if MODES[s] == "A":
-                for f in range(2):
-                    bank = psum.tile([P, 4, P], F32, name="acc", bufs=ACC)
-                    vbank[s, f] = bank
-                    for t in range(4):
-                        cols = slice(f * P, (f + 1) * P)
-                        mm(bank[:, t, :], g, t, wv_cod[:, h, cols], wv_scl[:, h, cols])
-            else:
-                for f in range(2):
-                    if ACS:
-                        bank = psum.tile([P, 2, DV], F32, name="acs", bufs=ACS)
-                    else:
-                        bank = psum.tile([P, 2, DV], F32, name="acc", bufs=ACC)
-                    vbank[s, f] = bank
-                    for i in range(2):
-                        mm(bank[:, i, :], g, 2 * f + i, wv_cod[:, h, :], wv_scl[:, h, :])
+                mm(kb[h, g][:, t, :], g, t, wk_cod[:, h, :], wk_scl[:, h, :])
 
-        kin = {}
-        vin = {}
-        vt = {}
-        kcod = {}
-        vcod = {}
+        def mm_direct(h, d):
+            g, f = divmod(NS + d, 2)
+            db[h, d] = v_bank()
+            cols = slice(f * P, (f + 1) * P)
+            for t in range(4):
+                mm(db[h, d][:, t, :], g, t, wv_cod[:, h, cols], wv_scl[:, h, cols])
 
-        def ins(s):
-            if s // 2 not in kin:
-                k_in = stage.tile([P, 2, DK, 4], BF16, name="k_in", align_bytes=64)
-                v_in = stage.tile([P, 2, DV, 4], BF16, name="v_in", align_bytes=64)
-                kin[s // 2] = k_in
-                vin[s // 2] = v_in
+        def s_shape(n):
+            g, f = divmod(n, 2)
+            if 2 * g + 1 < NS:
+                return g, (2 * f, 2 * f + 1), DV
+            return g, (0, 1, 2, 3), P
 
-        def key(s):
-            h, g = s // G, s % G
-            ins(s)
+        def mm_scalar(h, n):
+            g, ts, w = s_shape(n)
+            sb[h, n] = s_bank()
+            for i in range(len(ts)):
+                mm(sb[h, n][:, i * w : (i + 1) * w], g, ts[i], wv_cod[:, h, :w], wv_scl[:, h, :w])
+
+        k_in, v_dir, v_rows, v_grp, cod = {}, {}, {}, {}, {}
+
+        def key(h, g):
+            if g == 0:
+                k_in[h] = stage.tile([P, G, DK, 4], BF16, name="k_in", align_bytes=64)
             nc.vector.scalar_tensor_tensor(
-                out=kin[s // 2][:, s % 2, :, :],
-                in0=kbank.pop(s)[:].rearrange("p t n -> p n t"),
+                out=k_in[h][:, g, :, :],
+                in0=kb.pop((h, g))[:].rearrange("p t n -> p n t"),
                 scalar=0.0,
                 in1=kp[:, g, h, :].unsqueeze(1).to_broadcast([P, DK, 4]),
                 op0=ALU.max,
                 op1=ALU.mult,
             )
 
-        def val_direct(s):
-            h, g = s // G, s % G
-            ins(s)
-            for f in range(2):
-                nc.vector.tensor_tensor(
-                    out=vin[s // 2][:, s % 2, f * P : (f + 1) * P, :],
-                    in0=vbank.pop((s, f))[:].rearrange("p t n -> p n t"),
-                    in1=wr[:, g, h, :].unsqueeze(1).to_broadcast([P, P, 4]),
-                    op=ALU.mult,
-                )
-
-        def val_scalar(s):
-            h, g = s // G, s % G
-            v_t = stage.tile([P, 4, DV], BF16, name="v_t", align_bytes=64)
-            vt[s] = v_t
-            for t in range(4):
-                nc.scalar.activation(
-                    out=v_t[:, t, :] if MODES[s] != "P" else v_t[:].rearrange("p t n -> p (t n)").rearrange("p (q n e) -> p q n e", q=2, e=2)[:, t // 2, :, t % 2],
-                    in_=vbank[s, t // 2][:, t % 2, :], func=COPY, scale=wr[:, g, h, t : t + 1]
-                )
-
-        def val_group(s):
-            ins(s)
-            if MODES[s] == "P":
-                src = vt.pop(s)[:].rearrange("p t n -> p (t n)").bitcast(F32).rearrange("p (q n) -> p n q", q=2)
-                dst = vin[s // 2][:, s % 2, :, :].bitcast(F32)
-                if PG and s % PG == 0:
-                    nc.gpsimd.tensor_scalar(out=dst, in0=src, scalar1=1.0, scalar2=0.0, op0=ALU.mult, op1=ALU.add)
+        def val_direct(h, d):
+            if d == 0:
+                if h == 0:
+                    v_dir[h] = stage.tile([P, ND, P, 4], BF16, name="v_grp", bufs=1, align_bytes=64)
                 else:
-                    nc.vector.tensor_copy(out=dst, in_=src)
-                return
-            interleave("g" if MODES[s] == "G" else "v", vin[s // 2][:, s % 2, :, :], vt.pop(s)[:])
-
-        wbank = {}
-
-        def weave(s):
-            bank = psum.tile([P, DV, 4], BF16, name="w_acc", bufs=WB)
-            wbank[s] = bank
-            src = vt.pop(s)[:]
-            dst = bank[:].rearrange("p n t -> p t n")
-            for f in range(2):
-                cols = slice(2 * f, 2 * f + 2)
-                nc.tensor.matmul(out=dst[:, cols, :], lhsT=ident_b[:], rhs=src[:, cols, :], start=True, stop=True)
-
-        def weave_out(s):
-            ins(s)
-            nc.scalar.copy(out=vin[s // 2][:, s % 2, :, :], in_=wbank.pop(s)[:])
-
-        def quant_kv(p):
-            kc = stage.tile([P, 2, DK], U32, name="k_cod", bufs=5, align_bytes=64)
-            ks = stage.tile([P, 2, DK], U8, name="k_scl", bufs=5, align_bytes=64)
-            vc = stage.tile([P, 2, DV], U32, name="v_cod", bufs=5, align_bytes=64)
-            vs = stage.tile([P, 2, DV], U8, name="v_scl", bufs=5, align_bytes=64)
-            kcod[p] = (kc, ks)
-            vcod[p] = (vc, vs)
-            nc.vector.quantize_mx(
-                out=kc[:].rearrange("p a n -> p (a n)").bitcast(FP8X4),
-                scales=ks[:].rearrange("p a n -> p (a n)"),
-                in_=kin.pop(p)[:].rearrange("p a n t -> p (a n t)"),
-            )
-            nc.vector.quantize_mx(
-                out=vc[:].rearrange("p a n -> p (a n)").bitcast(FP8X4),
-                scales=vs[:].rearrange("p a n -> p (a n)"),
-                in_=vin.pop(p)[:].rearrange("p a n t -> p (a n t)"),
+                    v_dir[h] = stage.tile([P, ND, P, 4], BF16, name="v_dir", align_bytes=64)
+            nc.vector.tensor_tensor(
+                out=v_dir[h][:, d, :, :],
+                in0=db.pop((h, d))[:].rearrange("p t n -> p n t"),
+                in1=wr[:, (NS + d) // 2, h, :].unsqueeze(1).to_broadcast([P, P, 4]),
+                op=ALU.mult,
             )
 
-        obank = {}
+        def val_scalar(h, n):
+            if n == 0:
+                v_rows[h] = stage.tile([P, NS, 4, P], BF16, name="v_rows", align_bytes=64)
+            g, ts, w = s_shape(n)
+            bank = sb.pop((h, n))
+            for i in range(len(ts)):
+                nc.scalar.activation(
+                    out=v_rows[h][:, 2 * g : 2 * g + w // P, ts[i], :],
+                    in_=bank[:, i * w : (i + 1) * w].rearrange("p (f n) -> p f n", n=P),
+                    func=COPY,
+                    scale=wr[:, g, h, ts[i] : ts[i] + 1],
+                )
+
+        def group_v(h):
+            v_grp[h] = stage.tile([P, NS, P, 4], BF16, name="v_grp", bufs=1, align_bytes=64)
+            nc.gpsimd.tensor_scalar(
+                out=v_grp[h][:], in0=v_rows.pop(h)[:].rearrange("p m t n -> p m n t"), scalar1=1.0, scalar2=0.0, op0=ALU.mult, op1=ALU.add
+            )
+
+        def group_v_scalar(h, m):
+            if m == 0:
+                v_grp[h] = stage.tile([P, NS, P, 4], BF16, name="v_last", bufs=1, align_bytes=64)
+            interleave("s", v_grp[h][:, m, :, :], v_rows[h][:, m, :, :])
+
+        def codes(h):
+            kc = stage.tile([P, G * DK], U32, name="k_cod", bufs=3, align_bytes=64)
+            ks = stage.tile([P, G * DK], U8, name="k_scl", bufs=3, align_bytes=64)
+            vc = stage.tile([P, G * DV], U32, name="v_cod", bufs=3, align_bytes=64)
+            vs = stage.tile([P, G * DV], U8, name="v_scl", bufs=3, align_bytes=64)
+            cod[h] = (kc, ks, vc, vs)
+
+        def quant_k(h):
+            codes(h)
+            kc, ks, vc, vs = cod[h]
+            quantize(kc[:], ks[:], k_in.pop(h)[:].rearrange("p g n t -> p (g n t)"))
+
+        def quant_v(h, src, first, runs):
+            kc, ks, vc, vs = cod[h]
+            m = 0
+            for r in runs:
+                cols = slice((first + m) * P, (first + m + r) * P)
+                quantize(vc[:, cols], vs[:, cols], src[:, m : m + r, :, :].rearrange("p m n t -> p (m n t)"))
+                m = m + r
+
+        def quant_direct(h):
+            quant_v(h, v_dir.pop(h), NS, (1, 2))
+
+        def quant_grouped(h):
+            quant_v(h, v_grp.pop(h), 0, (4, 1))
+
+        ob = {}
 
         def fold(h):
-            bank = psum.tile([P, DV], F32, name="o_acc", bufs=OB)
-            obank[h] = bank
+            if h == H - 1:
+                ob[h] = s_bank()
+            else:
+                ob[h] = psum.tile([P, 512], F32, name="o_bank", bufs=1)
+            kc, ks, vc, vs = cod.pop(h)
             for g in range(G):
-                (kc, ks), (vc, vs) = kcod[2 * h + g // 2], vcod[2 * h + g // 2]
                 nc.tensor.matmul_mx(
-                    out=bank[:],
-                    lhsT=kc[:, g % 2, :].bitcast(FP8X4),
-                    lhsT_scale=ks[:, g % 2, :],
-                    rhs=vc[:, g % 2, :].bitcast(FP8X4),
-                    rhs_scale=vs[:, g % 2, :],
+                    out=ob[h][:, :DV],
+                    lhsT=kc[:, g * DK : (g + 1) * DK].bitcast(FP8X4),
+                    lhsT_scale=ks[:, g * DK : (g + 1) * DK],
+                    rhs=vc[:, g * DV : (g + 1) * DV].bitcast(FP8X4),
+                    rhs_scale=vs[:, g * DV : (g + 1) * DV],
                     start=(g == 0),
                     stop=(g == G - 1),
                 )
 
         def store(h):
-            o = stage.tile([P, DV], F32, name="o_sb", bufs=2)
-            nc.scalar.copy(out=o[:], in_=obank.pop(h)[:])
+            o = stage.tile([P, DV], F32, name="o_sb")
+            nc.scalar.copy(out=o[:], in_=ob.pop(h)[:, :DV])
             nc.sync.dma_start(out=out[h], in_=o[:])
 
-        def hold(p):
-            mark = stage.tile([P, 1], U32, name="mark", bufs=2)
-            nc.gpsimd.tensor_copy(out=mark[:], in_=vcod[p][0][:, 1, DV - 1 : DV])
+        widen(0, "svsv")
+        transpose_c(0, 0)
+        c_out(0, 0, "s")
+        transpose_c(0, 1)
+        c_out(0, 1, "s")
+        group_wv(0, "v")
+        group_wk(0, "v")
+        quant_wv(0)
+        quant_c(0, 0)
+        quant_wk(0)
+        quant_c(0, 1)
+        widen(1, "vvvv")
+        for b in range(2):
+            transpose_c(1, b)
+            c_out(1, b, "s")
+        mm_key(0, 0)
+        group_wv(1, "v")
+        key(0, 0)
+        quant_c(1, 0)
+        quant_c(1, 1)
+        for b in range(2):
+            transpose_c(2, b)
+            c_out(2, b, "s")
+        mm_key(0, 1)
+        group_wk(1, "v")
+        key(0, 1)
+        quant_c(2, 0)
+        quant_c(2, 1)
+        for b in range(2):
+            transpose_c(3, b)
+            c_out(3, b, "s")
+        mm_key(0, 2)
+        mm_direct(0, 0)
+        for n in range(2):
+            mm_scalar(0, n)
+            val_scalar(0, n)
+        key(0, 2)
+        quant_c(3, 0)
+        quant_c(3, 1)
+        val_direct(0, 0)
+        mm_key(0, 3)
+        mm_direct(0, 1)
+        mm_direct(0, 2)
+        for n in range(2, NS):
+            mm_scalar(0, n)
+            val_scalar(0, n)
+        key(0, 3)
+        val_direct(0, 1)
+        val_direct(0, 2)
 
-        PAIRS = UNITS // 2
-        if WARM:
-            bank = psum.tile([P, 512], F32, name="o_acc", bufs=OB)
-            for i in range(WARM):
-                nc.tensor.matmul(out=bank[:], lhsT=zero[:, :P], rhs=zero[:], start=True, stop=True)
+        for h in range(1, H):
+            last = h == H - 1
+            quant_wk(h)
+            quant_wv(h)
+            quant_k(h - 1)
+            quant_direct(h - 1)
+            if h >= 2:
+                quant_grouped(h - 2)
+            group_v(h - 1)
+            if not last:
+                widen(h + 1, "ssss")
+                group_wv(h + 1, "s")
+                group_wk(h + 1, "s")
+            for g in range(3):
+                mm_key(h, g)
+            mm_direct(h, 0)
+            for n in range(3):
+                mm_scalar(h, n)
+            if h >= 2:
+                fold(h - 2)
+                if not last:
+                    store(h - 2)
+            key(h, 0)
+            mm_key(h, 3)
+            key(h, 1)
+            mm_direct(h, 1)
+            val_scalar(h, 0)
+            mm_scalar(h, 3)
+            key(h, 2)
+            mm_direct(h, 2)
+            val_scalar(h, 1)
+            mm_scalar(h, 4)
+            if last:
+                store(h - 2)
+                group_v_scalar(h, 0)
+                group_v_scalar(h, 1)
+            val_direct(h, 0)
+            key(h, 3)
+            val_direct(h, 1)
+            val_direct(h, 2)
+            for n in range(2, NS):
+                val_scalar(h, n)
+            if last:
+                for m in range(2, NS):
+                    group_v_scalar(h, m)
 
-        def scales():
-            nc.vector.tensor_copy(out=wr[:], in_=wr_raw[:].rearrange("p g (t h) -> p g h t", t=4))
-            nc.vector.tensor_copy(out=kp[:], in_=kp_raw[:].rearrange("p g (t h) -> p g h t", t=4))
-
-        for item in HEAD:
-            f = item.split(":")
-            i = int(f[1])
-            if f[0] == "wd":
-                widen(i, i + 1, range(4), f[2])
-            elif f[0] == "iv":
-                group_wv(i, i + 1, f[2])
-            elif f[0] == "ik":
-                group_wk(i, i + 1, f[2])
-            elif f[0] == "qv":
-                quant_wv(i, i + 1)
-            elif f[0] == "qk":
-                quant_wk(i, i + 1)
-            elif f[0] == "t":
-                transpose_c(i)
-            elif f[0] == "o":
-                c_out(i, f[2])
-            elif f[0] == "q":
-                quant_c(i)
-            elif f[0] == "cv":
-                scales()
-            elif f[0] == "p":
-                project(i)
-            elif f[0] == "s":
-                if MODES[i] != "A":
-                    val_scalar(i)
-            elif f[0] == "k":
-                key(i)
-            elif f[0] == "a":
-                if MODES[i] == "A":
-                    val_direct(i)
-            elif f[0] == "g":
-                if MODES[i] in "VPG":
-                    val_group(i)
-            elif f[0] == "z":
-                quant_kv(i)
-
-        for p in range(2, PAIRS + 8):
-            u = p - LF
-            if 0 <= u < PAIRS and u % 2 == 1:
-                fold(u // 2)
-            gjobs = []
-            if 1 <= p - LQ < PAIRS:
-                quant_kv(p - LQ)
-            for a in range(HW, H):
-                first = 2 * a - LEAD
-                b = a + 1
-                if p == max(2, first):
-                    widen(a, b, range(4), WID_ENG)
-                    group_wk(a, b, WK_ENG)
-                if p == max(2, first + 1):
-                    if WV_ENG == "g":
-                        gjobs.append((group_wv, a, b))
-                    else:
-                        group_wv(a, b, WV_ENG)
-                    quant_wk(a, b)
-                if p == max(2, first + 2):
-                    quant_wv(a, b)
-            if 1 <= p - 1 < PAIRS:
-                for s in (2 * (p - 1), 2 * (p - 1) + 1):
-                    if MODES[s] in "VP":
-                        val_group(s)
-                    elif MODES[s] == "G":
-                        gjobs.append((val_group, s))
-            if gjobs and 1 <= p - LQ < PAIRS:
-                hold(p - LQ)
-            for job in gjobs:
-                if job[0] is val_group:
-                    val_group(job[1])
-                else:
-                    job[0](job[1], job[2], "g")
-            if p < PAIRS:
-                for s in (2 * p, 2 * p + 1):
-                    project(s)
-                    if MODES[s] != "A":
-                        val_scalar(s)
-                if KKAA:
-                    key(2 * p)
-                    key(2 * p + 1)
-                    for s in (2 * p, 2 * p + 1):
-                        if MODES[s] == "A":
-                            val_direct(s)
-                else:
-                    for s in (2 * p, 2 * p + 1):
-                        key(s)
-                        if MODES[s] == "A":
-                            val_direct(s)
-            u = p - LF - LO
-            if 0 <= u < PAIRS and u % 2 == 1:
-                store(u // 2)
+        h = H - 1
+        quant_grouped(h - 1)
+        fold(h - 1)
+        quant_k(h)
+        quant_direct(h)
+        quant_grouped(h)
+        store(h - 1)
+        fold(h)
+        store(h)

@@ -70,20 +70,22 @@ def tile_latent_kv_state_s7_kernel(tc, c, wk, wv_bytes, wv_scale, keep, write, o
             nc.sync.dma_start(out=wk_raw[a][0][:], in_=wk_view[:, :, a * DK : b * DK])
 
         nc.scalar.dma_start(out=wvs[:], in_=wv_scale.rearrange("(p j) o -> p (j o)", j=4))
-        load_c(0, 0)
         load_wv(*W_LOADS[0])
+        load_c(0, 0)
         load_c(0, 1)
         load_wk(*W_LOADS[0])
         load_c(1, 0)
         load_c(1, 1)
-        nc.scalar.dma_start(out=kp_raw[:], in_=keep.rearrange("(g p t) h -> p g (t h)", p=P, t=4))
+        load_c(2, 0)
+        nc.sync.dma_start(out=kp_raw[:], in_=keep.rearrange("(g p t) h -> p g (t h)", p=P, t=4))
         nc.sync.dma_start(out=wr_raw[:], in_=write.rearrange("(g p t) h -> p g (t h)", p=P, t=4))
-        for g in range(2, G):
-            load_c(g, 0)
-            load_c(g, 1)
-        for a, b in W_LOADS[1:]:
-            load_wv(a, b)
-            load_wk(a, b)
+        load_wv(*W_LOADS[1])
+        load_c(2, 1)
+        load_c(3, 0)
+        load_wk(*W_LOADS[1])
+        load_c(3, 1)
+        load_wv(*W_LOADS[2])
+        load_wk(*W_LOADS[2])
 
         make_identity(nc, ident[:])
         nc.gpsimd.tensor_copy(out=kp[:], in_=kp_raw[:].rearrange("p g (t h) -> p g h t", t=4))
@@ -113,11 +115,11 @@ def tile_latent_kv_state_s7_kernel(tc, c, wk, wv_bytes, wv_scale, keep, write, o
                     nc.vector.tensor_scalar(out=wide[h][:, j, :], in0=src, scalar1=wvs[:, j : j + 1], scalar2=None, op0=ALU.mult)
 
         def group_wv(h, engine):
-            wv_grp[h] = stage.tile([P, DV, 4], BF16, name="wv_grp", align_bytes=64)
+            wv_grp[h] = stage.tile([P, DV, 4], BF16, name="wv_grp", bufs=3, align_bytes=64)
             interleave(engine, wv_grp[h][:], wide.pop(h)[:])
 
         def group_wk(h, engine):
-            wk_grp[h] = stage.tile([P, DK, 4], BF16, name="wk_grp", align_bytes=64)
+            wk_grp[h] = stage.tile([P, DK, 4], BF16, name="wk_grp", bufs=3, align_bytes=64)
             raw, i = wk_raw[h]
             interleave(engine, wk_grp[h][:], raw[:, :, i * DK : (i + 1) * DK])
 
@@ -130,6 +132,9 @@ def tile_latent_kv_state_s7_kernel(tc, c, wk, wv_bytes, wv_scale, keep, write, o
         def s_bank():
             return psum.tile([P, 512], F32, name="s_bank", bufs=3)
 
+        def o_bank():
+            return psum.tile([P, 512], F32, name="o_bank", bufs=1)
+
         def v_bank():
             return psum.tile([P, 4, P], F32, name="v_bank", bufs=4)
 
@@ -137,7 +142,7 @@ def tile_latent_kv_state_s7_kernel(tc, c, wk, wv_bytes, wv_scale, keep, write, o
 
         def transpose_c(g, b):
             words = c_sb[g, b][:].bitcast(F32)
-            xt[g, b] = s_bank()
+            xt[g, b] = o_bank() if (g, b) in ((0, 0), (2, 0)) else s_bank()
             for i in range(2):
                 for u in range(2):
                     col = (2 * i + u) * P
@@ -198,7 +203,10 @@ def tile_latent_kv_state_s7_kernel(tc, c, wk, wv_bytes, wv_scale, keep, write, o
 
         def key(h, g):
             if g == 0:
-                k_in[h] = stage.tile([P, G, DK, 4], BF16, name="k_in", align_bytes=64)
+                if h == 0:
+                    k_in[h] = stage.tile([P, G, DK, 4], BF16, name="v_grp", bufs=1, align_bytes=64)
+                else:
+                    k_in[h] = stage.tile([P, G, DK, 4], BF16, name="k_in", align_bytes=64)
             nc.vector.scalar_tensor_tensor(
                 out=k_in[h][:, g, :, :],
                 in0=kb.pop((h, g))[:].rearrange("p t n -> p n t"),
@@ -210,10 +218,7 @@ def tile_latent_kv_state_s7_kernel(tc, c, wk, wv_bytes, wv_scale, keep, write, o
 
         def val_direct(h, d):
             if d == 0:
-                if h == 0:
-                    v_dir[h] = stage.tile([P, ND, P, 4], BF16, name="v_grp", bufs=1, align_bytes=64)
-                else:
-                    v_dir[h] = stage.tile([P, ND, P, 4], BF16, name="v_dir", align_bytes=64)
+                v_dir[h] = stage.tile([P, ND, P, 4], BF16, name="v_dir", align_bytes=64)
             nc.vector.tensor_tensor(
                 out=v_dir[h][:, d, :, :],
                 in0=db.pop((h, d))[:].rearrange("p t n -> p n t"),
@@ -253,23 +258,22 @@ def tile_latent_kv_state_s7_kernel(tc, c, wk, wv_bytes, wv_scale, keep, write, o
             cod[h] = (kc, ks, vc, vs)
 
         def quant_k(h):
-            codes(h)
+            if h not in cod:
+                codes(h)
             kc, ks, vc, vs = cod[h]
             quantize(kc[:], ks[:], k_in.pop(h)[:].rearrange("p g n t -> p (g n t)"))
 
-        def quant_v(h, src, first, runs):
+        def quant_v(h, src, first, a, b):
             kc, ks, vc, vs = cod[h]
-            m = 0
-            for r in runs:
-                cols = slice((first + m) * P, (first + m + r) * P)
-                quantize(vc[:, cols], vs[:, cols], src[:, m : m + r, :, :].rearrange("p m n t -> p (m n t)"))
-                m = m + r
+            cols = slice((first + a) * P, (first + b) * P)
+            quantize(vc[:, cols], vs[:, cols], src[:, a:b, :, :].rearrange("p m n t -> p (m n t)"))
 
-        def quant_direct(h):
-            quant_v(h, v_dir.pop(h), NS, (1, 2))
+        def quant_direct(h, a, b):
+            quant_v(h, v_dir[h], NS, a, b)
 
         def quant_grouped(h):
-            quant_v(h, v_grp.pop(h), 0, (4, 1))
+            quant_v(h, v_grp[h], 0, 0, 4)
+            quant_v(h, v_grp[h], 0, 4, NS)
 
         ob = {}
 
@@ -277,7 +281,7 @@ def tile_latent_kv_state_s7_kernel(tc, c, wk, wv_bytes, wv_scale, keep, write, o
             if h == H - 1:
                 ob[h] = s_bank()
             else:
-                ob[h] = psum.tile([P, 512], F32, name="o_bank", bufs=1)
+                ob[h] = o_bank()
             kc, ks, vc, vs = cod.pop(h)
             for g in range(G):
                 nc.tensor.matmul_mx(
@@ -296,68 +300,80 @@ def tile_latent_kv_state_s7_kernel(tc, c, wk, wv_bytes, wv_scale, keep, write, o
             nc.sync.dma_start(out=out[h], in_=o[:])
 
         widen(0, "svsv")
-        transpose_c(0, 0)
-        c_out(0, 0, "s")
-        transpose_c(0, 1)
-        c_out(0, 1, "s")
+        widen(1, "svsv")
+        for g in range(2):
+            for b in range(2):
+                transpose_c(g, b)
+                c_out(g, b, "s")
         group_wv(0, "v")
-        group_wk(0, "v")
+        group_wv(1, "v")
         quant_wv(0)
+        group_wk(0, "v")
         quant_c(0, 0)
         quant_wk(0)
         quant_c(0, 1)
-        widen(1, "vvvv")
-        for b in range(2):
-            transpose_c(1, b)
-            c_out(1, b, "s")
-        mm_key(0, 0)
-        group_wv(1, "v")
-        key(0, 0)
-        quant_c(1, 0)
-        quant_c(1, 1)
-        for b in range(2):
-            transpose_c(2, b)
-            c_out(2, b, "s")
-        mm_key(0, 1)
         group_wk(1, "v")
-        key(0, 1)
+        quant_c(1, 0)
+        quant_wv(1)
+        quant_c(1, 1)
+        quant_wk(1)
+        transpose_c(2, 0)
+        c_out(2, 0, "s")
+        mm_key(0, 0)
+        widen(2, "ssss")
+        transpose_c(2, 1)
+        c_out(2, 1, "s")
+        transpose_c(3, 0)
+        c_out(3, 0, "s")
+        group_wk(2, "s")
+        mm_key(0, 1)
+        transpose_c(3, 1)
+        c_out(3, 1, "s")
         quant_c(2, 0)
+        key(0, 0)
         quant_c(2, 1)
-        for b in range(2):
-            transpose_c(3, b)
-            c_out(3, b, "s")
-        mm_key(0, 2)
-        mm_direct(0, 0)
-        for n in range(2):
-            mm_scalar(0, n)
-            val_scalar(0, n)
-        key(0, 2)
+        key(0, 1)
         quant_c(3, 0)
+        mm_scalar(0, 0)
+        mm_key(0, 2)
+        mm_scalar(0, 1)
+        mm_direct(0, 0)
+        mm_scalar(0, 2)
         quant_c(3, 1)
-        val_direct(0, 0)
         mm_key(0, 3)
         mm_direct(0, 1)
+        key(0, 2)
         mm_direct(0, 2)
-        for n in range(2, NS):
-            mm_scalar(0, n)
+        for n in range(2):
             val_scalar(0, n)
+            mm_scalar(0, 3 + n)
+        for n in range(2, NS):
+            val_scalar(0, n)
+        group_wv(2, "s")
+        val_direct(0, 0)
         key(0, 3)
         val_direct(0, 1)
         val_direct(0, 2)
+        codes(0)
+        quant_direct(0, 0, 1)
 
         for h in range(1, H):
             last = h == H - 1
-            quant_wk(h)
-            quant_wv(h)
-            quant_k(h - 1)
-            quant_direct(h - 1)
             if h >= 2:
+                quant_wk(h)
+                quant_wv(h)
+            quant_k(h - 1)
+            if h >= 2:
+                quant_direct(h - 1, 0, 1)
                 quant_grouped(h - 2)
+                quant_direct(h - 1, 1, ND)
+            else:
+                quant_direct(0, 1, ND)
             group_v(h - 1)
-            if not last:
+            if 2 <= h < H - 1:
                 widen(h + 1, "ssss")
-                group_wv(h + 1, "s")
                 group_wk(h + 1, "s")
+                group_wv(h + 1, "s")
             for g in range(3):
                 mm_key(h, g)
             mm_direct(h, 0)
@@ -371,10 +387,10 @@ def tile_latent_kv_state_s7_kernel(tc, c, wk, wv_bytes, wv_scale, keep, write, o
             mm_key(h, 3)
             key(h, 1)
             mm_direct(h, 1)
-            val_scalar(h, 0)
-            mm_scalar(h, 3)
             key(h, 2)
             mm_direct(h, 2)
+            val_scalar(h, 0)
+            mm_scalar(h, 3)
             val_scalar(h, 1)
             mm_scalar(h, 4)
             if last:
@@ -395,8 +411,9 @@ def tile_latent_kv_state_s7_kernel(tc, c, wk, wv_bytes, wv_scale, keep, write, o
         quant_grouped(h - 1)
         fold(h - 1)
         quant_k(h)
-        quant_direct(h)
+        quant_direct(h, 0, 1)
         quant_grouped(h)
+        quant_direct(h, 1, ND)
         store(h - 1)
         fold(h)
         store(h)

@@ -17,9 +17,23 @@ P = 128
 G = 4
 FLOPS = 2 * T * L * H * (DK + DV) + 2 * T * H * DK * DV
 
-NS = 5
-ND = 2 * G - NS
 W_LOADS = ((0, 2), (2, 4), (4, 8))
+
+
+def direct_groups(r):
+    return 1 if r % 2 == 0 and r > 0 else 2
+
+
+def unit(r, u):
+    if r < 2:
+        return u % 2, 2 * r + u // 2
+    return r, u
+
+
+def place(h, g):
+    if h < 2:
+        return g // 2, 2 * (g % 2) + h
+    return h, g
 
 
 def tile_latent_kv_state_s7_kernel(tc, c, wk, wv_bytes, wv_scale, keep, write, out):
@@ -81,15 +95,17 @@ def tile_latent_kv_state_s7_kernel(tc, c, wk, wv_bytes, wv_scale, keep, write, o
         nc.sync.dma_start(out=wr_raw[:], in_=write.rearrange("(g p t) h -> p g (t h)", p=P, t=4))
         load_wv(*W_LOADS[1])
         load_c(2, 1)
-        load_c(3, 0)
         load_wk(*W_LOADS[1])
+        load_c(3, 0)
         load_c(3, 1)
         load_wv(*W_LOADS[2])
         load_wk(*W_LOADS[2])
 
         make_identity(nc, ident[:])
-        nc.gpsimd.tensor_copy(out=kp[:], in_=kp_raw[:].rearrange("p g (t h) -> p g h t", t=4))
-        nc.gpsimd.tensor_copy(out=wr[:], in_=wr_raw[:].rearrange("p g (t h) -> p g h t", t=4))
+
+        def factors():
+            nc.vector.tensor_copy(out=kp[:], in_=kp_raw[:].rearrange("p g (t h) -> p g h t", t=4))
+            nc.vector.tensor_copy(out=wr[:], in_=wr_raw[:].rearrange("p g (t h) -> p g h t", t=4))
 
         def interleave(engine, dst, src):
             d4 = dst.rearrange("p (c i) t -> p c t i", i=4)
@@ -175,121 +191,124 @@ def tile_latent_kv_state_s7_kernel(tc, c, wk, wv_bytes, wv_scale, keep, write, o
 
         kb, db, sb = {}, {}, {}
 
-        def mm_key(h, g):
-            kb[h, g] = v_bank()
+        def mm_key(r, u):
+            h, g = unit(r, u)
+            kb[r, u] = v_bank()
             for t in range(4):
-                mm(kb[h, g][:, t, :], g, t, wk_cod[:, h, :], wk_scl[:, h, :])
+                mm(kb[r, u][:, t, :], g, t, wk_cod[:, h, :], wk_scl[:, h, :])
 
-        def mm_direct(h, d):
-            g, f = divmod(NS + d, 2)
-            db[h, d] = v_bank()
+        def mm_direct(r, d):
+            u, f = divmod(d, 2)
+            h, g = unit(r, u)
+            db[r, d] = v_bank()
             cols = slice(f * P, (f + 1) * P)
             for t in range(4):
-                mm(db[h, d][:, t, :], g, t, wv_cod[:, h, cols], wv_scl[:, h, cols])
+                mm(db[r, d][:, t, :], g, t, wv_cod[:, h, cols], wv_scl[:, h, cols])
 
-        def s_shape(n):
-            g, f = divmod(n, 2)
-            if 2 * g + 1 < NS:
-                return g, (2 * f, 2 * f + 1), DV
-            return g, (0, 1, 2, 3), P
-
-        def mm_scalar(h, n):
-            g, ts, w = s_shape(n)
-            sb[h, n] = s_bank()
-            for i in range(len(ts)):
-                mm(sb[h, n][:, i * w : (i + 1) * w], g, ts[i], wv_cod[:, h, :w], wv_scl[:, h, :w])
+        def mm_scalar(r, n):
+            u, f = divmod(2 * direct_groups(r) + n, 2)
+            h, g = unit(r, u)
+            sb[r, n] = s_bank()
+            for i in range(2):
+                mm(sb[r, n][:, i * DV : (i + 1) * DV], g, 2 * f + i, wv_cod[:, h, :], wv_scl[:, h, :])
 
         k_in, v_dir, v_rows, v_grp, cod = {}, {}, {}, {}, {}
 
-        def key(h, g):
-            if g == 0:
-                if h == 0:
-                    k_in[h] = stage.tile([P, G, DK, 4], BF16, name="v_grp", bufs=1, align_bytes=64)
+        def key(r, u):
+            h, g = unit(r, u)
+            if u == 0:
+                if r == 0:
+                    k_in[r] = stage.tile([P, G, DK, 4], BF16, name="v_grp", bufs=1, align_bytes=64)
                 else:
-                    k_in[h] = stage.tile([P, G, DK, 4], BF16, name="k_in", align_bytes=64)
+                    k_in[r] = stage.tile([P, G, DK, 4], BF16, name="k_in", align_bytes=64)
             nc.vector.scalar_tensor_tensor(
-                out=k_in[h][:, g, :, :],
-                in0=kb.pop((h, g))[:].rearrange("p t n -> p n t"),
+                out=k_in[r][:, u, :, :],
+                in0=kb.pop((r, u))[:].rearrange("p t n -> p n t"),
                 scalar=0.0,
                 in1=kp[:, g, h, :].unsqueeze(1).to_broadcast([P, DK, 4]),
                 op0=ALU.max,
                 op1=ALU.mult,
             )
 
-        def val_direct(h, d):
+        def val_direct(r, d):
             if d == 0:
-                v_dir[h] = stage.tile([P, ND, P, 4], BF16, name="v_dir", align_bytes=64)
+                v_dir[r] = stage.tile([P, direct_groups(r), DV, 4], BF16, name="v_dir", align_bytes=64)
+            u, f = divmod(d, 2)
+            h, g = unit(r, u)
             nc.vector.tensor_tensor(
-                out=v_dir[h][:, d, :, :],
-                in0=db.pop((h, d))[:].rearrange("p t n -> p n t"),
-                in1=wr[:, (NS + d) // 2, h, :].unsqueeze(1).to_broadcast([P, P, 4]),
+                out=v_dir[r][:, u, f * P : (f + 1) * P, :],
+                in0=db.pop((r, d))[:].rearrange("p t n -> p n t"),
+                in1=wr[:, g, h, :].unsqueeze(1).to_broadcast([P, P, 4]),
                 op=ALU.mult,
             )
 
-        def val_scalar(h, n):
+        def val_scalar(r, n):
             if n == 0:
-                v_rows[h] = stage.tile([P, NS, 4, P], BF16, name="v_rows", align_bytes=64)
-            g, ts, w = s_shape(n)
-            bank = sb.pop((h, n))
-            for i in range(len(ts)):
+                v_rows[r] = stage.tile([P, G - direct_groups(r), 4, DV], BF16, name="v_rows", align_bytes=64)
+            u, f = divmod(n, 2)
+            h, g = unit(r, direct_groups(r) + u)
+            bank = sb.pop((r, n))
+            for i in range(2):
+                t = 2 * f + i
                 nc.scalar.activation(
-                    out=v_rows[h][:, 2 * g : 2 * g + w // P, ts[i], :],
-                    in_=bank[:, i * w : (i + 1) * w].rearrange("p (f n) -> p f n", n=P),
+                    out=v_rows[r][:, u, t, :],
+                    in_=bank[:, i * DV : (i + 1) * DV],
                     func=COPY,
-                    scale=wr[:, g, h, ts[i] : ts[i] + 1],
+                    scale=wr[:, g, h, t : t + 1],
                 )
 
         def group_v(h):
-            v_grp[h] = stage.tile([P, NS, P, 4], BF16, name="v_grp", bufs=1, align_bytes=64)
+            v_grp[h] = stage.tile([P, G - direct_groups(h), DV, 4], BF16, name="v_grp", bufs=1, align_bytes=64)
             nc.gpsimd.tensor_scalar(
-                out=v_grp[h][:], in0=v_rows.pop(h)[:].rearrange("p m t n -> p m n t"), scalar1=1.0, scalar2=0.0, op0=ALU.mult, op1=ALU.add
+                out=v_grp[h][:], in0=v_rows.pop(h)[:].rearrange("p u t n -> p u n t"), scalar1=1.0, scalar2=0.0, op0=ALU.mult, op1=ALU.add
             )
 
-        def group_v_scalar(h, m):
-            if m == 0:
-                v_grp[h] = stage.tile([P, NS, P, 4], BF16, name="v_last", bufs=1, align_bytes=64)
-            interleave("s", v_grp[h][:, m, :, :], v_rows[h][:, m, :, :])
+        def group_v_scalar(h, u):
+            if u == 0:
+                v_grp[h] = stage.tile([P, G - direct_groups(h), DV, 4], BF16, name="v_last", bufs=1, align_bytes=64)
+            interleave("s", v_grp[h][:, u, :, :], v_rows[h][:, u, :, :])
 
         def codes(h):
-            kc = stage.tile([P, G * DK], U32, name="k_cod", bufs=3, align_bytes=64)
-            ks = stage.tile([P, G * DK], U8, name="k_scl", bufs=3, align_bytes=64)
-            vc = stage.tile([P, G * DV], U32, name="v_cod", bufs=3, align_bytes=64)
-            vs = stage.tile([P, G * DV], U8, name="v_scl", bufs=3, align_bytes=64)
+            kc = stage.tile([P, G * DK], U32, name="k_cod", bufs=4, align_bytes=64)
+            ks = stage.tile([P, G * DK], U8, name="k_scl", bufs=4, align_bytes=64)
+            vc = stage.tile([P, G * DV], U32, name="v_cod", bufs=4, align_bytes=64)
+            vs = stage.tile([P, G * DV], U8, name="v_scl", bufs=4, align_bytes=64)
             cod[h] = (kc, ks, vc, vs)
 
         def quant_k(h):
-            if h not in cod:
-                codes(h)
+            codes(h)
             kc, ks, vc, vs = cod[h]
             quantize(kc[:], ks[:], k_in.pop(h)[:].rearrange("p g n t -> p (g n t)"))
 
         def quant_v(h, src, first, a, b):
             kc, ks, vc, vs = cod[h]
-            cols = slice((first + a) * P, (first + b) * P)
-            quantize(vc[:, cols], vs[:, cols], src[:, a:b, :, :].rearrange("p m n t -> p (m n t)"))
+            cols = slice((first + a) * DV, (first + b) * DV)
+            quantize(vc[:, cols], vs[:, cols], src[:, a:b, :, :].rearrange("p u n t -> p (u n t)"))
 
-        def quant_direct(h, a, b):
-            quant_v(h, v_dir[h], NS, a, b)
+        def quant_direct(h):
+            quant_v(h, v_dir.pop(h), 0, 0, direct_groups(h))
 
         def quant_grouped(h):
-            quant_v(h, v_grp[h], 0, 0, 4)
-            quant_v(h, v_grp[h], 0, 4, NS)
+            quant_v(h, v_grp[h], direct_groups(h), 0, 2)
+            if direct_groups(h) == 1:
+                quant_v(h, v_grp[h], 1, 2, 3)
 
         ob = {}
 
         def fold(h):
-            if h == H - 1:
+            if h == 0:
                 ob[h] = s_bank()
             else:
                 ob[h] = o_bank()
-            kc, ks, vc, vs = cod.pop(h)
             for g in range(G):
+                r, u = place(h, g)
+                kc, ks, vc, vs = cod[r]
                 nc.tensor.matmul_mx(
                     out=ob[h][:, :DV],
-                    lhsT=kc[:, g * DK : (g + 1) * DK].bitcast(FP8X4),
-                    lhsT_scale=ks[:, g * DK : (g + 1) * DK],
-                    rhs=vc[:, g * DV : (g + 1) * DV].bitcast(FP8X4),
-                    rhs_scale=vs[:, g * DV : (g + 1) * DV],
+                    lhsT=kc[:, u * DK : (u + 1) * DK].bitcast(FP8X4),
+                    lhsT_scale=ks[:, u * DK : (u + 1) * DK],
+                    rhs=vc[:, u * DV : (u + 1) * DV].bitcast(FP8X4),
+                    rhs_scale=vs[:, u * DV : (u + 1) * DV],
                     start=(g == 0),
                     stop=(g == G - 1),
                 )
@@ -313,107 +332,118 @@ def tile_latent_kv_state_s7_kernel(tc, c, wk, wv_bytes, wv_scale, keep, write, o
         quant_wk(0)
         quant_c(0, 1)
         group_wk(1, "v")
-        quant_c(1, 0)
         quant_wv(1)
-        quant_c(1, 1)
+        factors()
         quant_wk(1)
-        transpose_c(2, 0)
-        c_out(2, 0, "s")
+        quant_c(1, 0)
+        quant_c(1, 1)
         mm_key(0, 0)
+        mm_direct(0, 0)
+        mm_direct(0, 1)
+        transpose_c(2, 0)
+        mm_key(0, 1)
+        c_out(2, 0, "s")
         widen(2, "ssss")
         transpose_c(2, 1)
-        c_out(2, 1, "s")
-        transpose_c(3, 0)
-        c_out(3, 0, "s")
-        group_wk(2, "s")
-        mm_key(0, 1)
-        transpose_c(3, 1)
-        c_out(3, 1, "s")
-        quant_c(2, 0)
         key(0, 0)
-        quant_c(2, 1)
-        key(0, 1)
-        quant_c(3, 0)
-        mm_scalar(0, 0)
-        mm_key(0, 2)
-        mm_scalar(0, 1)
-        mm_direct(0, 0)
-        mm_scalar(0, 2)
-        quant_c(3, 1)
-        mm_key(0, 3)
-        mm_direct(0, 1)
-        key(0, 2)
         mm_direct(0, 2)
-        for n in range(2):
-            val_scalar(0, n)
-            mm_scalar(0, 3 + n)
-        for n in range(2, NS):
-            val_scalar(0, n)
-        group_wv(2, "s")
+        c_out(2, 1, "s")
         val_direct(0, 0)
-        key(0, 3)
+        mm_direct(0, 3)
+        transpose_c(3, 0)
+        transpose_c(3, 1)
         val_direct(0, 1)
+        mm_key(0, 2)
+        c_out(3, 0, "s")
+        mm_scalar(0, 0)
+        c_out(3, 1, "s")
+        key(0, 1)
+        mm_key(0, 3)
+        mm_scalar(0, 1)
+        mm_scalar(0, 2)
+        val_scalar(0, 0)
+        mm_scalar(0, 3)
+        for n in range(1, 4):
+            val_scalar(0, n)
+        quant_c(2, 0)
         val_direct(0, 2)
-        codes(0)
-        quant_direct(0, 0, 1)
+        quant_c(2, 1)
+        val_direct(0, 3)
+        quant_c(3, 0)
+        key(0, 2)
+        key(0, 3)
+        quant_c(3, 1)
+        group_wk(2, "s")
+        group_wv(2, "s")
 
         for h in range(1, H):
             last = h == H - 1
+            pieces = 2 * direct_groups(h)
             if h >= 2:
                 quant_wk(h)
                 quant_wv(h)
             quant_k(h - 1)
             if h >= 2:
-                quant_direct(h - 1, 0, 1)
                 quant_grouped(h - 2)
-                quant_direct(h - 1, 1, ND)
-            else:
-                quant_direct(0, 1, ND)
+            quant_direct(h - 1)
             group_v(h - 1)
             if 2 <= h < H - 1:
                 widen(h + 1, "ssss")
                 group_wk(h + 1, "s")
                 group_wv(h + 1, "s")
-            for g in range(3):
+            for g in range(G):
                 mm_key(h, g)
-            mm_direct(h, 0)
             for n in range(3):
                 mm_scalar(h, n)
-            if h >= 2:
+            if h >= 3:
                 fold(h - 2)
-                if not last:
-                    store(h - 2)
-            key(h, 0)
-            mm_key(h, 3)
-            key(h, 1)
-            mm_direct(h, 1)
-            key(h, 2)
-            mm_direct(h, 2)
-            val_scalar(h, 0)
-            mm_scalar(h, 3)
-            val_scalar(h, 1)
-            mm_scalar(h, 4)
-            if last:
-                store(h - 2)
-                group_v_scalar(h, 0)
-                group_v_scalar(h, 1)
-            val_direct(h, 0)
-            key(h, 3)
-            val_direct(h, 1)
-            val_direct(h, 2)
-            for n in range(2, NS):
+            for g in range(G):
+                key(h, g)
+                if g < pieces:
+                    mm_direct(h, g)
+            for n in range(2 * G - pieces):
                 val_scalar(h, n)
+                if n + 3 < 2 * G - pieces:
+                    mm_scalar(h, n + 3)
+                if n == 2 and h >= 3:
+                    store(h - 2)
+                if last and n == 2:
+                    group_v_scalar(h, 0)
             if last:
-                for m in range(2, NS):
-                    group_v_scalar(h, m)
+                group_v_scalar(h, 1)
+            if h == 3:
+                fold(0)
+                store(0)
+            for d in range(pieces):
+                val_direct(h, d)
 
         h = H - 1
         quant_grouped(h - 1)
         fold(h - 1)
         quant_k(h)
-        quant_direct(h, 0, 1)
-        quant_grouped(h)
-        quant_direct(h, 1, ND)
+        quant_direct(h)
+        quant_v(h, v_grp[h], 2, 0, 1)
         store(h - 1)
-        fold(h)
-        store(h)
+        kc, ks, vc, vs = cod[h]
+        for f in range(2):
+            cols = slice(3 * DV + f * P, 3 * DV + (f + 1) * P)
+            quantize(vc[:, cols], vs[:, cols], v_grp[h][:, 1, f * P : (f + 1) * P, :].rearrange("p n t -> p (n t)"))
+        halves = [s_bank(), s_bank()]
+        for g in range(G):
+            for f in range(2):
+                cols = slice(g * DV + f * P, g * DV + (f + 1) * P)
+                nc.tensor.matmul_mx(
+                    out=halves[f][:, :P],
+                    lhsT=kc[:, g * DK : (g + 1) * DK].bitcast(FP8X4),
+                    lhsT_scale=ks[:, g * DK : (g + 1) * DK],
+                    rhs=vc[:, cols].bitcast(FP8X4),
+                    rhs_scale=vs[:, cols],
+                    start=(g == 0),
+                    stop=(g == G - 1),
+                )
+        o0 = stage.tile([P, P], F32, name="o_half")
+        nc.scalar.copy(out=o0[:], in_=halves[0][:, :P])
+        nc.sync.dma_start(out=out[h][:, :P], in_=o0[:])
+        o1 = stage.tile([P, P], F32, name="o_half")
+        nc.vector.tensor_copy(out=o1[:], in_=halves[1][:, :P])
+        nc.scalar.dma_start(out=out[h][:, P:], in_=o1[:])

@@ -45,6 +45,7 @@ def tile_latent_kv_state_s7_kernel(tc, c, wk, wv_bytes, wv_scale, keep, write, o
 
         ident = const.tile([P, P], F32, name="ident")
         wvs = const.tile([P, 4], F32, name="wvs")
+        warm = const.tile([P, 1], F32, name="warm")
         kp_raw = const.tile([P, G, 32], BF16, name="kp_raw")
         wr_raw = const.tile([P, G, 32], BF16, name="wr_raw")
         kp = const.tile([P, G, H, 4], F32, name="kp")
@@ -101,6 +102,8 @@ def tile_latent_kv_state_s7_kernel(tc, c, wk, wv_bytes, wv_scale, keep, write, o
         load_wv(*W_LOADS[2])
         load_wk(*W_LOADS[2])
 
+        nc.vector.memset(warm[:], 0.0)
+        nc.scalar.activation(out=warm[:], in_=warm[:], func=COPY)
         make_identity(nc, ident[:])
 
         def factors():

@@ -168,7 +168,10 @@ def tile_latent_kv_state_s7_kernel(tc, c, wk, wv_bytes, wv_scale, keep, write, o
                     nc.tensor.transpose(xt[g, b][:, col : col + P], words[:, i, u::2], ident[:])
 
         def c_out(g, b, engine):
-            c_grp[g, b] = stage.tile([P, 2, P, 4], BF16, name="c_grp", bufs=4, align_bytes=64)
+            if (g, b) == (G - 1, 1):
+                c_grp[g, b] = stage.tile([P, 2, P, 4], BF16, name="v_grp", bufs=1, align_bytes=64)
+            else:
+                c_grp[g, b] = stage.tile([P, 2, P, 4], BF16, name="c_grp", bufs=4, align_bytes=64)
             dst = c_grp[g, b][:].bitcast(F32)
             src = xt.pop((g, b))[:].rearrange("q (i u r) -> q i r u", i=2, u=2)
             if engine == "s":
@@ -215,17 +218,14 @@ def tile_latent_kv_state_s7_kernel(tc, c, wk, wv_bytes, wv_scale, keep, write, o
             for i in range(2):
                 mm(sb[r, n][:, i * DV : (i + 1) * DV], g, 2 * f + i, wv_cod[:, h, :], wv_scl[:, h, :])
 
-        k_in, v_dir, v_rows, v_grp, cod = {}, {}, {}, {}, {}
+        kv_in, v_rows, v_grp, cod, whole = {}, {}, {}, {}, {}
 
         def key(r, u):
             h, g = unit(r, u)
             if u == 0:
-                if r == 0:
-                    k_in[r] = stage.tile([P, G, DK, 4], BF16, name="v_grp", bufs=1, align_bytes=64)
-                else:
-                    k_in[r] = stage.tile([P, G, DK, 4], BF16, name="k_in", align_bytes=64)
+                kv_in[r] = stage.tile([P, G + 2 * direct_groups(r), P, 4], BF16, name="kv_in", align_bytes=64)
             nc.vector.scalar_tensor_tensor(
-                out=k_in[r][:, u, :, :],
+                out=kv_in[r][:, u, :, :],
                 in0=kb.pop((r, u))[:].rearrange("p t n -> p n t"),
                 scalar=0.0,
                 in1=kp[:, g, h, :].unsqueeze(1).to_broadcast([P, DK, 4]),
@@ -234,12 +234,10 @@ def tile_latent_kv_state_s7_kernel(tc, c, wk, wv_bytes, wv_scale, keep, write, o
             )
 
         def val_direct(r, d):
-            if d == 0:
-                v_dir[r] = stage.tile([P, direct_groups(r), DV, 4], BF16, name="v_dir", align_bytes=64)
             u, f = divmod(d, 2)
             h, g = unit(r, u)
             nc.vector.tensor_tensor(
-                out=v_dir[r][:, u, f * P : (f + 1) * P, :],
+                out=kv_in[r][:, G + d, :, :],
                 in0=db.pop((r, d))[:].rearrange("p t n -> p n t"),
                 in1=wr[:, g, h, :].unsqueeze(1).to_broadcast([P, P, 4]),
                 op=ALU.mult,
@@ -271,25 +269,20 @@ def tile_latent_kv_state_s7_kernel(tc, c, wk, wv_bytes, wv_scale, keep, write, o
                 v_grp[h] = stage.tile([P, G - direct_groups(h), DV, 4], BF16, name="v_last", bufs=1, align_bytes=64)
             interleave("s", v_grp[h][:, u, :, :], v_rows[h][:, u, :, :])
 
-        def codes(h):
-            kc = stage.tile([P, G * DK], U32, name="k_cod", bufs=4, align_bytes=64)
-            ks = stage.tile([P, G * DK], U8, name="k_scl", bufs=4, align_bytes=64)
-            vc = stage.tile([P, G * DV], U32, name="v_cod", bufs=4, align_bytes=64)
-            vs = stage.tile([P, G * DV], U8, name="v_scl", bufs=4, align_bytes=64)
-            cod[h] = (kc, ks, vc, vs)
+        def codes(r):
+            kvc = stage.tile([P, G * (DK + DV)], U32, name="kv_cod", bufs=4, align_bytes=64)
+            kvs = stage.tile([P, G * (DK + DV)], U8, name="kv_scl", bufs=4, align_bytes=64)
+            cod[r] = (kvc[:, : G * DK], kvs[:, : G * DK], kvc[:, G * DK :], kvs[:, G * DK :])
+            whole[r] = (kvc, kvs)
 
-        def quant_k(h):
-            codes(h)
-            kc, ks, vc, vs = cod[h]
-            quantize(kc[:], ks[:], k_in.pop(h)[:].rearrange("p g n t -> p (g n t)"))
+        def quant_in(r, a, b):
+            kvc, kvs = whole[r]
+            quantize(kvc[:, a * P : b * P], kvs[:, a * P : b * P], kv_in[r][:, a:b, :, :].rearrange("p m n t -> p (m n t)"))
 
         def quant_v(h, src, first, a, b):
             kc, ks, vc, vs = cod[h]
             cols = slice((first + a) * DV, (first + b) * DV)
             quantize(vc[:, cols], vs[:, cols], src[:, a:b, :, :].rearrange("p u n t -> p (u n t)"))
-
-        def quant_direct(h):
-            quant_v(h, v_dir.pop(h), 0, 0, direct_groups(h))
 
         def quant_grouped(h):
             quant_v(h, v_grp[h], direct_groups(h), 0, 2)
@@ -321,12 +314,20 @@ def tile_latent_kv_state_s7_kernel(tc, c, wk, wv_bytes, wv_scale, keep, write, o
             nc.scalar.copy(out=o[:], in_=ob.pop(h)[:, :DV])
             nc.sync.dma_start(out=out[h], in_=o[:])
 
+        def warm_up(n):
+            bank = v_bank()
+            for i in range(n):
+                nc.tensor.matmul(out=bank[:, i % 4, :], lhsT=ident[:], rhs=ident[:], start=True, stop=True)
+
+        warm_up(4)
         widen(0, "svsv")
         widen(1, "svsv")
         for g in range(2):
             for b in range(2):
                 transpose_c(g, b)
                 c_out(g, b, "s")
+            if g == 0:
+                warm_up(2)
         group_wv(0, "v")
         group_wv(1, "v")
         quant_wv(0)
@@ -385,10 +386,12 @@ def tile_latent_kv_state_s7_kernel(tc, c, wk, wv_bytes, wv_scale, keep, write, o
             if h >= 2:
                 quant_wk(h)
                 quant_wv(h)
-            quant_k(h - 1)
+            codes(h - 1)
+            if direct_groups(h - 1) == 1:
+                quant_in(h - 1, G, G + 2)
             if h >= 2:
                 quant_grouped(h - 2)
-            quant_direct(h - 1)
+            quant_in(h - 1, 0, G if direct_groups(h - 1) == 1 else 2 * G)
             group_v(h - 1)
             if 2 <= h < H - 1:
                 widen(h + 1, "ssss")
@@ -423,8 +426,8 @@ def tile_latent_kv_state_s7_kernel(tc, c, wk, wv_bytes, wv_scale, keep, write, o
         h = H - 1
         quant_grouped(h - 1)
         fold(h - 1)
-        quant_k(h)
-        quant_direct(h)
+        codes(h)
+        quant_in(h, 0, 2 * G)
         quant_v(h, v_grp[h], 2, 0, 1)
         store(h - 1)
         kc, ks, vc, vs = cod[h]

@@ -142,8 +142,16 @@ def tile_latent_kv_state_s7_kernel(tc, c, wk, wv_bytes, wv_scale, keep, write, o
             raw, i = wk_raw[h]
             interleave(engine, wk_grp[h][:], raw[:, :, i * DK : (i + 1) * DK])
 
+        def group_wk_pair(h):
+            pair = stage.tile([P, 2 * DK, 4], BF16, name="wk_pair", bufs=1, align_bytes=64)
+            nc.gpsimd.tensor_scalar(
+                out=pair[:], in0=wk_raw[h][0][:].rearrange("p t n -> p n t"), scalar1=1.0, scalar2=0.0, op0=ALU.mult, op1=ALU.add
+            )
+            wk_grp[h] = pair[:, :DK, :]
+            wk_grp[h + 1] = pair[:, DK:, :]
+
         def quant_wk(h):
-            quantize(wk_cod[:, h, :], wk_scl[:, h, :], wk_grp.pop(h)[:].rearrange("p n t -> p (n t)"))
+            quantize(wk_cod[:, h, :], wk_scl[:, h, :], wk_grp.pop(h)[:, :, :].rearrange("p n t -> p (n t)"))
 
         def quant_wv(h):
             quantize(wv_cod[:, h, :], wv_scl[:, h, :], wv_grp.pop(h)[:].rearrange("p n t -> p (n t)"))
@@ -169,7 +177,7 @@ def tile_latent_kv_state_s7_kernel(tc, c, wk, wv_bytes, wv_scale, keep, write, o
 
         def c_out(g, b, engine):
             if (g, b) == (G - 1, 1):
-                c_grp[g, b] = stage.tile([P, 2, P, 4], BF16, name="v_grp", bufs=1, align_bytes=64)
+                c_grp[g, b] = stage.tile([P, 2, P, 4], BF16, name="wk_pair", bufs=1, align_bytes=64)
             else:
                 c_grp[g, b] = stage.tile([P, 2, P, 4], BF16, name="c_grp", bufs=4, align_bytes=64)
             dst = c_grp[g, b][:].bitcast(F32)
@@ -270,8 +278,8 @@ def tile_latent_kv_state_s7_kernel(tc, c, wk, wv_bytes, wv_scale, keep, write, o
             interleave("s", v_grp[h][:, u, :, :], v_rows[h][:, u, :, :])
 
         def codes(r):
-            kvc = stage.tile([P, G * (DK + DV)], U32, name="kv_cod", bufs=4, align_bytes=64)
-            kvs = stage.tile([P, G * (DK + DV)], U8, name="kv_scl", bufs=4, align_bytes=64)
+            kvc = stage.tile([P, G * (DK + DV)], U32, name="kv_cod", bufs=5, align_bytes=64)
+            kvs = stage.tile([P, G * (DK + DV)], U8, name="kv_scl", bufs=5, align_bytes=64)
             cod[r] = (kvc[:, : G * DK], kvs[:, : G * DK], kvc[:, G * DK :], kvs[:, G * DK :])
             whole[r] = (kvc, kvs)
 
@@ -377,12 +385,13 @@ def tile_latent_kv_state_s7_kernel(tc, c, wk, wv_bytes, wv_scale, keep, write, o
         key(0, 2)
         key(0, 3)
         quant_c(3, 1)
-        group_wk(2, "s")
         group_wv(2, "s")
 
         for h in range(1, H):
             last = h == H - 1
             pieces = 2 * direct_groups(h)
+            if h >= 4:
+                fold(h - 3)
             if h >= 2:
                 quant_wk(h)
                 quant_wv(h)
@@ -392,16 +401,21 @@ def tile_latent_kv_state_s7_kernel(tc, c, wk, wv_bytes, wv_scale, keep, write, o
             if h >= 2:
                 quant_grouped(h - 2)
             quant_in(h - 1, 0, G if direct_groups(h - 1) == 1 else 2 * G)
+            if h == 1:
+                group_wk_pair(2)
             group_v(h - 1)
             if 2 <= h < H - 1:
                 widen(h + 1, "ssss")
-                group_wk(h + 1, "s")
+                if h >= 3:
+                    group_wk(h + 1, "s")
                 group_wv(h + 1, "s")
+            if h >= 4:
+                store(h - 3)
             for g in range(G):
                 mm_key(h, g)
             for n in range(3):
                 mm_scalar(h, n)
-            if h >= 3:
+            if last:
                 fold(h - 2)
             for g in range(G):
                 key(h, g)
@@ -411,7 +425,7 @@ def tile_latent_kv_state_s7_kernel(tc, c, wk, wv_bytes, wv_scale, keep, write, o
                 val_scalar(h, n)
                 if n + 3 < 2 * G - pieces:
                     mm_scalar(h, n + 3)
-                if n == 2 and h >= 3:
+                if n == 2 and last:
                     store(h - 2)
                 if last and n == 2:
                     group_v_scalar(h, 0)
@@ -427,7 +441,9 @@ def tile_latent_kv_state_s7_kernel(tc, c, wk, wv_bytes, wv_scale, keep, write, o
         quant_grouped(h - 1)
         fold(h - 1)
         codes(h)
-        quant_in(h, 0, 2 * G)
+        quant_in(h, 0, G)
+        for u in range(2):
+            quant_in(h, G + 2 * u, G + 2 * u + 2)
         quant_v(h, v_grp[h], 2, 0, 1)
         store(h - 1)
         kc, ks, vc, vs = cod[h]

@@ -142,13 +142,12 @@ def tile_latent_kv_state_s7_kernel(tc, c, wk, wv_bytes, wv_scale, keep, write, o
             raw, i = wk_raw[h]
             interleave(engine, wk_grp[h][:], raw[:, :, i * DK : (i + 1) * DK])
 
-        def group_wk_pair(h):
-            pair = stage.tile([P, 2 * DK, 4], BF16, name="wk_pair", bufs=1, align_bytes=64)
+        def group_wk_gpsimd(h):
+            wk_grp[h] = stage.tile([P, DK, 4], BF16, name="wk_pair", bufs=1, align_bytes=64)
+            raw, i = wk_raw[h]
             nc.gpsimd.tensor_scalar(
-                out=pair[:], in0=wk_raw[h][0][:].rearrange("p t n -> p n t"), scalar1=1.0, scalar2=0.0, op0=ALU.mult, op1=ALU.add
+                out=wk_grp[h][:], in0=raw[:, :, i * DK : (i + 1) * DK].rearrange("p t n -> p n t"), scalar1=1.0, scalar2=0.0, op0=ALU.mult, op1=ALU.add
             )
-            wk_grp[h] = pair[:, :DK, :]
-            wk_grp[h + 1] = pair[:, DK:, :]
 
         def quant_wk(h):
             quantize(wk_cod[:, h, :], wk_scl[:, h, :], wk_grp.pop(h)[:, :, :].rearrange("p n t -> p (n t)"))
@@ -300,7 +299,9 @@ def tile_latent_kv_state_s7_kernel(tc, c, wk, wv_bytes, wv_scale, keep, write, o
         ob = {}
 
         def fold(h):
-            if h == 0:
+            if h >= H - 3:
+                ob[h] = psum.tile([P, 512], F32, name="v_bank", bufs=4)
+            elif h == 0:
                 ob[h] = s_bank()
             else:
                 ob[h] = o_bank()
@@ -402,12 +403,11 @@ def tile_latent_kv_state_s7_kernel(tc, c, wk, wv_bytes, wv_scale, keep, write, o
                 quant_grouped(h - 2)
             quant_in(h - 1, 0, G if direct_groups(h - 1) == 1 else 2 * G)
             if h == 1:
-                group_wk_pair(2)
+                group_wk_gpsimd(2)
             group_v(h - 1)
             if 2 <= h < H - 1:
                 widen(h + 1, "ssss")
-                if h >= 3:
-                    group_wk(h + 1, "s")
+                group_wk(h + 1, "s")
                 group_wv(h + 1, "s")
             if h >= 4:
                 store(h - 3)
@@ -415,8 +415,6 @@ def tile_latent_kv_state_s7_kernel(tc, c, wk, wv_bytes, wv_scale, keep, write, o
                 mm_key(h, g)
             for n in range(3):
                 mm_scalar(h, n)
-            if last:
-                fold(h - 2)
             for g in range(G):
                 key(h, g)
                 if g < pieces:
@@ -425,8 +423,6 @@ def tile_latent_kv_state_s7_kernel(tc, c, wk, wv_bytes, wv_scale, keep, write, o
                 val_scalar(h, n)
                 if n + 3 < 2 * G - pieces:
                     mm_scalar(h, n + 3)
-                if n == 2 and last:
-                    store(h - 2)
                 if last and n == 2:
                     group_v_scalar(h, 0)
             if last:
@@ -438,6 +434,9 @@ def tile_latent_kv_state_s7_kernel(tc, c, wk, wv_bytes, wv_scale, keep, write, o
                 val_direct(h, d)
 
         h = H - 1
+        halves = [psum.tile([P, 512], F32, name="v_bank", bufs=4), psum.tile([P, 512], F32, name="v_bank", bufs=4)]
+        fold(h - 2)
+        store(h - 2)
         quant_grouped(h - 1)
         fold(h - 1)
         codes(h)
@@ -450,7 +449,6 @@ def tile_latent_kv_state_s7_kernel(tc, c, wk, wv_bytes, wv_scale, keep, write, o
         for f in range(2):
             cols = slice(3 * DV + f * P, 3 * DV + (f + 1) * P)
             quantize(vc[:, cols], vs[:, cols], v_grp[h][:, 1, f * P : (f + 1) * P, :].rearrange("p n t -> p (n t)"))
-        halves = [s_bank(), s_bank()]
         for g in range(G):
             for f in range(2):
                 cols = slice(g * DV + f * P, g * DV + (f + 1) * P)

@@ -44,6 +44,7 @@ def tile_latent_kv_state_s7_kernel(tc, c, wk, wv_bytes, wv_scale, keep, write, o
         psum = ctx.enter_context(tc.psum_pool(name="psum", bufs=1))
 
         ident = const.tile([P, P], F32, name="ident")
+        ident_b = const.tile([P, P], BF16, name="ident_b")
         wvs = const.tile([P, 4], F32, name="wvs")
         warm = const.tile([P, 1], F32, name="warm")
         kp_raw = const.tile([P, G, 32], BF16, name="kp_raw")
@@ -105,6 +106,7 @@ def tile_latent_kv_state_s7_kernel(tc, c, wk, wv_bytes, wv_scale, keep, write, o
         nc.vector.memset(warm[:], 0.0)
         nc.scalar.activation(out=warm[:], in_=warm[:], func=COPY)
         make_identity(nc, ident[:])
+        nc.gpsimd.tensor_copy(out=ident_b[:], in_=ident[:])
 
         def factors():
             nc.vector.tensor_copy(out=kp[:], in_=kp_raw[:].rearrange("p g (t h) -> p g h t", t=4))
@@ -202,7 +204,7 @@ def tile_latent_kv_state_s7_kernel(tc, c, wk, wv_bytes, wv_scale, keep, write, o
                 stop=True,
             )
 
-        kb, db, sb = {}, {}, {}
+        kb, db, sb, shifted = {}, {}, {}, {}
 
         def mm_key(r, u):
             h, g = unit(r, u)
@@ -250,6 +252,23 @@ def tile_latent_kv_state_s7_kernel(tc, c, wk, wv_bytes, wv_scale, keep, write, o
                 op=ALU.mult,
             )
 
+        def mm_shift(r):
+            h, g = unit(r, 1)
+            sb[r, "x"] = s_bank()
+            for t in range(4):
+                mm(sb[r, "x"][:, t * P : (t + 1) * P], g, t, wv_cod[:, h, P:], wv_scl[:, h, P:])
+
+        def val_shift(r):
+            h, g = unit(r, 1)
+            rows = stage.tile([P, 4, P], BF16, name="shift_rows", bufs=1, align_bytes=64)
+            bank = sb.pop((r, "x"))
+            for t in range(4):
+                nc.scalar.activation(out=rows[:, t, :], in_=bank[:, t * P : (t + 1) * P], func=COPY, scale=wr[:, g, h, t : t + 1])
+            shifted[r] = rows
+
+        def group_shift(r):
+            interleave("s", kv_in[r][:, G + 3, :, :], shifted.pop(r)[:])
+
         def val_scalar(r, n):
             if n == 0:
                 v_rows[r] = stage.tile([P, G - direct_groups(r), 4, DV], BF16, name="v_rows", align_bytes=64)
@@ -296,10 +315,23 @@ def tile_latent_kv_state_s7_kernel(tc, c, wk, wv_bytes, wv_scale, keep, write, o
             if direct_groups(h) == 1:
                 quant_v(h, v_grp[h], 1, 2, 3)
 
-        ob = {}
+        ob, woven = {}, {}
 
-        def fold(h):
-            if h >= H - 3:
+        def weave_wk(h, bank):
+            raw, i = wk_raw[h]
+            woven[h] = bank[:, DV:].bitcast(BF16).rearrange("p (n j) -> p n j", j=4)
+            dst = woven[h].rearrange("p n j -> p j n")
+            for j in (0, 2):
+                nc.tensor.matmul(out=dst[:, j : j + 2, :], lhsT=ident_b[:], rhs=raw[:, j : j + 2, i * DK : (i + 1) * DK], start=True, stop=True)
+
+        def weave_out(h):
+            wk_grp[h] = stage.tile([P, DK, 4], BF16, name="wk_grp", bufs=3, align_bytes=64)
+            nc.scalar.copy(out=wk_grp[h][:], in_=woven.pop(h))
+
+        def fold(h, bank=None):
+            if bank is not None:
+                ob[h] = bank
+            elif h >= H - 3:
                 ob[h] = psum.tile([P, 512], F32, name="v_bank", bufs=4)
             elif h == 0:
                 ob[h] = s_bank()
@@ -391,8 +423,12 @@ def tile_latent_kv_state_s7_kernel(tc, c, wk, wv_bytes, wv_scale, keep, write, o
         for h in range(1, H):
             last = h == H - 1
             pieces = 2 * direct_groups(h)
+            if h >= 2:
+                bank = o_bank()
             if h >= 4:
-                fold(h - 3)
+                fold(h - 3, bank)
+            if 2 <= h < H - 1:
+                weave_wk(h + 1, bank)
             if h >= 2:
                 quant_wk(h)
                 quant_wv(h)
@@ -407,22 +443,32 @@ def tile_latent_kv_state_s7_kernel(tc, c, wk, wv_bytes, wv_scale, keep, write, o
             group_v(h - 1)
             if 2 <= h < H - 1:
                 widen(h + 1, "ssss")
-                group_wk(h + 1, "s")
+                weave_out(h + 1)
                 group_wv(h + 1, "s")
             if h >= 4:
                 store(h - 3)
             for g in range(G):
                 mm_key(h, g)
-            for n in range(3):
-                mm_scalar(h, n)
+            if h == 1:
+                mm_shift(h)
+                mm_scalar(h, 0)
+                mm_scalar(h, 1)
+            else:
+                for n in range(3):
+                    mm_scalar(h, n)
             for g in range(G):
                 key(h, g)
-                if g < pieces:
+                if g < pieces and (h, g) != (1, 3):
                     mm_direct(h, g)
+            if h == 1:
+                val_shift(h)
+                mm_scalar(h, 2)
             for n in range(2 * G - pieces):
                 val_scalar(h, n)
                 if n + 3 < 2 * G - pieces:
                     mm_scalar(h, n + 3)
+                if (h, n) == (1, 0):
+                    group_shift(h)
                 if last and n == 2:
                     group_v_scalar(h, 0)
             if last:
@@ -430,7 +476,7 @@ def tile_latent_kv_state_s7_kernel(tc, c, wk, wv_bytes, wv_scale, keep, write, o
             if h == 3:
                 fold(0)
                 store(0)
-            for d in range(pieces):
+            for d in range(3 if h == 1 else pieces):
                 val_direct(h, d)
 
         h = H - 1

@@ -17,10 +17,13 @@ P = 128
 G = 4
 FLOPS = 2 * T * L * H * (DK + DV) + 2 * T * H * DK * DV
 
-W_LOADS = ((0, 2), (2, 4), (4, 8))
+WEIGHT_LOADS = ((0, 2), (2, 4), (4, H))
+VECTOR_BANKS, SCALAR_BANKS = 4, 3
+CODE_BUFS = 5
+SHIFT_ROUND = 1
 
 
-def direct_groups(r):
+def direct_units(r):
     return 1 if r % 2 == 0 and r > 0 else 2
 
 
@@ -44,155 +47,178 @@ def tile_latent_kv_state_s7_kernel(tc, c, wk, wv_bytes, wv_scale, keep, write, o
         psum = ctx.enter_context(tc.psum_pool(name="psum", bufs=1))
 
         ident = const.tile([P, P], F32, name="ident")
-        ident_b = const.tile([P, P], BF16, name="ident_b")
-        wvs = const.tile([P, 4], F32, name="wvs")
+        ident_bf = const.tile([P, P], BF16, name="ident_bf")
+        row_scale = const.tile([P, 4], F32, name="row_scale")
         warm = const.tile([P, 1], F32, name="warm")
-        kp_raw = const.tile([P, G, 32], BF16, name="kp_raw")
-        wr_raw = const.tile([P, G, 32], BF16, name="wr_raw")
-        kp = const.tile([P, G, H, 4], F32, name="kp")
-        wr = const.tile([P, G, H, 4], F32, name="wr")
-        c_cod = const.tile([P, G, 512], U32, name="c_cod", align_bytes=64)
-        c_scl = const.tile([P, G, 512], U8, name="c_scl", align_bytes=64)
+        keep_raw = const.tile([P, G, 4 * H], BF16, name="keep_raw")
+        write_raw = const.tile([P, G, 4 * H], BF16, name="write_raw")
+        keep_f = const.tile([P, G, H, 4], F32, name="keep_f")
+        write_f = const.tile([P, G, H, 4], F32, name="write_f")
+        c_cod = const.tile([P, G, 4 * P], U32, name="c_cod", align_bytes=64)
+        c_scl = const.tile([P, G, 4 * P], U8, name="c_scl", align_bytes=64)
         wk_cod = const.tile([P, H, DK], U32, name="wk_cod", align_bytes=64)
         wk_scl = const.tile([P, H, DK], U8, name="wk_scl", align_bytes=64)
         wv_cod = const.tile([P, H, DV], U32, name="wv_cod", align_bytes=64)
         wv_scl = const.tile([P, H, DV], U8, name="wv_scl", align_bytes=64)
-        c_sb = {}
+
+        c_rows = {}
         for g in range(G):
             for b in range(2):
-                c_sb[g, b] = const.tile([P, 2, L], BF16, name="c_sb%d%d" % (g, b), align_bytes=64)
-        wv_raw = {}
-        wk_raw = {}
-        for a, b in W_LOADS:
-            tv = const.tile([P, 4, (b - a) * DV], U8, name="wv_raw%d" % a, align_bytes=64)
-            tk = const.tile([P, 4, (b - a) * DK], BF16, name="wk_raw%d" % a, align_bytes=64)
-            for h in range(a, b):
-                wv_raw[h] = (tv, h - a)
-                wk_raw[h] = (tk, h - a)
+                c_rows[g, b] = const.tile([P, 2, L], BF16, name="c_rows%d%d" % (g, b), align_bytes=64)
+        wk_load, wv_load = {}, {}
+        for first, end in WEIGHT_LOADS:
+            wv_load[first] = const.tile([P, 4, (end - first) * DV], U8, name="wv_load%d" % first, align_bytes=64)
+            wk_load[first] = const.tile([P, 4, (end - first) * DK], BF16, name="wk_load%d" % first, align_bytes=64)
+
+        def load_start(h):
+            return max(first for first, end in WEIGHT_LOADS if first <= h)
+
+        def wk_rows(h):
+            col = (h - load_start(h)) * DK
+            return wk_load[load_start(h)][:, :, col : col + DK]
+
+        def wv_row(h, j):
+            col = (h - load_start(h)) * DV
+            return wv_load[load_start(h)][:, j, col : col + DV]
 
         ctx.enter_context(tc.manual_schedule())
 
-        wv_view = wv_bytes.rearrange("(p j) w -> p j w", j=4)
-        wk_view = wk.rearrange("(p j) w -> p j w", j=4)
+        wv_view = wv_bytes.rearrange("(q j) w -> q j w", j=4)
+        wk_view = wk.rearrange("(q j) w -> q j w", j=4)
         c_view = c.rearrange("(g p b i) l -> g b p i l", p=P, b=2, i=2)
 
         def load_c(g, b):
-            nc.sync.dma_start(out=c_sb[g, b][:], in_=c_view[g, b])
+            nc.sync.dma_start(out=c_rows[g, b][:], in_=c_view[g, b])
 
-        def load_wv(a, b):
-            nc.sync.dma_start(out=wv_raw[a][0][:], in_=wv_view[:, :, a * DV : b * DV])
+        def load_wv(first, end):
+            nc.sync.dma_start(out=wv_load[first][:], in_=wv_view[:, :, first * DV : end * DV])
 
-        def load_wk(a, b):
-            nc.sync.dma_start(out=wk_raw[a][0][:], in_=wk_view[:, :, a * DK : b * DK])
+        def load_wk(first, end):
+            nc.sync.dma_start(out=wk_load[first][:], in_=wk_view[:, :, first * DK : end * DK])
 
-        nc.scalar.dma_start(out=wvs[:], in_=wv_scale.rearrange("(p j) o -> p (j o)", j=4))
-        load_wv(*W_LOADS[0])
+        nc.scalar.dma_start(out=row_scale[:], in_=wv_scale.rearrange("(q j) o -> q (j o)", j=4))
+        load_wv(*WEIGHT_LOADS[0])
         load_c(0, 0)
         load_c(0, 1)
-        load_wk(*W_LOADS[0])
+        load_wk(*WEIGHT_LOADS[0])
         load_c(1, 0)
         load_c(1, 1)
         load_c(2, 0)
-        nc.sync.dma_start(out=kp_raw[:], in_=keep.rearrange("(g p t) h -> p g (t h)", p=P, t=4))
-        nc.sync.dma_start(out=wr_raw[:], in_=write.rearrange("(g p t) h -> p g (t h)", p=P, t=4))
-        load_wv(*W_LOADS[1])
+        nc.sync.dma_start(out=keep_raw[:], in_=keep.rearrange("(g p t) h -> p g (t h)", p=P, t=4))
+        nc.sync.dma_start(out=write_raw[:], in_=write.rearrange("(g p t) h -> p g (t h)", p=P, t=4))
+        load_wv(*WEIGHT_LOADS[1])
         load_c(2, 1)
-        load_wk(*W_LOADS[1])
+        load_wk(*WEIGHT_LOADS[1])
         load_c(3, 0)
         load_c(3, 1)
-        load_wv(*W_LOADS[2])
-        load_wk(*W_LOADS[2])
+        load_wv(*WEIGHT_LOADS[2])
+        load_wk(*WEIGHT_LOADS[2])
 
         nc.vector.memset(warm[:], 0.0)
         nc.scalar.activation(out=warm[:], in_=warm[:], func=COPY)
         make_identity(nc, ident[:])
-        nc.gpsimd.tensor_copy(out=ident_b[:], in_=ident[:])
+        nc.gpsimd.tensor_copy(out=ident_bf[:], in_=ident[:])
 
-        def factors():
-            nc.vector.tensor_copy(out=kp[:], in_=kp_raw[:].rearrange("p g (t h) -> p g h t", t=4))
-            nc.vector.tensor_copy(out=wr[:], in_=wr_raw[:].rearrange("p g (t h) -> p g h t", t=4))
+        def vector_bank():
+            return psum.tile([P, 512], F32, name="vector_bank", bufs=VECTOR_BANKS)
 
-        def interleave(engine, dst, src):
-            d4 = dst.rearrange("p (c i) t -> p c t i", i=4)
-            s4 = src.rearrange("p t (c i) -> p c t i", i=4)
-            if engine == "s":
-                nc.scalar.copy(out=d4, in_=s4)
-            else:
-                nc.vector.tensor_copy(out=d4, in_=s4)
+        def scalar_bank():
+            return psum.tile([P, 512], F32, name="scalar_bank", bufs=SCALAR_BANKS)
+
+        def state_bank():
+            return psum.tile([P, 512], F32, name="state_bank")
+
+        def warm_up(count):
+            bank = vector_bank()
+            for i in range(count):
+                nc.tensor.matmul(out=bank[:, i * P : (i + 1) * P], lhsT=ident[:], rhs=ident[:], start=True, stop=True)
+
+        def interleave(copy, dst, src):
+            copy(out=dst.rearrange("p (c i) t -> p c t i", i=4), in_=src.rearrange("p t (c i) -> p c t i", i=4))
+
+        def pool_interleave(dst, src):
+            nc.gpsimd.tensor_scalar(out=dst, in0=src, scalar1=1.0, scalar2=0.0, op0=ALU.mult, op1=ALU.add)
 
         def quantize(cod, scl, src):
             nc.vector.quantize_mx(out=cod.bitcast(FP8X4), scales=scl, in_=src)
 
-        wide, wv_grp, wk_grp = {}, {}, {}
+        wv_wide, wv_words, wk_words, wk_woven, wv_woven = {}, {}, {}, {}, {}
 
-        def widen(h, engines):
-            wide[h] = stage.tile([P, 4, DV], BF16, name="wv_wide", align_bytes=64)
-            raw, i = wv_raw[h]
-            for j in range(4):
-                src = raw[:, j, i * DV : (i + 1) * DV].bitcast(FP8)
-                if engines[j] == "s":
-                    nc.scalar.activation(out=wide[h][:, j, :], in_=src, func=COPY, scale=wvs[:, j : j + 1])
-                else:
-                    nc.vector.tensor_scalar(out=wide[h][:, j, :], in0=src, scalar1=wvs[:, j : j + 1], scalar2=None, op0=ALU.mult)
+        def widen(h, j, on_vector=False):
+            if h not in wv_wide:
+                wv_wide[h] = stage.tile([P, 4, DV], BF16, name="wv_wide", align_bytes=64)
+            src = wv_row(h, j).bitcast(FP8)
+            if on_vector:
+                nc.vector.tensor_scalar(out=wv_wide[h][:, j, :], in0=src, scalar1=row_scale[:, j : j + 1], scalar2=None, op0=ALU.mult)
+            else:
+                nc.scalar.activation(out=wv_wide[h][:, j, :], in_=src, func=COPY, scale=row_scale[:, j : j + 1])
 
-        def group_wv(h, engine):
-            wv_grp[h] = stage.tile([P, DV, 4], BF16, name="wv_grp", bufs=3, align_bytes=64)
-            interleave(engine, wv_grp[h][:], wide.pop(h)[:])
+        def interleave_wv(h, copy):
+            wv_words[h] = stage.tile([P, DV, 4], BF16, name="wv_words", bufs=3, align_bytes=64)
+            interleave(copy, wv_words[h][:], wv_wide.pop(h)[:])
 
-        def group_wk(h, engine):
-            wk_grp[h] = stage.tile([P, DK, 4], BF16, name="wk_grp", bufs=3, align_bytes=64)
-            raw, i = wk_raw[h]
-            interleave(engine, wk_grp[h][:], raw[:, :, i * DK : (i + 1) * DK])
+        def interleave_wk(h):
+            wk_words[h] = stage.tile([P, DK, 4], BF16, name="wk_words", bufs=3, align_bytes=64)
+            interleave(nc.vector.tensor_copy, wk_words[h][:], wk_rows(h))
 
-        def group_wk_gpsimd(h):
-            wk_grp[h] = stage.tile([P, DK, 4], BF16, name="wk_pair", bufs=1, align_bytes=64)
-            raw, i = wk_raw[h]
-            nc.gpsimd.tensor_scalar(
-                out=wk_grp[h][:], in0=raw[:, :, i * DK : (i + 1) * DK].rearrange("p t n -> p n t"), scalar1=1.0, scalar2=0.0, op0=ALU.mult, op1=ALU.add
-            )
+        def pool_interleave_wk(h):
+            wk_words[h] = stage.tile([P, DK, 4], BF16, name="first_release", bufs=1, align_bytes=64)
+            pool_interleave(wk_words[h][:], wk_rows(h).rearrange("p j n -> p n j"))
 
-        def quant_wk(h):
-            quantize(wk_cod[:, h, :], wk_scl[:, h, :], wk_grp.pop(h)[:, :, :].rearrange("p n t -> p (n t)"))
+        def weave_wk(h, bank):
+            wk_woven[h] = bank[:, DV:].bitcast(BF16).rearrange("p (n j) -> p n j", j=4)
+            dst = wk_woven[h].rearrange("p n j -> p j n")
+            for j in (0, 2):
+                nc.tensor.matmul(out=dst[:, j : j + 2, :], lhsT=ident_bf[:], rhs=wk_rows(h)[:, j : j + 2, :], start=True, stop=True)
 
-        def quant_wv(h):
-            quantize(wv_cod[:, h, :], wv_scl[:, h, :], wv_grp.pop(h)[:].rearrange("p n t -> p (n t)"))
+        def weave_wv(h):
+            wv_woven[h] = psum.tile([P, DV, 4], BF16, name="state_bank")
+            dst = wv_woven[h][:].rearrange("p n j -> p j n")
+            src = wv_wide.pop(h)
+            for j in (0, 2):
+                nc.tensor.matmul(out=dst[:, j : j + 2, :], lhsT=ident_bf[:], rhs=src[:, j : j + 2, :], start=True, stop=True)
 
-        def s_bank():
-            return psum.tile([P, 512], F32, name="s_bank", bufs=3)
+        def woven_wv_out(h):
+            wv_words[h] = stage.tile([P, DV, 4], BF16, name="wv_words", bufs=3, align_bytes=64)
+            nc.scalar.copy(out=wv_words[h][:], in_=wv_woven.pop(h)[:])
 
-        def o_bank():
-            return psum.tile([P, 512], F32, name="o_bank", bufs=1)
+        def woven_wk_out(h):
+            wk_words[h] = stage.tile([P, DK, 4], BF16, name="wk_words", bufs=3, align_bytes=64)
+            nc.scalar.copy(out=wk_words[h][:], in_=wk_woven.pop(h))
 
-        def v_bank():
-            return psum.tile([P, 4, P], F32, name="v_bank", bufs=4)
+        def quantize_wk(h):
+            quantize(wk_cod[:, h, :], wk_scl[:, h, :], wk_words.pop(h)[:].rearrange("p n j -> p (n j)"))
 
-        xt, c_grp = {}, {}
+        def quantize_wv(h):
+            quantize(wv_cod[:, h, :], wv_scl[:, h, :], wv_words.pop(h)[:].rearrange("p n j -> p (n j)"))
+
+        c_turned, c_words = {}, {}
 
         def transpose_c(g, b):
-            words = c_sb[g, b][:].bitcast(F32)
-            xt[g, b] = o_bank() if (g, b) in ((0, 0), (2, 0)) else s_bank()
+            words = c_rows[g, b][:].bitcast(F32)
+            c_turned[g, b] = state_bank() if b == 0 and g % 2 == 0 else scalar_bank()
             for i in range(2):
                 for u in range(2):
                     col = (2 * i + u) * P
-                    nc.tensor.transpose(xt[g, b][:, col : col + P], words[:, i, u::2], ident[:])
+                    nc.tensor.transpose(c_turned[g, b][:, col : col + P], words[:, i, u::2], ident[:])
 
-        def c_out(g, b, engine):
+        def turned_c_out(g, b):
             if (g, b) == (G - 1, 1):
-                c_grp[g, b] = stage.tile([P, 2, P, 4], BF16, name="wk_pair", bufs=1, align_bytes=64)
+                c_words[g, b] = stage.tile([P, 2, P, 4], BF16, name="first_release", bufs=1, align_bytes=64)
             else:
-                c_grp[g, b] = stage.tile([P, 2, P, 4], BF16, name="c_grp", bufs=4, align_bytes=64)
-            dst = c_grp[g, b][:].bitcast(F32)
-            src = xt.pop((g, b))[:].rearrange("q (i u r) -> q i r u", i=2, u=2)
-            if engine == "s":
-                nc.scalar.copy(out=dst, in_=src)
-            else:
-                nc.vector.tensor_copy(out=dst, in_=src)
+                c_words[g, b] = stage.tile([P, 2, P, 4], BF16, name="c_words", bufs=4, align_bytes=64)
+            src = c_turned.pop((g, b))[:].rearrange("q (i u p) -> q i p u", i=2, u=2)
+            nc.scalar.copy(out=c_words[g, b][:].bitcast(F32), in_=src)
 
-        def quant_c(g, b):
+        def quantize_c(g, b):
             cols = slice(2 * b * P, 2 * (b + 1) * P)
-            quantize(c_cod[:, g, cols], c_scl[:, g, cols], c_grp.pop((g, b))[:].rearrange("q i r e -> q (i r e)"))
+            quantize(c_cod[:, g, cols], c_scl[:, g, cols], c_words.pop((g, b))[:].rearrange("q i p e -> q (i p e)"))
 
-        def mm(dst, g, t, cod, scl):
+        def widen_factors():
+            nc.vector.tensor_copy(out=keep_f[:], in_=keep_raw[:].rearrange("p g (t h) -> p g h t", t=4))
+            nc.vector.tensor_copy(out=write_f[:], in_=write_raw[:].rearrange("p g (t h) -> p g h t", t=4))
+
+        def project(dst, g, t, cod, scl):
             cols = slice(t * P, (t + 1) * P)
             nc.tensor.matmul_mx(
                 out=dst,
@@ -204,312 +230,276 @@ def tile_latent_kv_state_s7_kernel(tc, c, wk, wv_bytes, wv_scale, keep, write, o
                 stop=True,
             )
 
-        kb, db, sb, shifted = {}, {}, {}, {}
+        key_bank, piece_bank, rows_bank = {}, {}, {}
 
-        def mm_key(r, u):
+        def project_keys(r, u):
             h, g = unit(r, u)
-            kb[r, u] = v_bank()
+            key_bank[r, u] = vector_bank()
             for t in range(4):
-                mm(kb[r, u][:, t, :], g, t, wk_cod[:, h, :], wk_scl[:, h, :])
+                project(key_bank[r, u][:, t * DK : (t + 1) * DK], g, t, wk_cod[:, h, :], wk_scl[:, h, :])
 
-        def mm_direct(r, d):
-            u, f = divmod(d, 2)
-            h, g = unit(r, u)
-            db[r, d] = v_bank()
-            cols = slice(f * P, (f + 1) * P)
+        def project_piece(r, d, new_bank=vector_bank):
+            h, g = unit(r, d // 2)
+            piece_bank[r, d] = new_bank()
+            cols = slice((d % 2) * P, (d % 2 + 1) * P)
             for t in range(4):
-                mm(db[r, d][:, t, :], g, t, wv_cod[:, h, cols], wv_scl[:, h, cols])
+                project(piece_bank[r, d][:, t * P : (t + 1) * P], g, t, wv_cod[:, h, cols], wv_scl[:, h, cols])
 
-        def mm_scalar(r, n):
-            u, f = divmod(2 * direct_groups(r) + n, 2)
-            h, g = unit(r, u)
-            sb[r, n] = s_bank()
+        def project_rows(r, n):
+            h, g = unit(r, direct_units(r) + n // 2)
+            rows_bank[r, n] = scalar_bank()
             for i in range(2):
-                mm(sb[r, n][:, i * DV : (i + 1) * DV], g, 2 * f + i, wv_cod[:, h, :], wv_scl[:, h, :])
+                project(rows_bank[r, n][:, i * DV : (i + 1) * DV], g, 2 * (n % 2) + i, wv_cod[:, h, :], wv_scl[:, h, :])
 
-        kv_in, v_rows, v_grp, cod, whole = {}, {}, {}, {}, {}
+        kv_words, v_rows, v_words, shifted_rows = {}, {}, {}, {}
 
-        def key(r, u):
+        def keys_out(r, u):
             h, g = unit(r, u)
             if u == 0:
-                kv_in[r] = stage.tile([P, G + 2 * direct_groups(r), P, 4], BF16, name="kv_in", align_bytes=64)
+                kv_words[r] = stage.tile([P, G + 2 * direct_units(r), P, 4], BF16, name="kv_words", align_bytes=64)
             nc.vector.scalar_tensor_tensor(
-                out=kv_in[r][:, u, :, :],
-                in0=kb.pop((r, u))[:].rearrange("p t n -> p n t"),
+                out=kv_words[r][:, u, :, :],
+                in0=key_bank.pop((r, u))[:].rearrange("p (t n) -> p n t", t=4),
                 scalar=0.0,
-                in1=kp[:, g, h, :].unsqueeze(1).to_broadcast([P, DK, 4]),
+                in1=keep_f[:, g, h, :].unsqueeze(1).to_broadcast([P, DK, 4]),
                 op0=ALU.max,
                 op1=ALU.mult,
             )
 
-        def val_direct(r, d):
-            u, f = divmod(d, 2)
-            h, g = unit(r, u)
+        def piece_out(r, d):
+            h, g = unit(r, d // 2)
             nc.vector.tensor_tensor(
-                out=kv_in[r][:, G + d, :, :],
-                in0=db.pop((r, d))[:].rearrange("p t n -> p n t"),
-                in1=wr[:, g, h, :].unsqueeze(1).to_broadcast([P, P, 4]),
+                out=kv_words[r][:, G + d, :, :],
+                in0=piece_bank.pop((r, d))[:].rearrange("p (t n) -> p n t", t=4),
+                in1=write_f[:, g, h, :].unsqueeze(1).to_broadcast([P, P, 4]),
                 op=ALU.mult,
             )
 
-        def mm_shift(r):
-            h, g = unit(r, 1)
-            sb[r, "x"] = s_bank()
+        def shifted_piece_out(r, d):
+            h, g = unit(r, d // 2)
+            shifted_rows[r] = stage.tile([P, 4, P], BF16, name="shifted_rows", bufs=1, align_bytes=64)
+            bank = piece_bank.pop((r, d))
             for t in range(4):
-                mm(sb[r, "x"][:, t * P : (t + 1) * P], g, t, wv_cod[:, h, P:], wv_scl[:, h, P:])
+                nc.scalar.activation(out=shifted_rows[r][:, t, :], in_=bank[:, t * P : (t + 1) * P], func=COPY, scale=write_f[:, g, h, t : t + 1])
 
-        def val_shift(r):
-            h, g = unit(r, 1)
-            rows = stage.tile([P, 4, P], BF16, name="shift_rows", bufs=1, align_bytes=64)
-            bank = sb.pop((r, "x"))
-            for t in range(4):
-                nc.scalar.activation(out=rows[:, t, :], in_=bank[:, t * P : (t + 1) * P], func=COPY, scale=wr[:, g, h, t : t + 1])
-            shifted[r] = rows
-
-        def group_shift(r):
-            interleave("s", kv_in[r][:, G + 3, :, :], shifted.pop(r)[:])
-
-        def val_scalar(r, n):
+        def rows_out(r, n):
             if n == 0:
-                v_rows[r] = stage.tile([P, G - direct_groups(r), 4, DV], BF16, name="v_rows", align_bytes=64)
-            u, f = divmod(n, 2)
-            h, g = unit(r, direct_groups(r) + u)
-            bank = sb.pop((r, n))
+                v_rows[r] = stage.tile([P, G - direct_units(r), 4, DV], BF16, name="v_rows", align_bytes=64)
+            h, g = unit(r, direct_units(r) + n // 2)
+            bank = rows_bank.pop((r, n))
             for i in range(2):
-                t = 2 * f + i
-                nc.scalar.activation(
-                    out=v_rows[r][:, u, t, :],
-                    in_=bank[:, i * DV : (i + 1) * DV],
-                    func=COPY,
-                    scale=wr[:, g, h, t : t + 1],
-                )
+                t = 2 * (n % 2) + i
+                nc.scalar.activation(out=v_rows[r][:, n // 2, t, :], in_=bank[:, i * DV : (i + 1) * DV], func=COPY, scale=write_f[:, g, h, t : t + 1])
 
-        def group_v(h):
-            v_grp[h] = stage.tile([P, G - direct_groups(h), DV, 4], BF16, name="v_grp", bufs=1, align_bytes=64)
-            nc.gpsimd.tensor_scalar(
-                out=v_grp[h][:], in0=v_rows.pop(h)[:].rearrange("p u t n -> p u n t"), scalar1=1.0, scalar2=0.0, op0=ALU.mult, op1=ALU.add
+        def pool_interleave_v(r):
+            v_words[r] = stage.tile([P, G - direct_units(r), DV, 4], BF16, name="v_words", bufs=1, align_bytes=64)
+            pool_interleave(v_words[r][:], v_rows.pop(r)[:].rearrange("p u t n -> p u n t"))
+
+        def scalar_interleave_v(r, i):
+            if i == 0:
+                v_words[r] = stage.tile([P, G - direct_units(r), DV, 4], BF16, name="v_words_last", bufs=1, align_bytes=64)
+            interleave(nc.scalar.copy, v_words[r][:, i, :, :], v_rows[r][:, i, :, :])
+
+        kv_cod, kv_scl = {}, {}
+
+        def new_codes(r):
+            kv_cod[r] = stage.tile([P, G * (DK + DV)], U32, name="kv_cod", bufs=CODE_BUFS, align_bytes=64)
+            kv_scl[r] = stage.tile([P, G * (DK + DV)], U8, name="kv_scl", bufs=CODE_BUFS, align_bytes=64)
+
+        def quantize_kv(r, col, src):
+            flat = src.rearrange("p m n t -> p (m n t)")
+            cols = slice(col, col + flat.shape[1] // 4)
+            quantize(kv_cod[r][:, cols], kv_scl[r][:, cols], flat)
+
+        def quantize_pieces(r, first, end):
+            quantize_kv(r, first * P, kv_words[r][:, first:end, :, :])
+
+        def quantize_units(r, first, end):
+            quantize_kv(r, G * DK + (direct_units(r) + first) * DV, v_words[r][:, first:end, :, :])
+
+        def quantize_pooled(r):
+            quantize_units(r, 0, 2)
+            if direct_units(r) == 1:
+                quantize_units(r, 2, 3)
+
+        def state_pass(dst, h, g, first, end):
+            r, u = place(h, g)
+            k_cols = slice(u * DK, (u + 1) * DK)
+            v_cols = slice(G * DK + u * DV + first, G * DK + u * DV + end)
+            nc.tensor.matmul_mx(
+                out=dst,
+                lhsT=kv_cod[r][:, k_cols].bitcast(FP8X4),
+                lhsT_scale=kv_scl[r][:, k_cols],
+                rhs=kv_cod[r][:, v_cols].bitcast(FP8X4),
+                rhs_scale=kv_scl[r][:, v_cols],
+                start=(g == 0),
+                stop=(g == G - 1),
             )
 
-        def group_v_scalar(h, u):
-            if u == 0:
-                v_grp[h] = stage.tile([P, G - direct_groups(h), DV, 4], BF16, name="v_last", bufs=1, align_bytes=64)
-            interleave("s", v_grp[h][:, u, :, :], v_rows[h][:, u, :, :])
+        state = {}
 
-        def codes(r):
-            kvc = stage.tile([P, G * (DK + DV)], U32, name="kv_cod", bufs=5, align_bytes=64)
-            kvs = stage.tile([P, G * (DK + DV)], U8, name="kv_scl", bufs=5, align_bytes=64)
-            cod[r] = (kvc[:, : G * DK], kvs[:, : G * DK], kvc[:, G * DK :], kvs[:, G * DK :])
-            whole[r] = (kvc, kvs)
-
-        def quant_in(r, a, b):
-            kvc, kvs = whole[r]
-            quantize(kvc[:, a * P : b * P], kvs[:, a * P : b * P], kv_in[r][:, a:b, :, :].rearrange("p m n t -> p (m n t)"))
-
-        def quant_v(h, src, first, a, b):
-            kc, ks, vc, vs = cod[h]
-            cols = slice((first + a) * DV, (first + b) * DV)
-            quantize(vc[:, cols], vs[:, cols], src[:, a:b, :, :].rearrange("p u n t -> p (u n t)"))
-
-        def quant_grouped(h):
-            quant_v(h, v_grp[h], direct_groups(h), 0, 2)
-            if direct_groups(h) == 1:
-                quant_v(h, v_grp[h], 1, 2, 3)
-
-        ob, woven = {}, {}
-
-        def weave_wk(h, bank):
-            raw, i = wk_raw[h]
-            woven[h] = bank[:, DV:].bitcast(BF16).rearrange("p (n j) -> p n j", j=4)
-            dst = woven[h].rearrange("p n j -> p j n")
-            for j in (0, 2):
-                nc.tensor.matmul(out=dst[:, j : j + 2, :], lhsT=ident_b[:], rhs=raw[:, j : j + 2, i * DK : (i + 1) * DK], start=True, stop=True)
-
-        def weave_out(h):
-            wk_grp[h] = stage.tile([P, DK, 4], BF16, name="wk_grp", bufs=3, align_bytes=64)
-            nc.scalar.copy(out=wk_grp[h][:], in_=woven.pop(h))
-
-        def fold(h, bank=None):
-            if bank is not None:
-                ob[h] = bank
-            elif h >= H - 3:
-                ob[h] = psum.tile([P, 512], F32, name="v_bank", bufs=4)
-            elif h == 0:
-                ob[h] = s_bank()
-            else:
-                ob[h] = o_bank()
+        def sum_state(h, bank):
+            state[h] = bank
             for g in range(G):
-                r, u = place(h, g)
-                kc, ks, vc, vs = cod[r]
-                nc.tensor.matmul_mx(
-                    out=ob[h][:, :DV],
-                    lhsT=kc[:, u * DK : (u + 1) * DK].bitcast(FP8X4),
-                    lhsT_scale=ks[:, u * DK : (u + 1) * DK],
-                    rhs=vc[:, u * DV : (u + 1) * DV].bitcast(FP8X4),
-                    rhs_scale=vs[:, u * DV : (u + 1) * DV],
-                    start=(g == 0),
-                    stop=(g == G - 1),
-                )
+                state_pass(bank[:, :DV], h, g, 0, DV)
 
-        def store(h):
-            o = stage.tile([P, DV], F32, name="o_sb")
-            nc.scalar.copy(out=o[:], in_=ob.pop(h)[:, :DV])
-            nc.sync.dma_start(out=out[h], in_=o[:])
-
-        def warm_up(n):
-            bank = v_bank()
-            for i in range(n):
-                nc.tensor.matmul(out=bank[:, i % 4, :], lhsT=ident[:], rhs=ident[:], start=True, stop=True)
+        def store_state(h):
+            result = stage.tile([P, DV], F32, name="result")
+            nc.scalar.copy(out=result[:], in_=state.pop(h)[:, :DV])
+            nc.sync.dma_start(out=out[h], in_=result[:])
 
         warm_up(4)
-        widen(0, "svsv")
-        widen(1, "svsv")
+        for h in range(2):
+            for j in range(4):
+                widen(h, j, on_vector=(j % 2 == 1))
         for g in range(2):
             for b in range(2):
                 transpose_c(g, b)
-                c_out(g, b, "s")
+                turned_c_out(g, b)
             if g == 0:
                 warm_up(2)
-        group_wv(0, "v")
-        group_wv(1, "v")
-        quant_wv(0)
-        group_wk(0, "v")
-        quant_c(0, 0)
-        quant_wk(0)
-        quant_c(0, 1)
-        group_wk(1, "v")
-        quant_wv(1)
-        factors()
-        quant_wk(1)
-        quant_c(1, 0)
-        quant_c(1, 1)
-        mm_key(0, 0)
-        mm_direct(0, 0)
-        mm_direct(0, 1)
+        interleave_wv(0, nc.vector.tensor_copy)
+        interleave_wv(1, nc.vector.tensor_copy)
+        quantize_wv(0)
+        interleave_wk(0)
+        quantize_c(0, 0)
+        quantize_wk(0)
+        quantize_c(0, 1)
+        interleave_wk(1)
+        quantize_wv(1)
+        widen_factors()
+        quantize_wk(1)
+        quantize_c(1, 0)
+        quantize_c(1, 1)
+        project_keys(0, 0)
+        project_piece(0, 0)
+        project_piece(0, 1)
         transpose_c(2, 0)
-        mm_key(0, 1)
-        c_out(2, 0, "s")
-        widen(2, "ssss")
+        project_keys(0, 1)
+        turned_c_out(2, 0)
+        for j in range(4):
+            widen(2, j)
         transpose_c(2, 1)
-        key(0, 0)
-        mm_direct(0, 2)
-        c_out(2, 1, "s")
-        val_direct(0, 0)
-        mm_direct(0, 3)
-        transpose_c(3, 0)
-        transpose_c(3, 1)
-        val_direct(0, 1)
-        mm_key(0, 2)
-        c_out(3, 0, "s")
-        mm_scalar(0, 0)
-        c_out(3, 1, "s")
-        key(0, 1)
-        mm_key(0, 3)
-        mm_scalar(0, 1)
-        mm_scalar(0, 2)
-        val_scalar(0, 0)
-        mm_scalar(0, 3)
+        keys_out(0, 0)
+        project_piece(0, 2)
+        turned_c_out(2, 1)
+        piece_out(0, 0)
+        project_piece(0, 3)
+        for b in range(2):
+            transpose_c(3, b)
+        piece_out(0, 1)
+        project_keys(0, 2)
+        turned_c_out(3, 0)
+        project_rows(0, 0)
+        turned_c_out(3, 1)
+        keys_out(0, 1)
+        project_keys(0, 3)
+        project_rows(0, 1)
+        project_rows(0, 2)
+        rows_out(0, 0)
+        project_rows(0, 3)
         for n in range(1, 4):
-            val_scalar(0, n)
-        quant_c(2, 0)
-        val_direct(0, 2)
-        quant_c(2, 1)
-        val_direct(0, 3)
-        quant_c(3, 0)
-        key(0, 2)
-        key(0, 3)
-        quant_c(3, 1)
-        group_wv(2, "s")
+            rows_out(0, n)
+        for b in range(2):
+            quantize_c(2, b)
+            piece_out(0, 2 + b)
+        quantize_c(3, 0)
+        for u in (2, 3):
+            keys_out(0, u)
+        quantize_c(3, 1)
+        interleave_wv(2, nc.scalar.copy)
 
-        for h in range(1, H):
-            last = h == H - 1
-            pieces = 2 * direct_groups(h)
-            if h >= 2:
-                bank = o_bank()
-            if h >= 4:
-                fold(h - 3, bank)
-            if 2 <= h < H - 1:
-                weave_wk(h + 1, bank)
-            if h >= 2:
-                quant_wk(h)
-                quant_wv(h)
-            codes(h - 1)
-            if direct_groups(h - 1) == 1:
-                quant_in(h - 1, G, G + 2)
-            if h >= 2:
-                quant_grouped(h - 2)
-            quant_in(h - 1, 0, G if direct_groups(h - 1) == 1 else 2 * G)
-            if h == 1:
-                group_wk_gpsimd(2)
-            group_v(h - 1)
-            if 2 <= h < H - 1:
-                widen(h + 1, "ssss")
-                weave_out(h + 1)
-                group_wv(h + 1, "s")
-            if h >= 4:
-                store(h - 3)
-            for g in range(G):
-                mm_key(h, g)
-            if h == 1:
-                mm_shift(h)
-                mm_scalar(h, 0)
-                mm_scalar(h, 1)
-            else:
-                for n in range(3):
-                    mm_scalar(h, n)
-            for g in range(G):
-                key(h, g)
-                if g < pieces and (h, g) != (1, 3):
-                    mm_direct(h, g)
-            if h == 1:
-                val_shift(h)
-                mm_scalar(h, 2)
-            for n in range(2 * G - pieces):
-                val_scalar(h, n)
-                if n + 3 < 2 * G - pieces:
-                    mm_scalar(h, n + 3)
-                if (h, n) == (1, 0):
-                    group_shift(h)
-                if last and n == 2:
-                    group_v_scalar(h, 0)
-            if last:
-                group_v_scalar(h, 1)
-            if h == 3:
-                fold(0)
-                store(0)
-            for d in range(3 if h == 1 else pieces):
-                val_direct(h, d)
+        last = H - 1
+        for r in range(1, H):
+            pieces = 2 * direct_units(r)
+            on_vector = pieces - 1 if r == SHIFT_ROUND else pieces
+            row_banks = 2 * G - pieces
+            prepares = 2 <= r < last
+            weaves_wv = prepares and row_banks == 6
 
-        h = H - 1
-        halves = [psum.tile([P, 512], F32, name="v_bank", bufs=4), psum.tile([P, 512], F32, name="v_bank", bufs=4)]
-        fold(h - 2)
-        store(h - 2)
-        quant_grouped(h - 1)
-        fold(h - 1)
-        codes(h)
-        quant_in(h, 0, G)
+            if r >= 2:
+                bank = state_bank()
+            if r >= 4:
+                sum_state(r - 3, bank)
+            if prepares:
+                weave_wk(r + 1, bank)
+
+            if r >= 2:
+                quantize_wk(r)
+                quantize_wv(r)
+            new_codes(r - 1)
+            if direct_units(r - 1) == 1:
+                quantize_pieces(r - 1, G, G + 2)
+            if r >= 2:
+                quantize_pooled(r - 2)
+            quantize_pieces(r - 1, 0, G if direct_units(r - 1) == 1 else 2 * G)
+
+            if r == 1:
+                pool_interleave_wk(2)
+            pool_interleave_v(r - 1)
+
+            if prepares:
+                for j in range(4):
+                    widen(r + 1, j)
+                woven_wk_out(r + 1)
+                if not weaves_wv:
+                    interleave_wv(r + 1, nc.scalar.copy)
+            if r >= 4:
+                store_state(r - 3)
+
+            for u in range(G):
+                project_keys(r, u)
+            if r == SHIFT_ROUND:
+                project_piece(r, on_vector, scalar_bank)
+            ahead = SCALAR_BANKS - (pieces - on_vector)
+            for n in range(ahead):
+                project_rows(r, n)
+            if weaves_wv:
+                weave_wv(r + 1)
+            for u in range(G):
+                keys_out(r, u)
+                if u < on_vector:
+                    project_piece(r, u)
+            if r == SHIFT_ROUND:
+                shifted_piece_out(r, on_vector)
+                project_rows(r, ahead)
+            for n in range(row_banks):
+                rows_out(r, n)
+                if n + SCALAR_BANKS < row_banks:
+                    project_rows(r, n + SCALAR_BANKS)
+                if r == SHIFT_ROUND and n == 0:
+                    interleave(nc.scalar.copy, kv_words[r][:, G + on_vector, :, :], shifted_rows.pop(r)[:])
+                if weaves_wv and n == 2:
+                    woven_wv_out(r + 1)
+                if r == last and n == 2:
+                    scalar_interleave_v(r, 0)
+            if r == last:
+                scalar_interleave_v(r, 1)
+            if r == 3:
+                sum_state(0, scalar_bank())
+                store_state(0)
+            for d in range(on_vector):
+                piece_out(r, d)
+
+        halves = [vector_bank(), vector_bank()]
+        sum_state(last - 2, vector_bank())
+        store_state(last - 2)
+        quantize_pooled(last - 1)
+        sum_state(last - 1, vector_bank())
+        new_codes(last)
+        quantize_pieces(last, 0, G)
         for u in range(2):
-            quant_in(h, G + 2 * u, G + 2 * u + 2)
-        quant_v(h, v_grp[h], 2, 0, 1)
-        store(h - 1)
-        kc, ks, vc, vs = cod[h]
+            quantize_pieces(last, G + 2 * u, G + 2 * u + 2)
+        quantize_units(last, 0, 1)
+        store_state(last - 1)
         for f in range(2):
-            cols = slice(3 * DV + f * P, 3 * DV + (f + 1) * P)
-            quantize(vc[:, cols], vs[:, cols], v_grp[h][:, 1, f * P : (f + 1) * P, :].rearrange("p n t -> p (n t)"))
+            quantize_kv(last, G * DK + (G - 1) * DV + f * P, v_words[last][:, 1:, f * P : (f + 1) * P, :])
         for g in range(G):
             for f in range(2):
-                cols = slice(g * DV + f * P, g * DV + (f + 1) * P)
-                nc.tensor.matmul_mx(
-                    out=halves[f][:, :P],
-                    lhsT=kc[:, g * DK : (g + 1) * DK].bitcast(FP8X4),
-                    lhsT_scale=ks[:, g * DK : (g + 1) * DK],
-                    rhs=vc[:, cols].bitcast(FP8X4),
-                    rhs_scale=vs[:, cols],
-                    start=(g == 0),
-                    stop=(g == G - 1),
-                )
-        o0 = stage.tile([P, P], F32, name="o_half")
-        nc.scalar.copy(out=o0[:], in_=halves[0][:, :P])
-        nc.sync.dma_start(out=out[h][:, :P], in_=o0[:])
-        o1 = stage.tile([P, P], F32, name="o_half")
-        nc.vector.tensor_copy(out=o1[:], in_=halves[1][:, :P])
-        nc.scalar.dma_start(out=out[h][:, P:], in_=o1[:])
+                state_pass(halves[f][:, :P], last, g, f * P, (f + 1) * P)
+        low = stage.tile([P, P], F32, name="result_half")
+        nc.scalar.copy(out=low[:], in_=halves[0][:, :P])
+        nc.sync.dma_start(out=out[last][:, :P], in_=low[:])
+        high = stage.tile([P, P], F32, name="result_half")
+        nc.vector.tensor_copy(out=high[:], in_=halves[1][:, :P])
+        nc.scalar.dma_start(out=out[last][:, P:], in_=high[:])

@@ -17,26 +17,32 @@ P = 128
 G = 4
 FLOPS = 2 * T * L * H * (DK + DV) + 2 * T * H * DK * DV
 
-WEIGHT_LOADS = ((0, 2), (2, 4), (4, H))
-VECTOR_BANKS, SCALAR_BANKS = 4, 3
-CODE_BUFS = 5
-SHIFT_ROUND = 1
+WV_LOADS = ((0, 2), (2, 5), (5, H))
+WK_LOADS = ((0, 2), (2, 5), (5, H))
+VECTOR_BANKS, SCALAR_BANKS = 4, 4
+ROUNDS = H + 1
+DIRECT = (4, 3, 2, 3, 2, 2, 2, 2, 2)
+WOVEN = (0, 0, 0, 0, 1, 1, 1, 3, 2)
 
 
-def direct_units(r):
-    return 1 if r % 2 == 0 and r > 0 else 2
-
-
-def unit(r, u):
-    if r < 2:
-        return u % 2, 2 * r + u // 2
-    return r, u
+def units(r):
+    if r == 0:
+        return [(0, 0), (1, 0)]
+    if r == 1:
+        return [(0, 1), (1, 1), (2, 0), (2, 1)]
+    if r == 2:
+        return [(0, 2), (0, 3), (1, 2), (1, 3)]
+    return [(r - 1, 2), (r - 1, 3), (r, 0), (r, 1)][: 2 if r == H else 4]
 
 
 def place(h, g):
-    if h < 2:
-        return g // 2, 2 * (g % 2) + h
-    return h, g
+    for r in range(ROUNDS):
+        if (h, g) in units(r):
+            return r, units(r).index((h, g))
+
+
+def widths(n):
+    return [n] if n <= 4 else [4, n - 4] if n != 6 else [3, 3]
 
 
 def tile_latent_kv_state_s7_kernel(tc, c, wk, wv_bytes, wv_scale, keep, write, out):
@@ -62,33 +68,35 @@ def tile_latent_kv_state_s7_kernel(tc, c, wk, wv_bytes, wv_scale, keep, write, o
         wv_scl = const.tile([P, H, DV], U8, name="wv_scl", align_bytes=64)
 
         c_rows = {}
-        for g in range(G):
-            for b in range(2):
-                c_rows[g, b] = const.tile([P, 2, L], BF16, name="c_rows%d%d" % (g, b), align_bytes=64)
+        for b in range(2):
+            c_rows[0, b] = const.tile([P, 2, L], BF16, name="c_rows0%d" % b, align_bytes=64)
+        c_group = {}
+        for g in range(1, G):
+            c_group[g] = const.tile([P, 4 * L], BF16, name="c_group%d" % g, align_bytes=64)
         wk_load, wv_load = {}, {}
-        for first, end in WEIGHT_LOADS:
+        for first, end in WV_LOADS:
             wv_load[first] = const.tile([P, 4, (end - first) * DV], U8, name="wv_load%d" % first, align_bytes=64)
+        for first, end in WK_LOADS:
             wk_load[first] = const.tile([P, 4, (end - first) * DK], BF16, name="wk_load%d" % first, align_bytes=64)
 
-        def load_start(h):
-            return max(first for first, end in WEIGHT_LOADS if first <= h)
-
         def wk_rows(h):
-            col = (h - load_start(h)) * DK
-            return wk_load[load_start(h)][:, :, col : col + DK]
+            first = max(f for f, e in WK_LOADS if f <= h)
+            return wk_load[first][:, :, (h - first) * DK : (h - first + 1) * DK]
 
         def wv_row(h, j):
-            col = (h - load_start(h)) * DV
-            return wv_load[load_start(h)][:, j, col : col + DV]
+            first = max(f for f, e in WV_LOADS if f <= h)
+            return wv_load[first][:, j, (h - first) * DV : (h - first + 1) * DV]
 
         ctx.enter_context(tc.manual_schedule())
 
         wv_view = wv_bytes.rearrange("(q j) w -> q j w", j=4)
         wk_view = wk.rearrange("(q j) w -> q j w", j=4)
-        c_view = c.rearrange("(g p b i) l -> g b p i l", p=P, b=2, i=2)
 
-        def load_c(g, b):
-            nc.sync.dma_start(out=c_rows[g, b][:], in_=c_view[g, b])
+        def load_c(g):
+            nc.sync.dma_start(out=c_group[g][:], in_=c.rearrange("(g p t) l -> g p (t l)", p=P, t=4)[g])
+
+        def load_c_half(b):
+            nc.sync.dma_start(out=c_rows[0, b][:], in_=c.rearrange("(g p b i) l -> g b p i l", p=P, b=2, i=2)[0, b])
 
         def load_wv(first, end):
             nc.sync.dma_start(out=wv_load[first][:], in_=wv_view[:, :, first * DV : end * DV])
@@ -97,22 +105,19 @@ def tile_latent_kv_state_s7_kernel(tc, c, wk, wv_bytes, wv_scale, keep, write, o
             nc.sync.dma_start(out=wk_load[first][:], in_=wk_view[:, :, first * DK : end * DK])
 
         nc.scalar.dma_start(out=row_scale[:], in_=wv_scale.rearrange("(q j) o -> q (j o)", j=4))
-        load_wv(*WEIGHT_LOADS[0])
-        load_c(0, 0)
-        load_c(0, 1)
-        load_wk(*WEIGHT_LOADS[0])
-        load_c(1, 0)
-        load_c(1, 1)
-        load_c(2, 0)
+        load_wv(*WV_LOADS[0])
+        load_c_half(0)
+        load_c_half(1)
+        load_wk(*WK_LOADS[0])
+        load_wv(*WV_LOADS[1])
         nc.sync.dma_start(out=keep_raw[:], in_=keep.rearrange("(g p t) h -> p g (t h)", p=P, t=4))
         nc.sync.dma_start(out=write_raw[:], in_=write.rearrange("(g p t) h -> p g (t h)", p=P, t=4))
-        load_wv(*WEIGHT_LOADS[1])
-        load_c(2, 1)
-        load_wk(*WEIGHT_LOADS[1])
-        load_c(3, 0)
-        load_c(3, 1)
-        load_wv(*WEIGHT_LOADS[2])
-        load_wk(*WEIGHT_LOADS[2])
+        load_c(1)
+        load_wk(*WK_LOADS[1])
+        load_c(2)
+        load_c(3)
+        load_wv(*WV_LOADS[2])
+        load_wk(*WK_LOADS[2])
 
         nc.vector.memset(warm[:], 0.0)
         nc.scalar.activation(out=warm[:], in_=warm[:], func=COPY)
@@ -124,9 +129,6 @@ def tile_latent_kv_state_s7_kernel(tc, c, wk, wv_bytes, wv_scale, keep, write, o
 
         def scalar_bank():
             return psum.tile([P, 512], F32, name="scalar_bank", bufs=SCALAR_BANKS)
-
-        def state_bank():
-            return psum.tile([P, 512], F32, name="state_bank")
 
         def warm_up(count):
             bank = vector_bank()
@@ -142,77 +144,64 @@ def tile_latent_kv_state_s7_kernel(tc, c, wk, wv_bytes, wv_scale, keep, write, o
         def quantize(cod, scl, src):
             nc.vector.quantize_mx(out=cod.bitcast(FP8X4), scales=scl, in_=src)
 
-        wv_wide, wv_words, wk_words, wk_woven, wv_woven = {}, {}, {}, {}, {}
+        def weave(dst, rows):
+            for j in (0, 2):
+                nc.tensor.matmul(out=dst.rearrange("p n j -> p j n")[:, j : j + 2, :], lhsT=ident_bf[:], rhs=rows[:, j : j + 2, :], start=True, stop=True)
+
+        def as_words(bank, n):
+            return bank[:].bitcast(BF16)[:, : 4 * n].rearrange("p (n j) -> p n j", j=4)
+
+        quantised = set()
+        made = set()
+
+        wv_wide, words = {}, {}
 
         def widen(h, j, on_vector=False):
             if h not in wv_wide:
-                wv_wide[h] = stage.tile([P, 4, DV], BF16, name="wv_wide", align_bytes=64)
+                wv_wide[h] = stage.tile([P, 4, DV], BF16, name="wv_wide", bufs=3, align_bytes=64)
             src = wv_row(h, j).bitcast(FP8)
             if on_vector:
                 nc.vector.tensor_scalar(out=wv_wide[h][:, j, :], in0=src, scalar1=row_scale[:, j : j + 1], scalar2=None, op0=ALU.mult)
             else:
                 nc.scalar.activation(out=wv_wide[h][:, j, :], in_=src, func=COPY, scale=row_scale[:, j : j + 1])
+            made.add(("wide", h, j))
 
-        def interleave_wv(h, copy):
-            wv_words[h] = stage.tile([P, DV, 4], BF16, name="wv_words", bufs=3, align_bytes=64)
-            interleave(copy, wv_words[h][:], wv_wide.pop(h)[:])
+        def weight_rows(kind, h):
+            return wv_wide.pop(h)[:] if kind == "wv" else wk_rows(h)
 
-        def interleave_wk(h):
-            wk_words[h] = stage.tile([P, DK, 4], BF16, name="wk_words", bufs=3, align_bytes=64)
-            interleave(nc.vector.tensor_copy, wk_words[h][:], wk_rows(h))
+        def weight_words(kind, h):
+            n = DV if kind == "wv" else DK
+            tile = stage.tile([P, n, 4], BF16, name=kind + "_words", bufs=3, align_bytes=64)
+            words[kind, h] = tile[:]
+            return tile[:]
 
-        def pool_interleave_wk(h):
-            wk_words[h] = stage.tile([P, DK, 4], BF16, name="first_release", bufs=1, align_bytes=64)
-            pool_interleave(wk_words[h][:], wk_rows(h).rearrange("p j n -> p n j"))
+        def vector_interleave(kind, h):
+            interleave(nc.vector.tensor_copy, weight_words(kind, h), weight_rows(kind, h))
 
-        def weave_wk(h, bank):
-            wk_woven[h] = bank[:, DV:].bitcast(BF16).rearrange("p (n j) -> p n j", j=4)
-            dst = wk_woven[h].rearrange("p n j -> p j n")
-            for j in (0, 2):
-                nc.tensor.matmul(out=dst[:, j : j + 2, :], lhsT=ident_bf[:], rhs=wk_rows(h)[:, j : j + 2, :], start=True, stop=True)
+        def quantize_weight(kind, h):
+            cod, scl = (wv_cod, wv_scl) if kind == "wv" else (wk_cod, wk_scl)
+            quantize(cod[:, h, :], scl[:, h, :], words.pop((kind, h)).rearrange("p n j -> p (n j)"))
+            quantised.add((kind, h))
 
-        def weave_wv(h):
-            wv_woven[h] = psum.tile([P, DV, 4], BF16, name="state_bank")
-            dst = wv_woven[h][:].rearrange("p n j -> p j n")
-            src = wv_wide.pop(h)
-            for j in (0, 2):
-                nc.tensor.matmul(out=dst[:, j : j + 2, :], lhsT=ident_bf[:], rhs=src[:, j : j + 2, :], start=True, stop=True)
-
-        def woven_wv_out(h):
-            wv_words[h] = stage.tile([P, DV, 4], BF16, name="wv_words", bufs=3, align_bytes=64)
-            nc.scalar.copy(out=wv_words[h][:], in_=wv_woven.pop(h)[:])
-
-        def woven_wk_out(h):
-            wk_words[h] = stage.tile([P, DK, 4], BF16, name="wk_words", bufs=3, align_bytes=64)
-            nc.scalar.copy(out=wk_words[h][:], in_=wk_woven.pop(h))
-
-        def quantize_wk(h):
-            quantize(wk_cod[:, h, :], wk_scl[:, h, :], wk_words.pop(h)[:].rearrange("p n j -> p (n j)"))
-
-        def quantize_wv(h):
-            quantize(wv_cod[:, h, :], wv_scl[:, h, :], wv_words.pop(h)[:].rearrange("p n j -> p (n j)"))
-
-        c_turned, c_words = {}, {}
-
-        def transpose_c(g, b):
-            words = c_rows[g, b][:].bitcast(F32)
-            c_turned[g, b] = state_bank() if b == 0 and g % 2 == 0 else scalar_bank()
+        def transpose_c(bank, g, b):
+            if g == 0:
+                rows = c_rows[g, b][:].bitcast(F32)
+            else:
+                rows = c_group[g][:].bitcast(F32).rearrange("p (t w) -> p t w", t=4)[:, 2 * b : 2 * b + 2, :]
             for i in range(2):
                 for u in range(2):
                     col = (2 * i + u) * P
-                    nc.tensor.transpose(c_turned[g, b][:, col : col + P], words[:, i, u::2], ident[:])
+                    nc.tensor.transpose(bank[:, col : col + P], rows[:, i, u::2], ident[:])
 
-        def turned_c_out(g, b):
-            if (g, b) == (G - 1, 1):
-                c_words[g, b] = stage.tile([P, 2, P, 4], BF16, name="first_release", bufs=1, align_bytes=64)
-            else:
-                c_words[g, b] = stage.tile([P, 2, P, 4], BF16, name="c_words", bufs=4, align_bytes=64)
-            src = c_turned.pop((g, b))[:].rearrange("q (i u p) -> q i p u", i=2, u=2)
-            nc.scalar.copy(out=c_words[g, b][:].bitcast(F32), in_=src)
+        def turned_c_out(bank, g, b, copy, name="c_words", bufs=4):
+            tile = stage.tile([P, 2, P, 4], BF16, name=name, bufs=bufs, align_bytes=64)
+            copy(out=tile[:].bitcast(F32), in_=bank[:].rearrange("q (i u p) -> q i p u", i=2, u=2))
+            words["c", g, b] = tile[:]
 
         def quantize_c(g, b):
             cols = slice(2 * b * P, 2 * (b + 1) * P)
-            quantize(c_cod[:, g, cols], c_scl[:, g, cols], c_words.pop((g, b))[:].rearrange("q i p e -> q (i p e)"))
+            quantize(c_cod[:, g, cols], c_scl[:, g, cols], words.pop(("c", g, b)).rearrange("q i p e -> q (i p e)"))
+            quantised.add(("c", g, b))
 
         def widen_factors():
             nc.vector.tensor_copy(out=keep_f[:], in_=keep_raw[:].rearrange("p g (t h) -> p g h t", t=4))
@@ -230,270 +219,351 @@ def tile_latent_kv_state_s7_kernel(tc, c, wk, wv_bytes, wv_scale, keep, write, o
                 stop=True,
             )
 
-        key_bank, piece_bank, rows_bank = {}, {}, {}
-
-        def project_keys(r, u):
-            h, g = unit(r, u)
-            key_bank[r, u] = vector_bank()
+        def project_keys(bank, r, u):
+            h, g = units(r)[u]
             for t in range(4):
-                project(key_bank[r, u][:, t * DK : (t + 1) * DK], g, t, wk_cod[:, h, :], wk_scl[:, h, :])
+                project(bank[:, t * DK : (t + 1) * DK], g, t, wk_cod[:, h, :], wk_scl[:, h, :])
 
-        def project_piece(r, d, new_bank=vector_bank):
-            h, g = unit(r, d // 2)
-            piece_bank[r, d] = new_bank()
-            cols = slice((d % 2) * P, (d % 2 + 1) * P)
+        def project_piece(bank, r, m):
+            h, g = units(r)[m // 2]
+            cols = slice((m % 2) * P, (m % 2 + 1) * P)
             for t in range(4):
-                project(piece_bank[r, d][:, t * P : (t + 1) * P], g, t, wv_cod[:, h, cols], wv_scl[:, h, cols])
+                project(bank[:, t * P : (t + 1) * P], g, t, wv_cod[:, h, cols], wv_scl[:, h, cols])
 
-        def project_rows(r, n):
-            h, g = unit(r, direct_units(r) + n // 2)
-            rows_bank[r, n] = scalar_bank()
+        def project_rows(bank, r, u, b):
+            h, g = units(r)[u]
             for i in range(2):
-                project(rows_bank[r, n][:, i * DV : (i + 1) * DV], g, 2 * (n % 2) + i, wv_cod[:, h, :], wv_scl[:, h, :])
+                project(bank[:, i * DV : (i + 1) * DV], g, 2 * b + i, wv_cod[:, h, :], wv_scl[:, h, :])
 
-        kv_words, v_rows, v_words, shifted_rows = {}, {}, {}, {}
+        own, rows, woven = {}, {}, {}
 
-        def keys_out(r, u):
-            h, g = unit(r, u)
-            if u == 0:
-                kv_words[r] = stage.tile([P, G + 2 * direct_units(r), P, 4], BF16, name="kv_words", align_bytes=64)
+        def own_words(r):
+            if r not in own:
+                own[r] = stage.tile([P, len(units(r)) + DIRECT[r], P, 4], BF16, name="own_words", align_bytes=64)
+            return own[r]
+
+        def keys_out(bank, r, u):
+            h, g = units(r)[u]
             nc.vector.scalar_tensor_tensor(
-                out=kv_words[r][:, u, :, :],
-                in0=key_bank.pop((r, u))[:].rearrange("p (t n) -> p n t", t=4),
+                out=own_words(r)[:, u, :, :],
+                in0=bank[:].rearrange("p (t n) -> p n t", t=4),
                 scalar=0.0,
                 in1=keep_f[:, g, h, :].unsqueeze(1).to_broadcast([P, DK, 4]),
                 op0=ALU.max,
                 op1=ALU.mult,
             )
 
-        def piece_out(r, d):
-            h, g = unit(r, d // 2)
+        def piece_out(bank, r, m):
+            h, g = units(r)[m // 2]
             nc.vector.tensor_tensor(
-                out=kv_words[r][:, G + d, :, :],
-                in0=piece_bank.pop((r, d))[:].rearrange("p (t n) -> p n t", t=4),
+                out=own_words(r)[:, len(units(r)) + m, :, :],
+                in0=bank[:].rearrange("p (t n) -> p n t", t=4),
                 in1=write_f[:, g, h, :].unsqueeze(1).to_broadcast([P, P, 4]),
                 op=ALU.mult,
             )
 
-        def shifted_piece_out(r, d):
-            h, g = unit(r, d // 2)
-            shifted_rows[r] = stage.tile([P, 4, P], BF16, name="shifted_rows", bufs=1, align_bytes=64)
-            bank = piece_bank.pop((r, d))
+        def scaled_rows(r):
+            if r not in rows:
+                rows[r] = stage.tile([P, 2 * len(units(r)) - DIRECT[r], 4, P], BF16, name="rows", align_bytes=64)
+            return rows[r]
+
+        def half_out(bank, r, m):
+            h, g = units(r)[m // 2]
             for t in range(4):
-                nc.scalar.activation(out=shifted_rows[r][:, t, :], in_=bank[:, t * P : (t + 1) * P], func=COPY, scale=write_f[:, g, h, t : t + 1])
+                nc.scalar.activation(out=scaled_rows(r)[:, m - DIRECT[r], t, :], in_=bank[:, t * P : (t + 1) * P], func=COPY, scale=write_f[:, g, h, t : t + 1])
+            made.add(("rows", r, m))
 
-        def rows_out(r, n):
-            if n == 0:
-                v_rows[r] = stage.tile([P, G - direct_units(r), 4, DV], BF16, name="v_rows", align_bytes=64)
-            h, g = unit(r, direct_units(r) + n // 2)
-            bank = rows_bank.pop((r, n))
+        def rows_out(bank, r, u, b):
+            h, g = units(r)[u]
+            first = 2 * u - DIRECT[r]
             for i in range(2):
-                t = 2 * (n % 2) + i
-                nc.scalar.activation(out=v_rows[r][:, n // 2, t, :], in_=bank[:, i * DV : (i + 1) * DV], func=COPY, scale=write_f[:, g, h, t : t + 1])
+                t = 2 * b + i
+                src = bank[:, i * DV : (i + 1) * DV].rearrange("p (m n) -> p m n", m=2)
+                nc.scalar.activation(out=scaled_rows(r)[:, first : first + 2, t, :], in_=src, func=COPY, scale=write_f[:, g, h, t : t + 1])
+            if b == 1:
+                made.add(("rows", r, 2 * u))
+                made.add(("rows", r, 2 * u + 1))
 
-        def pool_interleave_v(r):
-            v_words[r] = stage.tile([P, G - direct_units(r), DV, 4], BF16, name="v_words", bufs=1, align_bytes=64)
-            pool_interleave(v_words[r][:], v_rows.pop(r)[:].rearrange("p u t n -> p u n t"))
+        def weave_piece(bank, r, i):
+            weave(as_words(bank, P), scaled_rows(r)[:, i, :, :])
 
-        def scalar_interleave_v(r, i):
-            if i == 0:
-                v_words[r] = stage.tile([P, G - direct_units(r), DV, 4], BF16, name="v_words_last", bufs=1, align_bytes=64)
-            interleave(nc.scalar.copy, v_words[r][:, i, :, :], v_rows[r][:, i, :, :])
+        def woven_piece_out(bank, r, i):
+            if r not in woven:
+                woven[r] = stage.tile([P, WOVEN[r], P, 4], BF16, name="woven", bufs=3, align_bytes=64)
+            nc.scalar.copy(out=woven[r][:, i, :, :], in_=as_words(bank, P))
 
-        kv_cod, kv_scl = {}, {}
+        def weave_weight(bank, kind, h):
+            weave(as_words(bank, DV if kind == "wv" else DK), weight_rows(kind, h))
 
-        def new_codes(r):
-            kv_cod[r] = stage.tile([P, G * (DK + DV)], U32, name="kv_cod", bufs=CODE_BUFS, align_bytes=64)
-            kv_scl[r] = stage.tile([P, G * (DK + DV)], U8, name="kv_scl", bufs=CODE_BUFS, align_bytes=64)
+        def woven_weight_out(bank, kind, h):
+            nc.scalar.copy(out=weight_words(kind, h), in_=as_words(bank, DV if kind == "wv" else DK))
 
-        def quantize_kv(r, col, src):
-            flat = src.rearrange("p m n t -> p (m n t)")
-            cols = slice(col, col + flat.shape[1] // 4)
-            quantize(kv_cod[r][:, cols], kv_scl[r][:, cols], flat)
+        pooled = {}
 
-        def quantize_pieces(r, first, end):
-            quantize_kv(r, first * P, kv_words[r][:, first:end, :, :])
+        def pool_tile(w, pieces):
+            pooled[w] = stage.tile([P, pieces, P, 4], BF16, name="pool_out", bufs=1, align_bytes=64)
 
-        def quantize_units(r, first, end):
-            quantize_kv(r, G * DK + (direct_units(r) + first) * DV, v_words[r][:, first:end, :, :])
+        def pool_weights(w, jobs):
+            pool_tile(w, sum(2 if kind == "wv" else 1 for kind, h in jobs))
+            at = 0
+            for kind, h in jobs:
+                n = 2 if kind == "wv" else 1
+                words[kind, h] = pooled[w][:, at : at + n, :, :].rearrange("p m n j -> p (m n) j")
+                pool_interleave(words[kind, h], weight_rows(kind, h).rearrange("p j n -> p n j"))
+                at = at + n
 
-        def quantize_pooled(r):
-            quantize_units(r, 0, 2)
-            if direct_units(r) == 1:
-                quantize_units(r, 2, 3)
+        def pool_values(r):
+            pool_tile(r + 1, 2 * len(units(r)) - DIRECT[r] - WOVEN[r])
+            pool_interleave(pooled[r + 1][:], scaled_rows(r)[:, WOVEN[r] :, :, :].rearrange("p m t n -> p m n t"))
+
+        cod, scl = {}, {}
+        for r in range(ROUNDS):
+            cod[r] = const.tile([P, len(units(r)) * (DK + DV)], U32, name="cod%d" % r, align_bytes=64)
+            scl[r] = const.tile([P, len(units(r)) * (DK + DV)], U8, name="scl%d" % r, align_bytes=64)
+
+        def quantize_pieces(r, at, src):
+            n = src.shape[1]
+            cols = slice(at * P, (at + n) * P)
+            quantize(cod[r][:, cols], scl[r][:, cols], src.rearrange("p m n t -> p (m n t)"))
+            for m in range(at, at + n):
+                quantised.add(("piece", r, m))
+
+        def quantize_calls(r, at, tile, first, end):
+            calls = []
+            for n in widths(end - first):
+                calls.append((quantize_pieces, r, at + first, tile[:, first : first + n, :, :]))
+                first = first + n
+            return calls
 
         def state_pass(dst, h, g, first, end):
             r, u = place(h, g)
             k_cols = slice(u * DK, (u + 1) * DK)
-            v_cols = slice(G * DK + u * DV + first, G * DK + u * DV + end)
+            at = len(units(r)) * DK + u * DV
+            v_cols = slice(at + first, at + end)
             nc.tensor.matmul_mx(
                 out=dst,
-                lhsT=kv_cod[r][:, k_cols].bitcast(FP8X4),
-                lhsT_scale=kv_scl[r][:, k_cols],
-                rhs=kv_cod[r][:, v_cols].bitcast(FP8X4),
-                rhs_scale=kv_scl[r][:, v_cols],
+                lhsT=cod[r][:, k_cols].bitcast(FP8X4),
+                lhsT_scale=scl[r][:, k_cols],
+                rhs=cod[r][:, v_cols].bitcast(FP8X4),
+                rhs_scale=scl[r][:, v_cols],
                 start=(g == 0),
                 stop=(g == G - 1),
             )
 
-        state = {}
-
-        def sum_state(h, bank):
-            state[h] = bank
+        def sum_state(bank, h):
             for g in range(G):
                 state_pass(bank[:, :DV], h, g, 0, DV)
 
-        def store_state(h):
+        def store_state(bank, h):
             result = stage.tile([P, DV], F32, name="result")
-            nc.scalar.copy(out=result[:], in_=state.pop(h)[:, :DV])
+            nc.scalar.copy(out=result[:], in_=bank[:, :DV])
             nc.sync.dma_start(out=out[h], in_=result[:])
 
+        def head_pieces(h):
+            need = []
+            for g in range(G):
+                r, u = place(h, g)
+                n = len(units(r))
+                need.extend([("piece", r, u), ("piece", r, n + 2 * u), ("piece", r, n + 2 * u + 1)])
+            return need
+
+        def unit_operands(kind, r, u):
+            h, g = units(r)[u]
+            return [(kind, h), ("c", g, 0), ("c", g, 1)]
+
+        def vector_jobs(r):
+            keys = [(project_keys, keys_out, (r, u), unit_operands("wk", r, u)) for u in range(len(units(r)))]
+            pieces = [(project_piece, piece_out, (r, m), unit_operands("wv", r, m // 2)) for m in range(DIRECT[r])]
+            if r == 0:
+                return keys[:1] + pieces[:2] + keys[1:] + pieces[2:]
+            return keys[:2] + pieces + keys[2:]
+
+        def row_jobs(r):
+            jobs = []
+            if DIRECT[r] % 2:
+                jobs.append((project_piece, half_out, (r, DIRECT[r]), unit_operands("wv", r, DIRECT[r] // 2)))
+            for u in range((DIRECT[r] + 1) // 2, len(units(r))):
+                jobs.extend((project_rows, rows_out, (r, u, b), unit_operands("wv", r, u)) for b in range(2))
+            return jobs
+
+        def piece_job(r, i):
+            return (weave_piece, woven_piece_out, (r, i), [("rows", r, DIRECT[r] + i)])
+
+        def weight_job(kind, h):
+            return (weave_weight, woven_weight_out, (kind, h), [("wide", h, j) for j in range(4)] if kind == "wv" else [])
+
+        def turn_job(g, b):
+            return (transpose_c, turned_out, (g, b), [("turn", g)])
+
+        def turned_out(bank, g, b):
+            turned_c_out(bank, g, b, nc.scalar.copy)
+
+        def state_job(h):
+            return (sum_state, store_state, (h,), head_pieces(h))
+
+        def widen_pair(h, j):
+            widen(h, j)
+            widen(h, j + 1)
+
+        def widen_jobs(h):
+            return [(None, widen_pair, (h, j), []) for j in (0, 2)]
+
+        def scalar_steps(p):
+            row = [[job] for job in row_jobs(p)]
+            wide = [[[job] for job in widen_jobs(h)] for h in range(H)]
+            if p == 0:
+                return [[], wide[3][0], [turn_job(1, 0)], [turn_job(1, 1)], wide[3][1], [turn_job(2, 0)], [turn_job(2, 1)]] + wide[4]
+            if p == 1:
+                return [[turn_job(3, 0)], [turn_job(3, 1)]] + wide[5] + row[:3] + [[weight_job("wk", 4), weight_job("wk", 5)]] + row[3:4] + [[weight_job("wv", 5)]] + row[4:]
+            if p == 2:
+                return wide[6] + row[:3] + [[weight_job("wk", 6)]] + row[3:4] + [[weight_job("wv", 6)]] + row[4:]
+            if p == 3:
+                return wide[7] + row[:3] + [[weight_job("wk", 7)]] + row[3:4] + [[weight_job("wv", 7)]] + row[4:]
+            if p == 4:
+                return row[:4] + [[state_job(0)]] + row[4:5] + [[piece_job(p, 0)]] + row[5:]
+            if p == 5:
+                return row[:4] + [[state_job(1)]] + row[4:5] + [[piece_job(p, 0), state_job(2)]] + row[5:]
+            if p == 6:
+                return row[:4] + [[state_job(3)]] + row[4:5] + [[piece_job(p, 0)]] + row[5:]
+            if p == 7:
+                return row[:4] + [[state_job(4), piece_job(p, 0)]] + row[4:5] + [[piece_job(p, 1)]] + row[5:] + [[piece_job(p, 2)]]
+            return row + [[state_job(5)], [piece_job(p, 0)], [piece_job(p, 1)]]
+
+        v_jobs = vector_jobs(0)
+        s_jobs = [job for p in range(ROUNDS) for step in scalar_steps(p) for job in step if job[0] is not None]
+        v_full, s_full = [], []
+
+        def refill(jobs, full, new_bank, depth, most=VECTOR_BANKS):
+            for i in range(most):
+                if not (jobs and len(full) < depth and all(x in quantised or x in made for x in jobs[0][3])):
+                    break
+                fill, empty, args, need = jobs.pop(0)
+                bank = new_bank()
+                fill(bank, *args)
+                full.append(bank)
+
+        def refill_both(most=VECTOR_BANKS):
+            refill(v_jobs, v_full, vector_bank, VECTOR_BANKS, most)
+            refill(s_jobs, s_full, scalar_bank, SCALAR_BANKS)
+
+        def run(job, full):
+            fill, empty, args, need = job
+            if fill is None:
+                empty(*args)
+            else:
+                empty(full.pop(0), *args)
+            refill_both(1)
+
         warm_up(4)
-        for h in range(2):
-            for j in range(4):
-                widen(h, j, on_vector=(j % 2 == 1))
-        for g in range(2):
-            for b in range(2):
-                transpose_c(g, b)
-                turned_c_out(g, b)
-            if g == 0:
-                warm_up(2)
-        interleave_wv(0, nc.vector.tensor_copy)
-        interleave_wv(1, nc.vector.tensor_copy)
-        quantize_wv(0)
-        interleave_wk(0)
-        quantize_c(0, 0)
-        quantize_wk(0)
-        quantize_c(0, 1)
-        interleave_wk(1)
-        quantize_wv(1)
-        widen_factors()
-        quantize_wk(1)
-        quantize_c(1, 0)
-        quantize_c(1, 1)
-        project_keys(0, 0)
-        project_piece(0, 0)
-        project_piece(0, 1)
-        transpose_c(2, 0)
-        project_keys(0, 1)
-        turned_c_out(2, 0)
         for j in range(4):
-            widen(2, j)
-        transpose_c(2, 1)
-        keys_out(0, 0)
-        project_piece(0, 2)
-        turned_c_out(2, 1)
-        piece_out(0, 0)
-        project_piece(0, 3)
+            widen(0, j, on_vector=(j % 2 == 1))
+        for j in range(4):
+            widen(1, j, on_vector=(j % 2 == 1))
+        turned = [scalar_bank(), scalar_bank()]
         for b in range(2):
-            transpose_c(3, b)
-        piece_out(0, 1)
-        project_keys(0, 2)
-        turned_c_out(3, 0)
-        project_rows(0, 0)
-        turned_c_out(3, 1)
-        keys_out(0, 1)
-        project_keys(0, 3)
-        project_rows(0, 1)
-        project_rows(0, 2)
-        rows_out(0, 0)
-        project_rows(0, 3)
-        for n in range(1, 4):
-            rows_out(0, n)
-        for b in range(2):
-            quantize_c(2, b)
-            piece_out(0, 2 + b)
-        quantize_c(3, 0)
-        for u in (2, 3):
-            keys_out(0, u)
-        quantize_c(3, 1)
-        interleave_wv(2, nc.scalar.copy)
+            transpose_c(turned[b], 0, b)
+        warm_up(2)
+        turned_c_out(turned[0], 0, 0, nc.scalar.copy)
+        turned_c_out(turned[1], 0, 1, nc.scalar.copy)
+        vector_interleave("wv", 0)
+        vector_interleave("wv", 1)
+        quantize_weight("wv", 0)
+        quantize_c(0, 0)
+        vector_interleave("wk", 0)
+        quantize_c(0, 1)
+        quantize_weight("wk", 0)
+        refill_both()
+        words["wk", 1] = stage.tile([P, DK, 4], BF16, name="pool_out", bufs=1, align_bytes=64)[:]
+        interleave(nc.vector.tensor_copy, words["wk", 1], wk_rows(1))
+        widen_factors()
+        quantize_weight("wk", 1)
+        quantize_weight("wv", 1)
+        refill_both()
+
+        def scalar_pieces(r):
+            at = len(units(r)) + DIRECT[r]
+            calls = quantize_calls(r, at, woven[r], 0, WOVEN[r]) if WOVEN[r] else []
+            return calls + quantize_calls(r, at + WOVEN[r], pooled[r + 1], 0, pooled[r + 1].shape[1])
+
+        def quantize_run(r):
+            n = len(units(r - 1))
+            first = []
+            if r == 1:
+                first = [(quantize_c, 1, 0), (quantize_c, 1, 1)]
+            if r == 2:
+                first = [(quantize_c, g, b) for g in (2, 3) for b in range(2)]
+            if r in (3, 4, 5):
+                h = r + 2
+                first = [(quantize_weight, "wk", h), (quantize_weight, "wv", h)]
+                if r == 3:
+                    first.append((quantize_weight, "wk", 4))
+            mine = quantize_calls(r - 1, 0, own_words(r - 1), n, n + DIRECT[r - 1])
+            if r == 1:
+                release = [(quantize_weight, "wk", 2), (quantize_weight, "wv", 2)]
+            elif r == 2:
+                release = [(quantize_weight, "wk", 3), (quantize_weight, "wv", 3), (quantize_weight, "wv", 4)]
+            else:
+                release = scalar_pieces(r - 2)
+            return first + mine + release + quantize_calls(r - 1, 0, own_words(r - 1), 0, n)
+
+        def width(step):
+            if step[0] is quantize_pieces:
+                return step[3].shape[1] * 4 * P
+            return 4 * DK if step[1] == "wk" else 4 * DV
+
+        def call(step):
+            step[0](*step[1:])
+            refill_both(1)
+
+        def scalar_step(steps):
+            for job in steps.pop(0) if steps else []:
+                run(job, s_full)
+
+        for p in range(ROUNDS):
+            steps = scalar_steps(p)
+            if p == 0:
+                for job in widen_jobs(2):
+                    run(job, s_full)
+                made.add(("turn", 1))
+                refill_both()
+                pool_weights(0, [("wv", 2), ("wk", 2)])
+            elif p == 1:
+                pool_weights(1, [("wv", 3), ("wk", 3), ("wv", 4)])
+            else:
+                pool_values(p - 1)
+            for i, job in enumerate(vector_jobs(p)):
+                if p == 0 and i == 3:
+                    made.add(("turn", 2))
+                run(job, v_full)
+                scalar_step(steps)
+            if p == H:
+                break
+            columns = 0
+            v_jobs.extend(vector_jobs(p + 1))
+            for step in quantize_run(p + 1):
+                call(step)
+                columns = columns + width(step)
+                if columns >= 4 * 4 * P:
+                    columns = columns - 4 * 4 * P
+                    if p == 0:
+                        made.add(("turn", 3))
+                    scalar_step(steps)
+            while steps:
+                scalar_step(steps)
 
         last = H - 1
-        for r in range(1, H):
-            pieces = 2 * direct_units(r)
-            on_vector = pieces - 1 if r == SHIFT_ROUND else pieces
-            row_banks = 2 * G - pieces
-            prepares = 2 <= r < last
-            weaves_wv = prepares and row_banks == 6
-
-            if r >= 2:
-                bank = state_bank()
-            if r >= 4:
-                sum_state(r - 3, bank)
-            if prepares:
-                weave_wk(r + 1, bank)
-
-            if r >= 2:
-                quantize_wk(r)
-                quantize_wv(r)
-            new_codes(r - 1)
-            if direct_units(r - 1) == 1:
-                quantize_pieces(r - 1, G, G + 2)
-            if r >= 2:
-                quantize_pooled(r - 2)
-            quantize_pieces(r - 1, 0, G if direct_units(r - 1) == 1 else 2 * G)
-
-            if r == 1:
-                pool_interleave_wk(2)
-            pool_interleave_v(r - 1)
-
-            if prepares:
-                for j in range(4):
-                    widen(r + 1, j)
-                woven_wk_out(r + 1)
-                if not weaves_wv:
-                    interleave_wv(r + 1, nc.scalar.copy)
-            if r >= 4:
-                store_state(r - 3)
-
-            for u in range(G):
-                project_keys(r, u)
-            if r == SHIFT_ROUND:
-                project_piece(r, on_vector, scalar_bank)
-            ahead = SCALAR_BANKS - (pieces - on_vector)
-            for n in range(ahead):
-                project_rows(r, n)
-            if weaves_wv:
-                weave_wv(r + 1)
-            for u in range(G):
-                keys_out(r, u)
-                if u < on_vector:
-                    project_piece(r, u)
-            if r == SHIFT_ROUND:
-                shifted_piece_out(r, on_vector)
-                project_rows(r, ahead)
-            for n in range(row_banks):
-                rows_out(r, n)
-                if n + SCALAR_BANKS < row_banks:
-                    project_rows(r, n + SCALAR_BANKS)
-                if r == SHIFT_ROUND and n == 0:
-                    interleave(nc.scalar.copy, kv_words[r][:, G + on_vector, :, :], shifted_rows.pop(r)[:])
-                if weaves_wv and n == 2:
-                    woven_wv_out(r + 1)
-                if r == last and n == 2:
-                    scalar_interleave_v(r, 0)
-            if r == last:
-                scalar_interleave_v(r, 1)
-            if r == 3:
-                sum_state(0, scalar_bank())
-                store_state(0)
-            for d in range(on_vector):
-                piece_out(r, d)
-
         halves = [vector_bank(), vector_bank()]
-        sum_state(last - 2, vector_bank())
-        store_state(last - 2)
-        quantize_pooled(last - 1)
-        sum_state(last - 1, vector_bank())
-        new_codes(last)
-        quantize_pieces(last, 0, G)
-        for u in range(2):
-            quantize_pieces(last, G + 2 * u, G + 2 * u + 2)
-        quantize_units(last, 0, 1)
-        store_state(last - 1)
+        n = len(units(H))
+        for step in quantize_calls(H, 0, own_words(H), n, n + DIRECT[H]) + scalar_pieces(last):
+            call(step)
+        before_last = vector_bank()
+        sum_state(before_last, last - 1)
+        call(quantize_calls(H, 0, own_words(H), 0, n)[0])
+        while steps:
+            scalar_step(steps)
+        store_state(before_last, last - 1)
         for f in range(2):
-            quantize_kv(last, G * DK + (G - 1) * DV + f * P, v_words[last][:, 1:, f * P : (f + 1) * P, :])
+            quantize_pieces(H, n + DIRECT[H] + f, woven[H][:, f : f + 1, :, :])
         for g in range(G):
             for f in range(2):
                 state_pass(halves[f][:, :P], last, g, f * P, (f + 1) * P)

@@ -21,8 +21,8 @@ WV_LOADS = ((0, 2), (2, 5), (5, H))
 WK_LOADS = ((0, 2), (2, 5), (5, H))
 VECTOR_BANKS, SCALAR_BANKS = 4, 4
 ROUNDS = H + 1
-DIRECT = (4, 3, 2, 3, 2, 2, 2, 2, 2)
-WOVEN = (0, 0, 0, 0, 1, 1, 1, 3, 2)
+DIRECT = (4, 3, 3, 2, 2, 2, 2, 2, 1)
+WOVEN = (0, 0, 0, 1, 1, 1, 1, 4, 3)
 
 
 def units(r):
@@ -287,10 +287,13 @@ def tile_latent_kv_state_s7_kernel(tc, c, wk, wv_bytes, wv_scale, keep, write, o
         def weave_piece(bank, r, i):
             weave(as_words(bank, P), scaled_rows(r)[:, i, :, :])
 
-        def woven_piece_out(bank, r, i):
+        def woven_words(r):
             if r not in woven:
                 woven[r] = stage.tile([P, WOVEN[r], P, 4], BF16, name="woven", bufs=3, align_bytes=64)
-            nc.scalar.copy(out=woven[r][:, i, :, :], in_=as_words(bank, P))
+            return woven[r]
+
+        def woven_piece_out(bank, r, i):
+            nc.scalar.copy(out=woven_words(r)[:, i, :, :], in_=as_words(bank, P))
 
         def weave_weight(bank, kind, h):
             weave(as_words(bank, DV if kind == "wv" else DK), weight_rows(kind, h))
@@ -389,11 +392,17 @@ def tile_latent_kv_state_s7_kernel(tc, c, wk, wv_bytes, wv_scale, keep, write, o
         def piece_job(r, i):
             return (weave_piece, woven_piece_out, (r, i), [("rows", r, DIRECT[r] + i)])
 
+        def copy_piece(r, i):
+            interleave(nc.scalar.copy, woven_words(r)[:, i, :, :], scaled_rows(r)[:, i, :, :])
+
+        def copy_job(r, i):
+            return (None, copy_piece, (r, i), [])
+
         def weight_job(kind, h):
-            return (weave_weight, woven_weight_out, (kind, h), [("wide", h, j) for j in range(4)] if kind == "wv" else [])
+            return (weave_weight, woven_weight_out, (kind, h), [("wide", h, j) for j in range(4)] if kind == "wv" else [("turn", 1, 1)])
 
         def turn_job(g, b):
-            return (transpose_c, turned_out, (g, b), [("turn", g)])
+            return (transpose_c, turned_out, (g, b), [("turn", g, b)])
 
         def turned_out(bank, g, b):
             turned_c_out(bank, g, b, nc.scalar.copy)
@@ -412,22 +421,22 @@ def tile_latent_kv_state_s7_kernel(tc, c, wk, wv_bytes, wv_scale, keep, write, o
             row = [[job] for job in row_jobs(p)]
             wide = [[[job] for job in widen_jobs(h)] for h in range(H)]
             if p == 0:
-                return [[], wide[3][0], [turn_job(1, 0)], [turn_job(1, 1)], wide[3][1], [turn_job(2, 0)], [turn_job(2, 1)]] + wide[4]
+                return [[], wide[3][0], [turn_job(1, 0)], wide[3][1], [turn_job(1, 1)], [weight_job("wk", 4)], wide[4][0], [turn_job(2, 0)], wide[4][1]]
             if p == 1:
-                return [[turn_job(3, 0)], [turn_job(3, 1)]] + wide[5] + row[:3] + [[weight_job("wk", 4), weight_job("wk", 5)]] + row[3:4] + [[weight_job("wv", 5)]] + row[4:]
+                return wide[5][:1] + [[turn_job(2, 1)]] + wide[5][1:] + row[:1] + [[turn_job(3, 0)]] + row[1:2] + [[turn_job(3, 1)]] + row[2:] + [[weight_job("wk", 5)]]
             if p == 2:
-                return wide[6] + row[:3] + [[weight_job("wk", 6)]] + row[3:4] + [[weight_job("wv", 6)]] + row[4:]
+                return row + [[weight_job("wv", 5)], [weight_job("wk", 6), weight_job("wk", 7)]] + wide[6]
             if p == 3:
-                return wide[7] + row[:3] + [[weight_job("wk", 7)]] + row[3:4] + [[weight_job("wv", 7)]] + row[4:]
+                return row + [[weight_job("wv", 6)], [piece_job(p, 0)]] + wide[7]
             if p == 4:
-                return row[:4] + [[state_job(0)]] + row[4:5] + [[piece_job(p, 0)]] + row[5:]
+                return row + [[weight_job("wv", 7)], [piece_job(p, 0), state_job(0)]]
             if p == 5:
-                return row[:4] + [[state_job(1)]] + row[4:5] + [[piece_job(p, 0), state_job(2)]] + row[5:]
+                return row + [[state_job(1), piece_job(p, 0)], [state_job(2)]]
             if p == 6:
-                return row[:4] + [[state_job(3)]] + row[4:5] + [[piece_job(p, 0)]] + row[5:]
+                return row + [[state_job(3), piece_job(p, 0)]]
             if p == 7:
-                return row[:4] + [[state_job(4), piece_job(p, 0)]] + row[4:5] + [[piece_job(p, 1)]] + row[5:] + [[piece_job(p, 2)]]
-            return row + [[state_job(5)], [piece_job(p, 0)], [piece_job(p, 1)]]
+                return row + [[piece_job(p, 0), piece_job(p, 1)], [copy_job(p, 2)], [copy_job(p, 3)], [state_job(4)]]
+            return row + [[piece_job(p, 0)], [copy_job(p, 2)], [piece_job(p, 1)]]
 
         v_jobs = vector_jobs(0)
         s_jobs = [job for p in range(ROUNDS) for step in scalar_steps(p) for job in step if job[0] is not None]
@@ -446,13 +455,13 @@ def tile_latent_kv_state_s7_kernel(tc, c, wk, wv_bytes, wv_scale, keep, write, o
             refill(v_jobs, v_full, vector_bank, VECTOR_BANKS, most)
             refill(s_jobs, s_full, scalar_bank, SCALAR_BANKS)
 
-        def run(job, full):
+        def run(job, full, most=1):
             fill, empty, args, need = job
             if fill is None:
                 empty(*args)
             else:
                 empty(full.pop(0), *args)
-            refill_both(1)
+            refill_both(most)
 
         warm_up(4)
         for j in range(4):
@@ -492,11 +501,12 @@ def tile_latent_kv_state_s7_kernel(tc, c, wk, wv_bytes, wv_scale, keep, write, o
                 first = [(quantize_c, 1, 0), (quantize_c, 1, 1)]
             if r == 2:
                 first = [(quantize_c, g, b) for g in (2, 3) for b in range(2)]
-            if r in (3, 4, 5):
-                h = r + 2
-                first = [(quantize_weight, "wk", h), (quantize_weight, "wv", h)]
-                if r == 3:
-                    first.append((quantize_weight, "wk", 4))
+            if r == 3:
+                first = [(quantize_weight, "wk", 4), (quantize_weight, "wk", 5)]
+            if r == 4:
+                first = [(quantize_weight, "wv", 5), (quantize_weight, "wk", 6), (quantize_weight, "wk", 7)]
+            if r in (5, 6):
+                first = [(quantize_weight, "wv", r + 1)]
             mine = quantize_calls(r - 1, 0, own_words(r - 1), n, n + DIRECT[r - 1])
             if r == 1:
                 release = [(quantize_weight, "wk", 2), (quantize_weight, "wv", 2)]
@@ -515,57 +525,70 @@ def tile_latent_kv_state_s7_kernel(tc, c, wk, wv_bytes, wv_scale, keep, write, o
             step[0](*step[1:])
             refill_both(1)
 
-        def scalar_step(steps):
+        def scalar_step(steps, most=1):
             for job in steps.pop(0) if steps else []:
-                run(job, s_full)
+                run(job, s_full, most)
 
         for p in range(ROUNDS):
             steps = scalar_steps(p)
             if p == 0:
                 for job in widen_jobs(2):
                     run(job, s_full)
-                made.add(("turn", 1))
+                made.add(("turn", 1, 0))
                 refill_both()
                 pool_weights(0, [("wv", 2), ("wk", 2)])
             elif p == 1:
                 pool_weights(1, [("wv", 3), ("wk", 3), ("wv", 4)])
             else:
                 pool_values(p - 1)
+            if p == H:
+                early = vector_bank()
+                sum_state(early, H - 3)
             for i, job in enumerate(vector_jobs(p)):
-                if p == 0 and i == 3:
-                    made.add(("turn", 2))
                 run(job, v_full)
+                if p == 0 and i == 1:
+                    made.add(("turn", 1, 1))
+                if p == 0 and i == 3:
+                    made.add(("turn", 2, 0))
+                if p == 1 and i in (1, 3):
+                    made.add(("turn", 3, i // 2))
+                refill_both(0)
                 scalar_step(steps)
             if p == H:
                 break
             columns = 0
             v_jobs.extend(vector_jobs(p + 1))
+            refill_both(1)
             for step in quantize_run(p + 1):
-                call(step)
+                step[0](*step[1:])
                 columns = columns + width(step)
-                if columns >= 4 * 4 * P:
-                    columns = columns - 4 * 4 * P
-                    if p == 0:
-                        made.add(("turn", 3))
-                    scalar_step(steps)
+                if columns >= 3 * 4 * P:
+                    columns = columns - 3 * 4 * P
+                    refill_both(1)
+                    scalar_step(steps, 0)
+            refill_both()
             while steps:
                 scalar_step(steps)
+            if p == 0:
+                made.add(("turn", 2, 1))
+                refill_both()
 
         last = H - 1
         halves = [vector_bank(), vector_bank()]
         n = len(units(H))
-        for step in quantize_calls(H, 0, own_words(H), n, n + DIRECT[H]) + scalar_pieces(last):
+        for step in scalar_pieces(last):
             call(step)
         before_last = vector_bank()
         sum_state(before_last, last - 1)
-        call(quantize_calls(H, 0, own_words(H), 0, n)[0])
+        call(quantize_calls(H, 0, own_words(H), 0, n + DIRECT[H])[0])
         while steps:
             scalar_step(steps)
+        store_state(early, H - 3)
         store_state(before_last, last - 1)
-        for f in range(2):
+        for f in (0, 2, 1):
             quantize_pieces(H, n + DIRECT[H] + f, woven[H][:, f : f + 1, :, :])
         for g in range(G):
-            for f in range(2):
+            for f in (1, 0):
                 state_pass(halves[f][:, :P], last, g, f * P, (f + 1) * P)
         low = stage.tile([P, P], F32, name="result_half")
         nc.scalar.copy(out=low[:], in_=halves[0][:, :P])

@@ -21,8 +21,8 @@ WV_LOADS = ((0, 2), (2, 5), (5, H))
 WK_LOADS = ((0, 2), (2, 5), (5, H))
 VECTOR_BANKS, SCALAR_BANKS = 4, 4
 ROUNDS = H + 1
-DIRECT = (4, 3, 3, 2, 2, 2, 2, 2, 1)
-WOVEN = (0, 0, 0, 1, 1, 1, 1, 4, 3)
+DIRECT = (4, 3, 2, 2, 2, 2, 2, 2, 1)
+WOVEN = (0, 0, 1, 1, 1, 1, 1, 4, 3)
 
 
 def units(r):
@@ -115,8 +115,8 @@ def tile_latent_kv_state_s7_kernel(tc, c, wk, wv_bytes, wv_scale, keep, write, o
         load_c(1)
         load_wk(*WK_LOADS[1])
         load_c(2)
-        load_c(3)
         load_wv(*WV_LOADS[2])
+        load_c(3)
         load_wk(*WK_LOADS[2])
 
         nc.vector.memset(warm[:], 0.0)
@@ -158,7 +158,7 @@ def tile_latent_kv_state_s7_kernel(tc, c, wk, wv_bytes, wv_scale, keep, write, o
 
         def widen(h, j, on_vector=False):
             if h not in wv_wide:
-                wv_wide[h] = stage.tile([P, 4, DV], BF16, name="wv_wide", bufs=3, align_bytes=64)
+                wv_wide[h] = stage.tile([P, 4, DV], BF16, name="wv_wide", bufs=5, align_bytes=64)
             src = wv_row(h, j).bitcast(FP8)
             if on_vector:
                 nc.vector.tensor_scalar(out=wv_wide[h][:, j, :], in0=src, scalar1=row_scale[:, j : j + 1], scalar2=None, op0=ALU.mult)
@@ -358,7 +358,7 @@ def tile_latent_kv_state_s7_kernel(tc, c, wk, wv_bytes, wv_scale, keep, write, o
                 state_pass(bank[:, :DV], h, g, 0, DV)
 
         def store_state(bank, h):
-            result = stage.tile([P, DV], F32, name="result")
+            result = stage.tile([P, DV], F32, name="result", bufs=4)
             nc.scalar.copy(out=result[:], in_=bank[:, :DV])
             nc.sync.dma_start(out=out[h], in_=result[:])
 
@@ -421,19 +421,19 @@ def tile_latent_kv_state_s7_kernel(tc, c, wk, wv_bytes, wv_scale, keep, write, o
             row = [[job] for job in row_jobs(p)]
             wide = [[[job] for job in widen_jobs(h)] for h in range(H)]
             if p == 0:
-                return [[], wide[3][0], [turn_job(1, 0)], wide[3][1], [turn_job(1, 1)], [weight_job("wk", 4)], wide[4][0], [turn_job(2, 0)], wide[4][1]]
+                return wide[3] + wide[4][:1] + [[turn_job(1, 0)], wide[4][1], [turn_job(1, 1)], [weight_job("wk", 4)], wide[5][0], [turn_job(2, 0)]]
             if p == 1:
-                return wide[5][:1] + [[turn_job(2, 1)]] + wide[5][1:] + row[:1] + [[turn_job(3, 0)]] + row[1:2] + [[turn_job(3, 1)]] + row[2:] + [[weight_job("wk", 5)]]
+                return wide[5][1:] + wide[6][:1] + [[turn_job(2, 1)]] + row[:1] + wide[6][1:] + [[turn_job(3, 0)]] + row[1:2] + [[turn_job(3, 1)]] + row[2:] + [[weight_job("wk", 5)]]
             if p == 2:
-                return row + [[weight_job("wv", 5)], [weight_job("wk", 6), weight_job("wk", 7)]] + wide[6]
+                return row + [[weight_job("wv", 5)], [copy_job(p, 0)]]
             if p == 3:
-                return row + [[weight_job("wv", 6)], [piece_job(p, 0)]] + wide[7]
+                return row + [[weight_job("wv", 6)], [piece_job(p, 0), weight_job("wk", 6)]] + wide[7][:1]
             if p == 4:
-                return row + [[weight_job("wv", 7)], [piece_job(p, 0), state_job(0)]]
+                return row + [[weight_job("wk", 7), piece_job(p, 0)], [state_job(0)]] + wide[7][1:]
             if p == 5:
-                return row + [[state_job(1), piece_job(p, 0)], [state_job(2)]]
+                return row + [[weight_job("wv", 7)], [copy_job(p, 0)], [state_job(1)]]
             if p == 6:
-                return row + [[state_job(3), piece_job(p, 0)]]
+                return row + [[state_job(2), piece_job(p, 0)], [state_job(3)]]
             if p == 7:
                 return row + [[piece_job(p, 0), piece_job(p, 1)], [copy_job(p, 2)], [copy_job(p, 3)], [state_job(4)]]
             return row + [[piece_job(p, 0)], [copy_job(p, 2)], [piece_job(p, 1)]]
@@ -504,9 +504,13 @@ def tile_latent_kv_state_s7_kernel(tc, c, wk, wv_bytes, wv_scale, keep, write, o
             if r == 3:
                 first = [(quantize_weight, "wk", 4), (quantize_weight, "wk", 5)]
             if r == 4:
-                first = [(quantize_weight, "wv", 5), (quantize_weight, "wk", 6), (quantize_weight, "wk", 7)]
-            if r in (5, 6):
-                first = [(quantize_weight, "wv", r + 1)]
+                first = [(quantize_weight, "wv", 5)]
+            if r == 5:
+                first = [(quantize_weight, "wv", 6), (quantize_weight, "wk", 6)]
+            if r == 6:
+                first = [(quantize_weight, "wk", 7)]
+            if r == 7:
+                first = [(quantize_weight, "wv", 7)]
             mine = quantize_calls(r - 1, 0, own_words(r - 1), n, n + DIRECT[r - 1])
             if r == 1:
                 release = [(quantize_weight, "wk", 2), (quantize_weight, "wv", 2)]

@@ -22,7 +22,7 @@ WK_LOADS = ((0, 2), (2, 5), (5, H))
 VECTOR_BANKS, SCALAR_BANKS = 4, 4
 ROUNDS = H + 1
 DIRECT = (4, 3, 2, 2, 2, 2, 2, 2, 1)
-WOVEN = (0, 0, 1, 1, 1, 1, 1, 4, 3)
+WOVEN = (0, 0, 0, 0, 0, 0, 0, 4, 3)
 
 
 def units(r):
@@ -139,6 +139,8 @@ def tile_latent_kv_state_s7_kernel(tc, c, wk, wv_bytes, wv_scale, keep, write, o
             copy(out=dst.rearrange("p (c i) t -> p c t i", i=4), in_=src.rearrange("p t (c i) -> p c t i", i=4))
 
         def pool_interleave(dst, src):
+            dst = dst.rearrange("p (c i) t -> p c t i", i=4)
+            src = src.rearrange("p t (c i) -> p c t i", i=4)
             nc.gpsimd.tensor_scalar(out=dst, in0=src, scalar1=1.0, scalar2=0.0, op0=ALU.mult, op1=ALU.add)
 
         def quantize(cod, scl, src):
@@ -264,13 +266,16 @@ def tile_latent_kv_state_s7_kernel(tc, c, wk, wv_bytes, wv_scale, keep, write, o
 
         def scaled_rows(r):
             if r not in rows:
-                rows[r] = stage.tile([P, 2 * len(units(r)) - DIRECT[r], 4, P], BF16, name="rows", align_bytes=64)
+                rows[r] = stage.tile([P, 4, (2 * len(units(r)) - DIRECT[r]) * P], BF16, name="rows", align_bytes=64)
             return rows[r]
+
+        def piece_rows(r, i):
+            return scaled_rows(r)[:, :, i * P : (i + 1) * P]
 
         def half_out(bank, r, m):
             h, g = units(r)[m // 2]
             for t in range(4):
-                nc.scalar.activation(out=scaled_rows(r)[:, m - DIRECT[r], t, :], in_=bank[:, t * P : (t + 1) * P], func=COPY, scale=write_f[:, g, h, t : t + 1])
+                nc.scalar.activation(out=piece_rows(r, m - DIRECT[r])[:, t, :], in_=bank[:, t * P : (t + 1) * P], func=COPY, scale=write_f[:, g, h, t : t + 1])
             made.add(("rows", r, m))
 
         def rows_out(bank, r, u, b):
@@ -278,14 +283,13 @@ def tile_latent_kv_state_s7_kernel(tc, c, wk, wv_bytes, wv_scale, keep, write, o
             first = 2 * u - DIRECT[r]
             for i in range(2):
                 t = 2 * b + i
-                src = bank[:, i * DV : (i + 1) * DV].rearrange("p (m n) -> p m n", m=2)
-                nc.scalar.activation(out=scaled_rows(r)[:, first : first + 2, t, :], in_=src, func=COPY, scale=write_f[:, g, h, t : t + 1])
+                nc.scalar.activation(out=scaled_rows(r)[:, t, first * P : (first + 2) * P], in_=bank[:, i * DV : (i + 1) * DV], func=COPY, scale=write_f[:, g, h, t : t + 1])
             if b == 1:
                 made.add(("rows", r, 2 * u))
                 made.add(("rows", r, 2 * u + 1))
 
         def weave_piece(bank, r, i):
-            weave(as_words(bank, P), scaled_rows(r)[:, i, :, :])
+            weave(as_words(bank, P), piece_rows(r, i))
 
         def woven_words(r):
             if r not in woven:
@@ -312,12 +316,12 @@ def tile_latent_kv_state_s7_kernel(tc, c, wk, wv_bytes, wv_scale, keep, write, o
             for kind, h in jobs:
                 n = 2 if kind == "wv" else 1
                 words[kind, h] = pooled[w][:, at : at + n, :, :].rearrange("p m n j -> p (m n) j")
-                pool_interleave(words[kind, h], weight_rows(kind, h).rearrange("p j n -> p n j"))
+                pool_interleave(words[kind, h], weight_rows(kind, h))
                 at = at + n
 
         def pool_values(r):
             pool_tile(r + 1, 2 * len(units(r)) - DIRECT[r] - WOVEN[r])
-            pool_interleave(pooled[r + 1][:], scaled_rows(r)[:, WOVEN[r] :, :, :].rearrange("p m t n -> p m n t"))
+            pool_interleave(pooled[r + 1][:].rearrange("p m n t -> p (m n) t"), scaled_rows(r)[:, :, WOVEN[r] * P :])
 
         cod, scl = {}, {}
         for r in range(ROUNDS):
@@ -393,7 +397,7 @@ def tile_latent_kv_state_s7_kernel(tc, c, wk, wv_bytes, wv_scale, keep, write, o
             return (weave_piece, woven_piece_out, (r, i), [("rows", r, DIRECT[r] + i)])
 
         def copy_piece(r, i):
-            interleave(nc.scalar.copy, woven_words(r)[:, i, :, :], scaled_rows(r)[:, i, :, :])
+            interleave(nc.scalar.copy, woven_words(r)[:, i, :, :], piece_rows(r, i))
 
         def copy_job(r, i):
             return (None, copy_piece, (r, i), [])
@@ -425,15 +429,15 @@ def tile_latent_kv_state_s7_kernel(tc, c, wk, wv_bytes, wv_scale, keep, write, o
             if p == 1:
                 return wide[5][1:] + wide[6][:1] + [[turn_job(2, 1)]] + row[:1] + wide[6][1:] + [[turn_job(3, 0)]] + row[1:2] + [[turn_job(3, 1)]] + row[2:] + [[weight_job("wk", 5)]]
             if p == 2:
-                return row + [[weight_job("wv", 5)], [copy_job(p, 0)]]
+                return row + [[weight_job("wv", 5)]]
             if p == 3:
-                return row + [[weight_job("wv", 6)], [piece_job(p, 0), weight_job("wk", 6)]] + wide[7][:1]
+                return row + [[weight_job("wv", 6)], [weight_job("wk", 6)]] + wide[7][:1]
             if p == 4:
-                return row + [[weight_job("wk", 7), piece_job(p, 0)], [state_job(0)]] + wide[7][1:]
+                return row + [[weight_job("wk", 7)], [state_job(0)]] + wide[7][1:]
             if p == 5:
-                return row + [[weight_job("wv", 7)], [copy_job(p, 0)], [state_job(1)]]
+                return row + [[weight_job("wv", 7)], [state_job(1)]]
             if p == 6:
-                return row + [[state_job(2), piece_job(p, 0)], [state_job(3)]]
+                return row + [[state_job(2)], [state_job(3)]]
             if p == 7:
                 return row + [[piece_job(p, 0), piece_job(p, 1)], [copy_job(p, 2)], [copy_job(p, 3)], [state_job(4)]]
             return row + [[piece_job(p, 0)], [copy_job(p, 2)], [piece_job(p, 1)]]

@@ -21,8 +21,8 @@ WV_LOADS = ((0, 2), (2, 5), (5, H))
 WK_LOADS = ((0, 2), (2, 5), (5, H))
 VECTOR_BANKS, SCALAR_BANKS = 4, 4
 ROUNDS = H + 1
-DIRECT = (4, 3, 2, 2, 2, 2, 2, 2, 1)
-WOVEN = (0, 0, 0, 0, 0, 0, 0, 4, 3)
+DIRECT = (4, 2, 2, 2, 2, 2, 1, 2, 1)
+WOVEN = (0, 0, 0, 0, 0, 1, 1, 3, 3)
 
 
 def units(r):
@@ -31,7 +31,7 @@ def units(r):
     if r == 1:
         return [(0, 1), (1, 1), (2, 0), (2, 1)]
     if r == 2:
-        return [(0, 2), (0, 3), (1, 2), (1, 3)]
+        return [(0, 2), (1, 2), (0, 3), (1, 3)]
     return [(r - 1, 2), (r - 1, 3), (r, 0), (r, 1)][: 2 if r == H else 4]
 
 
@@ -427,19 +427,19 @@ def tile_latent_kv_state_s7_kernel(tc, c, wk, wv_bytes, wv_scale, keep, write, o
             if p == 0:
                 return wide[3] + wide[4][:1] + [[turn_job(1, 0)], wide[4][1], [turn_job(1, 1)], [weight_job("wk", 4)], wide[5][0], [turn_job(2, 0)]]
             if p == 1:
-                return wide[5][1:] + wide[6][:1] + [[turn_job(2, 1)]] + row[:1] + wide[6][1:] + [[turn_job(3, 0)]] + row[1:2] + [[turn_job(3, 1)]] + row[2:] + [[weight_job("wk", 5)]]
+                return wide[5][1:] + row[:2] + [[turn_job(2, 1)]] + row[2:3] + [[turn_job(3, 0)]] + row[3:4] + [[turn_job(3, 1)]] + row[4:]
             if p == 2:
-                return row + [[weight_job("wv", 5)]]
+                return row + [[weight_job("wv", 5)], [weight_job("wk", 6)]] + wide[6]
             if p == 3:
-                return row + [[weight_job("wv", 6)], [weight_job("wk", 6)]] + wide[7][:1]
+                return row + [[weight_job("wv", 6)], [weight_job("wk", 7)]] + wide[7]
             if p == 4:
-                return row + [[weight_job("wk", 7)], [state_job(0)]] + wide[7][1:]
+                return row + [[weight_job("wv", 7)], [state_job(0)]]
             if p == 5:
-                return row + [[weight_job("wv", 7)], [state_job(1)]]
+                return row + [[piece_job(p, 0), state_job(1)], [state_job(2)]]
             if p == 6:
-                return row + [[state_job(2)], [state_job(3)]]
+                return row + [[piece_job(p, 0), state_job(3)]]
             if p == 7:
-                return row + [[piece_job(p, 0), piece_job(p, 1)], [copy_job(p, 2)], [copy_job(p, 3)], [state_job(4)]]
+                return row + [[piece_job(p, 0), piece_job(p, 1)], [copy_job(p, 2)], [state_job(4)]]
             return row + [[piece_job(p, 0)], [copy_job(p, 2)], [piece_job(p, 1)]]
 
         v_jobs = vector_jobs(0)
@@ -504,22 +504,20 @@ def tile_latent_kv_state_s7_kernel(tc, c, wk, wv_bytes, wv_scale, keep, write, o
             if r == 1:
                 first = [(quantize_c, 1, 0), (quantize_c, 1, 1)]
             if r == 2:
-                first = [(quantize_c, g, b) for g in (2, 3) for b in range(2)]
+                first = [(quantize_c, 2, 0), (quantize_c, 2, 1)]
             if r == 3:
-                first = [(quantize_weight, "wk", 4), (quantize_weight, "wk", 5)]
+                first = [(quantize_weight, "wk", 4)]
             if r == 4:
-                first = [(quantize_weight, "wv", 5)]
+                first = [(quantize_weight, "wv", 5), (quantize_weight, "wk", 6)]
             if r == 5:
-                first = [(quantize_weight, "wv", 6), (quantize_weight, "wk", 6)]
+                first = [(quantize_weight, "wv", 6), (quantize_weight, "wk", 7)]
             if r == 6:
-                first = [(quantize_weight, "wk", 7)]
-            if r == 7:
                 first = [(quantize_weight, "wv", 7)]
             mine = quantize_calls(r - 1, 0, own_words(r - 1), n, n + DIRECT[r - 1])
             if r == 1:
-                release = [(quantize_weight, "wk", 2), (quantize_weight, "wv", 2)]
+                release = [(quantize_weight, "wk", 2), (quantize_weight, "wv", 2), (quantize_weight, "wk", 3)]
             elif r == 2:
-                release = [(quantize_weight, "wk", 3), (quantize_weight, "wv", 3), (quantize_weight, "wv", 4)]
+                release = [(quantize_weight, "wv", 3), (quantize_c, 3, 0), (quantize_weight, "wv", 4), (quantize_c, 3, 1), (quantize_weight, "wk", 5)]
             else:
                 release = scalar_pieces(r - 2)
             return first + mine + release + quantize_calls(r - 1, 0, own_words(r - 1), 0, n)
@@ -544,9 +542,9 @@ def tile_latent_kv_state_s7_kernel(tc, c, wk, wv_bytes, wv_scale, keep, write, o
                     run(job, s_full)
                 made.add(("turn", 1, 0))
                 refill_both()
-                pool_weights(0, [("wv", 2), ("wk", 2)])
+                pool_weights(0, [("wv", 2), ("wk", 2), ("wk", 3)])
             elif p == 1:
-                pool_weights(1, [("wv", 3), ("wk", 3), ("wv", 4)])
+                pool_weights(1, [("wv", 3), ("wv", 4), ("wk", 5)])
             else:
                 pool_values(p - 1)
             if p == H:
@@ -558,8 +556,8 @@ def tile_latent_kv_state_s7_kernel(tc, c, wk, wv_bytes, wv_scale, keep, write, o
                     made.add(("turn", 1, 1))
                 if p == 0 and i == 3:
                     made.add(("turn", 2, 0))
-                if p == 1 and i in (1, 3):
-                    made.add(("turn", 3, i // 2))
+                if p == 1 and i in (2, 4):
+                    made.add(("turn", 3, i // 2 - 1))
                 refill_both(0)
                 scalar_step(steps)
             if p == H:

@@ -17,12 +17,12 @@ P = 128
 G = 4
 FLOPS = 2 * T * L * H * (DK + DV) + 2 * T * H * DK * DV
 
-WV_LOADS = ((0, 2), (2, 5), (5, H))
+WV_LOADS = ((0, 2), (2, 6), (6, H))
 WK_LOADS = ((0, 2), (2, 5), (5, H))
 VECTOR_BANKS, SCALAR_BANKS = 4, 4
 ROUNDS = H + 1
-DIRECT = (4, 2, 2, 2, 2, 2, 1, 2, 1)
-WOVEN = (0, 0, 0, 0, 0, 1, 1, 3, 3)
+DIRECT = (4, 2, 2, 2, 1, 2, 1, 2, 1)
+WOVEN = (0, 0, 0, 1, 1, 1, 1, 3, 3)
 
 
 def units(r):
@@ -108,11 +108,11 @@ def tile_latent_kv_state_s7_kernel(tc, c, wk, wv_bytes, wv_scale, keep, write, o
         load_wv(*WV_LOADS[0])
         load_c_half(0)
         load_c_half(1)
-        load_wk(*WK_LOADS[0])
         load_wv(*WV_LOADS[1])
-        nc.sync.dma_start(out=keep_raw[:], in_=keep.rearrange("(g p t) h -> p g (t h)", p=P, t=4))
+        load_wk(*WK_LOADS[0])
         nc.sync.dma_start(out=write_raw[:], in_=write.rearrange("(g p t) h -> p g (t h)", p=P, t=4))
         load_c(1)
+        nc.sync.dma_start(out=keep_raw[:], in_=keep.rearrange("(g p t) h -> p g (t h)", p=P, t=4))
         load_wk(*WK_LOADS[1])
         load_c(2)
         load_wv(*WV_LOADS[2])
@@ -148,7 +148,7 @@ def tile_latent_kv_state_s7_kernel(tc, c, wk, wv_bytes, wv_scale, keep, write, o
 
         def weave(dst, rows):
             for j in (0, 2):
-                nc.tensor.matmul(out=dst.rearrange("p n j -> p j n")[:, j : j + 2, :], lhsT=ident_bf[:], rhs=rows[:, j : j + 2, :], start=True, stop=True)
+                nc.tensor.matmul(out=dst[:, :, j : j + 2], lhsT=ident_bf[:], rhs=rows[:, j : j + 2, :].rearrange("p j n -> p n j"), start=True, stop=True)
 
         def as_words(bank, n):
             return bank[:].bitcast(BF16)[:, : 4 * n].rearrange("p (n j) -> p n j", j=4)
@@ -195,7 +195,7 @@ def tile_latent_kv_state_s7_kernel(tc, c, wk, wv_bytes, wv_scale, keep, write, o
                     col = (2 * i + u) * P
                     nc.tensor.transpose(bank[:, col : col + P], rows[:, i, u::2], ident[:])
 
-        def turned_c_out(bank, g, b, copy, name="c_words", bufs=4):
+        def turned_c_out(bank, g, b, copy, name="c_words", bufs=2 * G):
             tile = stage.tile([P, 2, P, 4], BF16, name=name, bufs=bufs, align_bytes=64)
             copy(out=tile[:].bitcast(F32), in_=bank[:].rearrange("q (i u p) -> q i p u", i=2, u=2))
             words["c", g, b] = tile[:]
@@ -206,7 +206,6 @@ def tile_latent_kv_state_s7_kernel(tc, c, wk, wv_bytes, wv_scale, keep, write, o
             quantised.add(("c", g, b))
 
         def widen_factors():
-            nc.vector.tensor_copy(out=keep_f[:], in_=keep_raw[:].rearrange("p g (t h) -> p g h t", t=4))
             nc.vector.tensor_copy(out=write_f[:], in_=write_raw[:].rearrange("p g (t h) -> p g h t", t=4))
 
         def project(dst, g, t, cod, scl):
@@ -266,7 +265,7 @@ def tile_latent_kv_state_s7_kernel(tc, c, wk, wv_bytes, wv_scale, keep, write, o
 
         def scaled_rows(r):
             if r not in rows:
-                rows[r] = stage.tile([P, 4, (2 * len(units(r)) - DIRECT[r]) * P], BF16, name="rows", align_bytes=64)
+                rows[r] = stage.tile([P, 4, (2 * len(units(r)) - DIRECT[r]) * P], BF16, name="rows", bufs=3, align_bytes=64)
             return rows[r]
 
         def piece_rows(r, i):
@@ -316,6 +315,8 @@ def tile_latent_kv_state_s7_kernel(tc, c, wk, wv_bytes, wv_scale, keep, write, o
             for kind, h in jobs:
                 n = 2 if kind == "wv" else 1
                 words[kind, h] = pooled[w][:, at : at + n, :, :].rearrange("p m n j -> p (m n) j")
+                if (kind, h) == ("wk", 2):
+                    nc.gpsimd.tensor_scalar(out=keep_f[:], in0=keep_raw[:].rearrange("p g (t h) -> p g h t", t=4), scalar1=1.0, scalar2=0.0, op0=ALU.mult, op1=ALU.add)
                 pool_interleave(words[kind, h], weight_rows(kind, h))
                 at = at + n
 
@@ -357,13 +358,13 @@ def tile_latent_kv_state_s7_kernel(tc, c, wk, wv_bytes, wv_scale, keep, write, o
                 stop=(g == G - 1),
             )
 
-        def sum_state(bank, h):
+        def sum_state(bank, h, at=0):
             for g in range(G):
-                state_pass(bank[:, :DV], h, g, 0, DV)
+                state_pass(bank[:, at : at + DV], h, g, 0, DV)
 
-        def store_state(bank, h):
-            result = stage.tile([P, DV], F32, name="result", bufs=4)
-            nc.scalar.copy(out=result[:], in_=bank[:, :DV])
+        def store_state(bank, h, at=0):
+            result = stage.tile([P, DV], F32, name="result", bufs=H - 1)
+            nc.scalar.copy(out=result[:], in_=bank[:, at : at + DV])
             nc.sync.dma_start(out=out[h], in_=result[:])
 
         def head_pieces(h):
@@ -382,7 +383,7 @@ def tile_latent_kv_state_s7_kernel(tc, c, wk, wv_bytes, wv_scale, keep, write, o
             keys = [(project_keys, keys_out, (r, u), unit_operands("wk", r, u)) for u in range(len(units(r)))]
             pieces = [(project_piece, piece_out, (r, m), unit_operands("wv", r, m // 2)) for m in range(DIRECT[r])]
             if r == 0:
-                return keys[:1] + pieces[:2] + keys[1:] + pieces[2:]
+                return pieces + keys
             return keys[:2] + pieces + keys[2:]
 
         def row_jobs(r):
@@ -425,21 +426,21 @@ def tile_latent_kv_state_s7_kernel(tc, c, wk, wv_bytes, wv_scale, keep, write, o
             row = [[job] for job in row_jobs(p)]
             wide = [[[job] for job in widen_jobs(h)] for h in range(H)]
             if p == 0:
-                return wide[3] + wide[4][:1] + [[turn_job(1, 0)], wide[4][1], [turn_job(1, 1)], [weight_job("wk", 4)], wide[5][0], [turn_job(2, 0)]]
+                return [wide[3][0] + wide[3][1]] + wide[4] + [[turn_job(1, 0)], wide[5][0], [turn_job(1, 1)], [weight_job("wk", 4)], wide[5][1], [turn_job(2, 0)]]
             if p == 1:
-                return wide[5][1:] + row[:2] + [[turn_job(2, 1)]] + row[2:3] + [[turn_job(3, 0)]] + row[3:4] + [[turn_job(3, 1)]] + row[4:]
+                return wide[6][:1] + row[:2] + [[turn_job(2, 1)]] + row[2:3] + [wide[6][1] + [turn_job(3, 0)]] + row[3:4] + [[turn_job(3, 1)]] + row[4:]
             if p == 2:
-                return row + [[weight_job("wv", 5)], [weight_job("wk", 6)]] + wide[6]
+                return row + [[weight_job("wv", 5)], [weight_job("wk", 6)]] + wide[7]
             if p == 3:
-                return row + [[weight_job("wv", 6)], [weight_job("wk", 7)]] + wide[7]
+                return row + [[weight_job("wv", 6)], [weight_job("wk", 7)], [copy_job(p, 0)]]
             if p == 4:
-                return row + [[weight_job("wv", 7)], [state_job(0)]]
+                return row + [[weight_job("wv", 7)], [piece_job(p, 0)]]
             if p == 5:
-                return row + [[piece_job(p, 0), state_job(1)], [state_job(2)]]
+                return row + [[piece_job(p, 0), state_job(0)], [state_job(1)]]
             if p == 6:
-                return row + [[piece_job(p, 0), state_job(3)]]
+                return row + [[piece_job(p, 0), state_job(2)]]
             if p == 7:
-                return row + [[piece_job(p, 0), piece_job(p, 1)], [copy_job(p, 2)], [state_job(4)]]
+                return row + [[piece_job(p, 0), piece_job(p, 1)], [copy_job(p, 2)], [state_job(3)]]
             return row + [[piece_job(p, 0)], [copy_job(p, 2)], [piece_job(p, 1)]]
 
         v_jobs = vector_jobs(0)
@@ -482,15 +483,15 @@ def tile_latent_kv_state_s7_kernel(tc, c, wk, wv_bytes, wv_scale, keep, write, o
         vector_interleave("wv", 1)
         quantize_weight("wv", 0)
         quantize_c(0, 0)
-        vector_interleave("wk", 0)
+        quantize_weight("wv", 1)
         quantize_c(0, 1)
-        quantize_weight("wk", 0)
         refill_both()
+        vector_interleave("wk", 0)
         words["wk", 1] = stage.tile([P, DK, 4], BF16, name="pool_out", bufs=1, align_bytes=64)[:]
         interleave(nc.vector.tensor_copy, words["wk", 1], wk_rows(1))
+        quantize_weight("wk", 0)
         widen_factors()
         quantize_weight("wk", 1)
-        quantize_weight("wv", 1)
         refill_both()
 
         def scalar_pieces(r):
@@ -549,7 +550,7 @@ def tile_latent_kv_state_s7_kernel(tc, c, wk, wv_bytes, wv_scale, keep, write, o
                 pool_values(p - 1)
             if p == H:
                 early = vector_bank()
-                sum_state(early, H - 3)
+                sum_state(early, H - 4, DV)
             for i, job in enumerate(vector_jobs(p)):
                 run(job, v_full)
                 if p == 0 and i == 1:
@@ -580,6 +581,7 @@ def tile_latent_kv_state_s7_kernel(tc, c, wk, wv_bytes, wv_scale, keep, write, o
                 refill_both()
 
         last = H - 1
+        sum_state(early, H - 3)
         halves = [vector_bank(), vector_bank()]
         n = len(units(H))
         for step in scalar_pieces(last):
@@ -589,6 +591,7 @@ def tile_latent_kv_state_s7_kernel(tc, c, wk, wv_bytes, wv_scale, keep, write, o
         call(quantize_calls(H, 0, own_words(H), 0, n + DIRECT[H])[0])
         while steps:
             scalar_step(steps)
+        store_state(early, H - 4, DV)
         store_state(early, H - 3)
         store_state(before_last, last - 1)
         for f in (0, 2, 1):

@@ -148,7 +148,7 @@ def tile_latent_kv_state_s7_kernel(tc, c, wk, wv_bytes, wv_scale, keep, write, o
 
         def weave(dst, rows):
             for j in (0, 2):
-                nc.tensor.matmul(out=dst[:, :, j : j + 2], lhsT=ident_bf[:], rhs=rows[:, j : j + 2, :].rearrange("p j n -> p n j"), start=True, stop=True)
+                nc.tensor.matmul(out=dst.rearrange("p n j -> p j n")[:, j : j + 2, :], lhsT=ident_bf[:], rhs=rows[:, j : j + 2, :], start=True, stop=True)
 
         def as_words(bank, n):
             return bank[:].bitcast(BF16)[:, : 4 * n].rearrange("p (n j) -> p n j", j=4)

@@ -16,33 +16,107 @@ T, L, H, DK, DV = 2048, 512, 8, 128, 256
 P = 128
 G = 4
 FLOPS = 2 * T * L * H * (DK + DV) + 2 * T * H * DK * DV
-
-WV_LOADS = ((0, 2), (2, 6), (6, H))
-WK_LOADS = ((0, 2), (2, 5), (5, H))
 VECTOR_BANKS, SCALAR_BANKS = 4, 4
-ROUNDS = H + 1
-DIRECT = (4, 2, 2, 2, 1, 2, 1, 2, 1)
-WOVEN = (0, 0, 0, 1, 1, 1, 1, 3, 3)
 
 
-def units(r):
-    if r == 0:
-        return [(0, 0), (1, 0)]
-    if r == 1:
-        return [(0, 1), (1, 1), (2, 0), (2, 1)]
-    if r == 2:
-        return [(0, 2), (1, 2), (0, 3), (1, 3)]
-    return [(r - 1, 2), (r - 1, 3), (r, 0), (r, 1)][: 2 if r == H else 4]
+def keys(*units):
+    return [("k", h, g) for h, g in units]
 
 
-def place(h, g):
-    for r in range(ROUNDS):
-        if (h, g) in units(r):
-            return r, units(r).index((h, g))
+def values(*units):
+    return [("v", h, g, f) for h, g in units for f in range(2)]
+
+
+WV_LOADS = ((0, 2), (2, 4), (4, 6), (6, H))
+ROUNDS = 7
+WINDOW = [
+    values((0, 0), (1, 0)) + keys((0, 0), (1, 0)),
+    keys((2, 0), (3, 0), (0, 1), (1, 1)) + values((0, 1)) + keys((2, 1), (3, 1)),
+    keys((0, 2), (1, 2)) + values((0, 2), (0, 3)) + keys((0, 3), (1, 3)),
+    keys((2, 2), (2, 3), (3, 2), (3, 3)) + values((3, 2)) + keys((4, 0), (4, 1)),
+    keys((4, 2), (4, 3), (5, 0), (5, 1)) + values((4, 3)) + keys((5, 2), (5, 3)),
+    keys((6, 0), (6, 1), (6, 2), (6, 3)) + values((6, 1), (6, 2)),
+    keys((7, 0), (7, 1), (7, 2), (7, 3)),
+]
+ROWS = [
+    [],
+    [(1, 1), (2, 0), (2, 1), (3, 0)],
+    [(1, 2), (1, 3), (3, 1), (2, 2), (2, 3)],
+    [(3, 3), (4, 0), (4, 1), (4, 2)],
+    [(5, 0), (5, 1), (5, 2), (5, 3), (6, 0)],
+    [(7, 0), (7, 1), (6, 3), (7, 2)],
+    [(7, 3)],
+]
+ROW_BUFS = 3
+POOL = [
+    [("wk", 2), ("wk", 3), ("wv", 2, 0), ("wv", 2, 1)],
+    [("wv", h, f) for h in (4, 5) for f in range(2)] + [("wk", h) for h in range(4, H)],
+] + [values(*ROWS[r - 1])[: len(WINDOW[r])] for r in range(2, ROUNDS)]
+SCALAR_WORDS = [
+    [("wv", 3, 0), ("wv", 3, 1)] + [("c", 1, t) for t in range(4)],
+    [("c", g, t) for g in (2, 3) for t in range(4)],
+    [],
+    [("wv", 6, 0), ("wv", 6, 1)] + values((2, 3)),
+    [("wv", 7, 0), ("wv", 7, 1)],
+    values((6, 0)),
+    values((6, 3), (7, 2), (7, 3)),
+]
+PACE = 4
+LEAD = 4
+
+
+def row_steps(p):
+    return [("rows", h, g, b) for h, g in ROWS[p] for b in range(2)]
+
+
+def woven(*pieces):
+    return [("weave", piece, 1) for piece in pieces]
+
+
+def pair(h, g):
+    return [("weave", ("v", h, g, 0), 1), ("copy", ("v", h, g, 1))]
+
+
+def insert(steps, at, *extra):
+    return steps[:at] + list(extra) + steps[at:]
+
+
+SCALAR = (
+    [("widen", h, 1, j) for h in (2, 3) for j in range(4)]
+    + [("keep",), ("widen", 4, 2, 0), ("weave", ("wv", 3, 0), 2), ("allow", "turn", 1, 0), ("allow", "turn", 1, 1), ("widen", 4, 2, 1)]
+    + [("turn", 1, 0), ("allow", "turn", 2, 0), ("allow", "turn", 2, 1), ("turn", 1, 1), ("widen", 4, 2, 2), ("widen", 4, 2, 3)]
+    + [("turn", 2, 0), ("allow", "turn", 3, 0), ("allow", "turn", 3, 1), ("turn", 2, 1), ("widen", 6, 1, 0), ("widen", 6, 1, 1)]
+    + [("turn", 3, 0), ("allow", "rows"), ("turn", 3, 1), ("widen", 6, 1, 2)]
+    + row_steps(1)
+    + insert(insert(row_steps(2), 8, ("weave", ("wv", 6, 0), 2)), 0, ("widen", 6, 1, 3))
+    + insert(row_steps(3), 6, *woven(*values((2, 3))))
+    + [("widen", 7, 1, j) for j in range(4)]
+    + [("state", 0)]
+    + insert(insert(row_steps(4), 8, ("state", 1), ("state", 2)), 6, ("weave", ("wv", 7, 0), 2))
+    + insert(insert(row_steps(5), 6, ("state", 3)), 4, *woven(*values((6, 0))))
+    + pair(6, 3)
+    + row_steps(6)
+    + pair(7, 2)
+    + [("state", 4)]
+    + pair(7, 3)
+)
+HEAD_START = 60
+
+
+def span(step):
+    if step[0] == "widen":
+        return 8 * step[2] + 1
+    if step[0] == "weave":
+        return 8 * step[2]
+    return {"rows": 18, "turn": 16, "copy": 16, "state": 8, "keep": 4, "allow": 0}[step[0]]
 
 
 def widths(n):
-    return [n] if n <= 4 else [4, n - 4] if n != 6 else [3, 3]
+    if n in (8, 4, 3, 2, 1, 0):
+        return [n] if n else []
+    if n == 6:
+        return [3, 3]
+    return [8] + widths(n - 8) if n > 8 else [4] + widths(n - 4)
 
 
 def tile_latent_kv_state_s7_kernel(tc, c, wk, wv_bytes, wv_scale, keep, write, out):
@@ -56,36 +130,24 @@ def tile_latent_kv_state_s7_kernel(tc, c, wk, wv_bytes, wv_scale, keep, write, o
         ident_bf = const.tile([P, P], BF16, name="ident_bf")
         row_scale = const.tile([P, 4], F32, name="row_scale")
         warm = const.tile([P, 1], F32, name="warm")
-        keep_raw = const.tile([P, G, 4 * H], BF16, name="keep_raw")
-        write_raw = const.tile([P, G, 4 * H], BF16, name="write_raw")
-        keep_f = const.tile([P, G, H, 4], F32, name="keep_f")
-        write_f = const.tile([P, G, H, 4], F32, name="write_f")
-        c_cod = const.tile([P, G, 4 * P], U32, name="c_cod", align_bytes=64)
-        c_scl = const.tile([P, G, 4 * P], U8, name="c_scl", align_bytes=64)
-        wk_cod = const.tile([P, H, DK], U32, name="wk_cod", align_bytes=64)
-        wk_scl = const.tile([P, H, DK], U8, name="wk_scl", align_bytes=64)
-        wv_cod = const.tile([P, H, DV], U32, name="wv_cod", align_bytes=64)
-        wv_scl = const.tile([P, H, DV], U8, name="wv_scl", align_bytes=64)
+        factor_raw = const.tile([P, 2, G, 4 * H], BF16, name="factor_raw")
+        factor = const.tile([P, 2, G, H, 4], F32, name="factor")
+        c_half = [const.tile([P, 2, L], BF16, name="c_half%d" % b, align_bytes=64) for b in range(2)]
+        c_group = {g: const.tile([P, 4 * L], BF16, name="c_group%d" % g, align_bytes=64) for g in range(1, G)}
+        wv_load = {first: const.tile([P, 4, (end - first) * DV], U8, name="wv_load%d" % first, align_bytes=64) for first, end in WV_LOADS}
+        early = const.tile([P, 4, 4 * DK + 2 * DV], BF16, name="early", align_bytes=64)
+        late = const.tile([P, 4, 2 * DV + 4 * DK], BF16, name="late", align_bytes=64)
+        wv_first = [const.tile([P, 4, DV], BF16, name="wv_first%d" % h, align_bytes=64) for h in range(2)]
+        wv_last = const.tile([P, 4, 2 * DV], BF16, name="wv_last", align_bytes=64)
 
-        c_rows = {}
-        for b in range(2):
-            c_rows[0, b] = const.tile([P, 2, L], BF16, name="c_rows0%d" % b, align_bytes=64)
-        c_group = {}
-        for g in range(1, G):
-            c_group[g] = const.tile([P, 4 * L], BF16, name="c_group%d" % g, align_bytes=64)
-        wk_load, wv_load = {}, {}
-        for first, end in WV_LOADS:
-            wv_load[first] = const.tile([P, 4, (end - first) * DV], U8, name="wv_load%d" % first, align_bytes=64)
-        for first, end in WK_LOADS:
-            wk_load[first] = const.tile([P, 4, (end - first) * DK], BF16, name="wk_load%d" % first, align_bytes=64)
-
-        def wk_rows(h):
-            first = max(f for f, e in WK_LOADS if f <= h)
-            return wk_load[first][:, :, (h - first) * DK : (h - first + 1) * DK]
-
-        def wv_row(h, j):
-            first = max(f for f, e in WV_LOADS if f <= h)
-            return wv_load[first][:, j, (h - first) * DV : (h - first + 1) * DV]
+        def weight_rows(kind, h, n=1):
+            if kind == "wk":
+                return early[:, :, h * DK : (h + n) * DK] if h < 4 else late[:, :, 2 * DV + (h - 4) * DK : 2 * DV + (h - 4 + n) * DK]
+            if h < 2:
+                return wv_first[h][:]
+            if h < 4:
+                return early[:, :, 4 * DK + (h - 2) * DV : 4 * DK + (h - 2 + n) * DV]
+            return late[:, :, (h - 4) * DV : (h - 4 + n) * DV] if h < 6 else wv_last[:, :, (h - 6) * DV : (h - 6 + n) * DV]
 
         ctx.enter_context(tc.manual_schedule())
 
@@ -96,28 +158,31 @@ def tile_latent_kv_state_s7_kernel(tc, c, wk, wv_bytes, wv_scale, keep, write, o
             nc.sync.dma_start(out=c_group[g][:], in_=c.rearrange("(g p t) l -> g p (t l)", p=P, t=4)[g])
 
         def load_c_half(b):
-            nc.sync.dma_start(out=c_rows[0, b][:], in_=c.rearrange("(g p b i) l -> g b p i l", p=P, b=2, i=2)[0, b])
+            nc.sync.dma_start(out=c_half[b][:], in_=c.rearrange("(g p b i) l -> g b p i l", p=P, b=2, i=2)[0, b])
 
         def load_wv(first, end):
             nc.sync.dma_start(out=wv_load[first][:], in_=wv_view[:, :, first * DV : end * DV])
 
         def load_wk(first, end):
-            nc.sync.dma_start(out=wk_load[first][:], in_=wk_view[:, :, first * DK : end * DK])
+            nc.sync.dma_start(out=weight_rows("wk", first, end - first), in_=wk_view[:, :, first * DK : end * DK])
+
+        def load_factor(i, src):
+            nc.sync.dma_start(out=factor_raw[:, i, :, :], in_=src.rearrange("(g p t) h -> p g (t h)", p=P, t=4))
 
         nc.scalar.dma_start(out=row_scale[:], in_=wv_scale.rearrange("(q j) o -> q (j o)", j=4))
         load_wv(*WV_LOADS[0])
         load_c_half(0)
         load_c_half(1)
         load_wv(*WV_LOADS[1])
-        load_wk(*WK_LOADS[0])
-        nc.sync.dma_start(out=write_raw[:], in_=write.rearrange("(g p t) h -> p g (t h)", p=P, t=4))
-        load_c(1)
-        nc.sync.dma_start(out=keep_raw[:], in_=keep.rearrange("(g p t) h -> p g (t h)", p=P, t=4))
-        load_wk(*WK_LOADS[1])
-        load_c(2)
+        load_wk(0, 4)
+        load_factor(1, write)
+        load_factor(0, keep)
         load_wv(*WV_LOADS[2])
+        load_c(1)
+        load_c(2)
+        load_wk(4, H)
         load_c(3)
-        load_wk(*WK_LOADS[2])
+        load_wv(*WV_LOADS[3])
 
         nc.vector.memset(warm[:], 0.0)
         nc.scalar.activation(out=warm[:], in_=warm[:], func=COPY)
@@ -135,470 +200,328 @@ def tile_latent_kv_state_s7_kernel(tc, c, wk, wv_bytes, wv_scale, keep, write, o
             for i in range(count):
                 nc.tensor.matmul(out=bank[:, i * P : (i + 1) * P], lhsT=ident[:], rhs=ident[:], start=True, stop=True)
 
+        def walk(dst, src):
+            return dst.rearrange("p (c i) t -> p c t i", i=4), src.rearrange("p t (c i) -> p c t i", i=4)
+
         def interleave(copy, dst, src):
-            copy(out=dst.rearrange("p (c i) t -> p c t i", i=4), in_=src.rearrange("p t (c i) -> p c t i", i=4))
+            dst, src = walk(dst, src)
+            copy(out=dst, in_=src)
 
-        def pool_interleave(dst, src):
-            dst = dst.rearrange("p (c i) t -> p c t i", i=4)
-            src = src.rearrange("p t (c i) -> p c t i", i=4)
-            nc.gpsimd.tensor_scalar(out=dst, in0=src, scalar1=1.0, scalar2=0.0, op0=ALU.mult, op1=ALU.add)
+        done = set()
+        codes = {}
+        slot = {}
 
-        def quantize(cod, scl, src):
-            nc.vector.quantize_mx(out=cod.bitcast(FP8X4), scales=scl, in_=src)
+        def word_tile(tag, pieces, bufs):
+            words = stage.tile([P, len(pieces), P, 4], BF16, name=tag, bufs=bufs, align_bytes=64)
+            cod = const.tile([P, len(pieces) * P], U32, name="cod%d" % len(codes), align_bytes=64)
+            scl = const.tile([P, len(pieces) * P], U8, name="scl%d" % len(codes), align_bytes=64)
+            for i, piece in enumerate(pieces):
+                slot[piece] = (words, i)
+                codes[piece] = (cod, scl, i * P)
+            return words
 
-        def weave(dst, rows):
-            for j in (0, 2):
-                nc.tensor.matmul(out=dst.rearrange("p n j -> p j n")[:, j : j + 2, :], lhsT=ident_bf[:], rhs=rows[:, j : j + 2, :], start=True, stop=True)
+        def words_of(piece, n=1):
+            words, i = slot[piece]
+            return words[:, i : i + n, :, :].rearrange("p m n t -> p (m n) t")
 
-        def as_words(bank, n):
-            return bank[:].bitcast(BF16)[:, : 4 * n].rearrange("p (n j) -> p n j", j=4)
+        def operand(piece, n=1):
+            cod, scl, at = codes[piece]
+            return cod[:, at : at + n * P].bitcast(FP8X4), scl[:, at : at + n * P]
 
-        quantised = set()
-        made = set()
+        def quantize(pieces):
+            cod, scl = operand(pieces[0], len(pieces))
+            nc.vector.quantize_mx(out=cod, scales=scl, in_=words_of(pieces[0], len(pieces)).rearrange("p n t -> p (n t)"))
+            done.update(pieces)
 
-        wv_wide, words = {}, {}
+        def calls(pieces, split=None):
+            result, at = [], 0
+            for n in split or widths(len(pieces)):
+                result.append(pieces[at : at + n])
+                at = at + n
+            return result
 
-        def widen(h, j, on_vector=False):
-            if h not in wv_wide:
-                wv_wide[h] = stage.tile([P, 4, DV], BF16, name="wv_wide", bufs=5, align_bytes=64)
-            src = wv_row(h, j).bitcast(FP8)
-            if on_vector:
-                nc.vector.tensor_scalar(out=wv_wide[h][:, j, :], in0=src, scalar1=row_scale[:, j : j + 1], scalar2=None, op0=ALU.mult)
+        def weight_pieces(kind, h):
+            return [("wk", h)] if kind == "wk" else [("wv", h, 0), ("wv", h, 1)]
+
+        def latent_pieces(g):
+            return [("c", g, t) for t in range(4)]
+
+        def widen(h, n, j, engine="scalar"):
+            first = max(f for f, e in WV_LOADS if f <= h)
+            src = wv_load[first][:, j, (h - first) * DV : (h - first + n) * DV].bitcast(FP8)
+            dst = weight_rows("wv", h, n)[:, j, :]
+            if engine == "vector":
+                nc.vector.tensor_scalar(out=dst, in0=src, scalar1=row_scale[:, j : j + 1], scalar2=None, op0=ALU.mult)
             else:
-                nc.scalar.activation(out=wv_wide[h][:, j, :], in_=src, func=COPY, scale=row_scale[:, j : j + 1])
-            made.add(("wide", h, j))
+                nc.scalar.activation(out=dst, in_=src, func=COPY, scale=row_scale[:, j : j + 1])
+            done.update(("wide", h + i, j) for i in range(n))
 
-        def weight_rows(kind, h):
-            return wv_wide.pop(h)[:] if kind == "wv" else wk_rows(h)
-
-        def weight_words(kind, h):
-            n = DV if kind == "wv" else DK
-            tile = stage.tile([P, n, 4], BF16, name=kind + "_words", bufs=3, align_bytes=64)
-            words[kind, h] = tile[:]
-            return tile[:]
-
-        def vector_interleave(kind, h):
-            interleave(nc.vector.tensor_copy, weight_words(kind, h), weight_rows(kind, h))
-
-        def quantize_weight(kind, h):
-            cod, scl = (wv_cod, wv_scl) if kind == "wv" else (wk_cod, wk_scl)
-            quantize(cod[:, h, :], scl[:, h, :], words.pop((kind, h)).rearrange("p n j -> p (n j)"))
-            quantised.add((kind, h))
-
-        def transpose_c(bank, g, b):
+        def turn(bank, g, b):
             if g == 0:
-                rows = c_rows[g, b][:].bitcast(F32)
+                src = c_half[b][:].bitcast(F32)
             else:
-                rows = c_group[g][:].bitcast(F32).rearrange("p (t w) -> p t w", t=4)[:, 2 * b : 2 * b + 2, :]
+                src = c_group[g][:].bitcast(F32).rearrange("p (t w) -> p t w", t=4)[:, 2 * b : 2 * b + 2, :]
             for i in range(2):
                 for u in range(2):
                     col = (2 * i + u) * P
-                    nc.tensor.transpose(bank[:, col : col + P], rows[:, i, u::2], ident[:])
+                    nc.tensor.transpose(bank[:, col : col + P], src[:, i, u::2], ident[:])
 
-        def turned_c_out(bank, g, b, copy, name="c_words", bufs=2 * G):
-            tile = stage.tile([P, 2, P, 4], BF16, name=name, bufs=bufs, align_bytes=64)
-            copy(out=tile[:].bitcast(F32), in_=bank[:].rearrange("q (i u p) -> q i p u", i=2, u=2))
-            words["c", g, b] = tile[:]
+        def turn_out(bank, g, b):
+            words, i = slot["c", g, 2 * b]
+            nc.scalar.copy(out=words[:, i : i + 2, :, :].bitcast(F32), in_=bank[:].rearrange("q (i u p) -> q i p u", i=2, u=2))
 
-        def quantize_c(g, b):
-            cols = slice(2 * b * P, 2 * (b + 1) * P)
-            quantize(c_cod[:, g, cols], c_scl[:, g, cols], words.pop(("c", g, b)).rearrange("q i p e -> q (i p e)"))
-            quantised.add(("c", g, b))
+        def project(dst, g, t, weight, n):
+            lhs, lhs_scale = operand(("c", g, t))
+            rhs, rhs_scale = operand(weight, n)
+            nc.tensor.matmul_mx(out=dst, lhsT=lhs, lhsT_scale=lhs_scale, rhs=rhs, rhs_scale=rhs_scale, start=True, stop=True)
 
-        def widen_factors():
-            nc.vector.tensor_copy(out=write_f[:], in_=write_raw[:].rearrange("p g (t h) -> p g h t", t=4))
+        def weight_of(piece):
+            return ("wk", piece[1]) if piece[0] == "k" else ("wv", piece[1], piece[3])
 
-        def project(dst, g, t, cod, scl):
-            cols = slice(t * P, (t + 1) * P)
-            nc.tensor.matmul_mx(
-                out=dst,
-                lhsT=c_cod[:, g, cols].bitcast(FP8X4),
-                lhsT_scale=c_scl[:, g, cols],
-                rhs=cod.bitcast(FP8X4),
-                rhs_scale=scl,
-                start=True,
-                stop=True,
-            )
-
-        def project_keys(bank, r, u):
-            h, g = units(r)[u]
+        def project_piece(bank, piece):
             for t in range(4):
-                project(bank[:, t * DK : (t + 1) * DK], g, t, wk_cod[:, h, :], wk_scl[:, h, :])
+                project(bank[:, t * P : (t + 1) * P], piece[2], t, weight_of(piece), 1)
 
-        def project_piece(bank, r, m):
-            h, g = units(r)[m // 2]
-            cols = slice((m % 2) * P, (m % 2 + 1) * P)
-            for t in range(4):
-                project(bank[:, t * P : (t + 1) * P], g, t, wv_cod[:, h, cols], wv_scl[:, h, cols])
+        def piece_out(bank, piece):
+            h, g = piece[1:3]
+            src = bank[:].rearrange("p (t n) -> p n t", t=4)
+            if piece[0] == "k":
+                by = factor[:, 0, g, h, :].unsqueeze(1).to_broadcast([P, P, 4])
+                nc.vector.scalar_tensor_tensor(out=words_of(piece), in0=src, scalar=0.0, in1=by, op0=ALU.max, op1=ALU.mult)
+            else:
+                by = factor[:, 1, g, h, :].unsqueeze(1).to_broadcast([P, P, 4])
+                nc.vector.tensor_tensor(out=words_of(piece), in0=src, in1=by, op=ALU.mult)
 
-        def project_rows(bank, r, u, b):
-            h, g = units(r)[u]
+        rows = {}
+
+        def rows_tile(p):
+            pieces = values(*ROWS[p])
+            tile = stage.tile([P, 4, len(pieces) * P], BF16, name="rows", bufs=ROW_BUFS, align_bytes=64)
+            for i, piece in enumerate(pieces):
+                rows[piece] = (tile, i)
+
+        def rows_of(piece, n=1):
+            if piece[0] != "v":
+                return weight_rows(piece[0], piece[1])[:, :, : n * P] if piece[0] == "wk" else weight_rows("wv", piece[1])[:, :, piece[2] * P : (piece[2] + n) * P]
+            tile, i = rows[piece]
+            return tile[:, :, i * P : (i + n) * P]
+
+        def project_rows(bank, h, g, b):
             for i in range(2):
-                project(bank[:, i * DV : (i + 1) * DV], g, 2 * b + i, wv_cod[:, h, :], wv_scl[:, h, :])
+                project(bank[:, i * DV : (i + 1) * DV], g, 2 * b + i, ("wv", h, 0), 2)
 
-        own, rows, woven = {}, {}, {}
-
-        def own_words(r):
-            if r not in own:
-                own[r] = stage.tile([P, len(units(r)) + DIRECT[r], P, 4], BF16, name="own_words", align_bytes=64)
-            return own[r]
-
-        def keys_out(bank, r, u):
-            h, g = units(r)[u]
-            nc.vector.scalar_tensor_tensor(
-                out=own_words(r)[:, u, :, :],
-                in0=bank[:].rearrange("p (t n) -> p n t", t=4),
-                scalar=0.0,
-                in1=keep_f[:, g, h, :].unsqueeze(1).to_broadcast([P, DK, 4]),
-                op0=ALU.max,
-                op1=ALU.mult,
-            )
-
-        def piece_out(bank, r, m):
-            h, g = units(r)[m // 2]
-            nc.vector.tensor_tensor(
-                out=own_words(r)[:, len(units(r)) + m, :, :],
-                in0=bank[:].rearrange("p (t n) -> p n t", t=4),
-                in1=write_f[:, g, h, :].unsqueeze(1).to_broadcast([P, P, 4]),
-                op=ALU.mult,
-            )
-
-        def scaled_rows(r):
-            if r not in rows:
-                rows[r] = stage.tile([P, 4, (2 * len(units(r)) - DIRECT[r]) * P], BF16, name="rows", bufs=3, align_bytes=64)
-            return rows[r]
-
-        def piece_rows(r, i):
-            return scaled_rows(r)[:, :, i * P : (i + 1) * P]
-
-        def half_out(bank, r, m):
-            h, g = units(r)[m // 2]
-            for t in range(4):
-                nc.scalar.activation(out=piece_rows(r, m - DIRECT[r])[:, t, :], in_=bank[:, t * P : (t + 1) * P], func=COPY, scale=write_f[:, g, h, t : t + 1])
-            made.add(("rows", r, m))
-
-        def rows_out(bank, r, u, b):
-            h, g = units(r)[u]
-            first = 2 * u - DIRECT[r]
+        def rows_out(bank, h, g, b):
             for i in range(2):
                 t = 2 * b + i
-                nc.scalar.activation(out=scaled_rows(r)[:, t, first * P : (first + 2) * P], in_=bank[:, i * DV : (i + 1) * DV], func=COPY, scale=write_f[:, g, h, t : t + 1])
-            if b == 1:
-                made.add(("rows", r, 2 * u))
-                made.add(("rows", r, 2 * u + 1))
+                nc.scalar.activation(out=rows_of(("v", h, g, 0), 2)[:, t, :], in_=bank[:, i * DV : (i + 1) * DV], func=COPY, scale=factor[:, 1, g, h, t : t + 1])
+            done.add(("rows", h, g, b))
 
-        def weave_piece(bank, r, i):
-            weave(as_words(bank, P), piece_rows(r, i))
+        def as_words(bank, n):
+            return bank[:].bitcast(BF16)[:, : 4 * n * P].rearrange("p (n j) -> p n j", j=4)
 
-        def woven_words(r):
-            if r not in woven:
-                woven[r] = stage.tile([P, WOVEN[r], P, 4], BF16, name="woven", bufs=3, align_bytes=64)
-            return woven[r]
+        def weave(bank, piece, n):
+            dst = as_words(bank, n).rearrange("p n j -> p j n")
+            for j in (0, 2):
+                nc.tensor.matmul(out=dst[:, j : j + 2, :], lhsT=ident_bf[:], rhs=rows_of(piece, n)[:, j : j + 2, :], start=True, stop=True)
 
-        def woven_piece_out(bank, r, i):
-            nc.scalar.copy(out=woven_words(r)[:, i, :, :], in_=as_words(bank, P))
+        def weave_out(bank, piece, n):
+            nc.scalar.copy(out=words_of(piece, n), in_=as_words(bank, n))
 
-        def weave_weight(bank, kind, h):
-            weave(as_words(bank, DV if kind == "wv" else DK), weight_rows(kind, h))
+        def copy_piece(piece):
+            interleave(nc.scalar.copy, words_of(piece), rows_of(piece))
 
-        def woven_weight_out(bank, kind, h):
-            nc.scalar.copy(out=weight_words(kind, h), in_=as_words(bank, DV if kind == "wv" else DK))
+        def state_pass(dst, h, g, f, n, start, stop):
+            lhs, lhs_scale = operand(("k", h, g))
+            rhs, rhs_scale = operand(("v", h, g, f), n)
+            nc.tensor.matmul_mx(out=dst, lhsT=lhs, lhsT_scale=lhs_scale, rhs=rhs, rhs_scale=rhs_scale, start=start, stop=stop)
 
-        pooled = {}
-
-        def pool_tile(w, pieces):
-            pooled[w] = stage.tile([P, pieces, P, 4], BF16, name="pool_out", bufs=1, align_bytes=64)
-
-        def pool_weights(w, jobs):
-            pool_tile(w, sum(2 if kind == "wv" else 1 for kind, h in jobs))
-            at = 0
-            for kind, h in jobs:
-                n = 2 if kind == "wv" else 1
-                words[kind, h] = pooled[w][:, at : at + n, :, :].rearrange("p m n j -> p (m n) j")
-                if (kind, h) == ("wk", 2):
-                    nc.gpsimd.tensor_scalar(out=keep_f[:], in0=keep_raw[:].rearrange("p g (t h) -> p g h t", t=4), scalar1=1.0, scalar2=0.0, op0=ALU.mult, op1=ALU.add)
-                pool_interleave(words[kind, h], weight_rows(kind, h))
-                at = at + n
-
-        def pool_values(r):
-            pool_tile(r + 1, 2 * len(units(r)) - DIRECT[r] - WOVEN[r])
-            pool_interleave(pooled[r + 1][:].rearrange("p m n t -> p (m n) t"), scaled_rows(r)[:, :, WOVEN[r] * P :])
-
-        cod, scl = {}, {}
-        for r in range(ROUNDS):
-            cod[r] = const.tile([P, len(units(r)) * (DK + DV)], U32, name="cod%d" % r, align_bytes=64)
-            scl[r] = const.tile([P, len(units(r)) * (DK + DV)], U8, name="scl%d" % r, align_bytes=64)
-
-        def quantize_pieces(r, at, src):
-            n = src.shape[1]
-            cols = slice(at * P, (at + n) * P)
-            quantize(cod[r][:, cols], scl[r][:, cols], src.rearrange("p m n t -> p (m n t)"))
-            for m in range(at, at + n):
-                quantised.add(("piece", r, m))
-
-        def quantize_calls(r, at, tile, first, end):
-            calls = []
-            for n in widths(end - first):
-                calls.append((quantize_pieces, r, at + first, tile[:, first : first + n, :, :]))
-                first = first + n
-            return calls
-
-        def state_pass(dst, h, g, first, end):
-            r, u = place(h, g)
-            k_cols = slice(u * DK, (u + 1) * DK)
-            at = len(units(r)) * DK + u * DV
-            v_cols = slice(at + first, at + end)
-            nc.tensor.matmul_mx(
-                out=dst,
-                lhsT=cod[r][:, k_cols].bitcast(FP8X4),
-                lhsT_scale=scl[r][:, k_cols],
-                rhs=cod[r][:, v_cols].bitcast(FP8X4),
-                rhs_scale=scl[r][:, v_cols],
-                start=(g == 0),
-                stop=(g == G - 1),
-            )
+        def side_by_side(h, g):
+            low, high = codes["v", h, g, 0], codes["v", h, g, 1]
+            return low[0] is high[0] and high[2] == low[2] + P
 
         def sum_state(bank, h, at=0):
-            for g in range(G):
-                state_pass(bank[:, at : at + DV], h, g, 0, DV)
+            whole = [g for g in range(G) if side_by_side(h, g)]
+            passes = [(g, 0, 2) for g in whole] + [(g, f, 1) for g in range(G) if g not in whole for f in range(2)]
+            for i, (g, f, n) in enumerate(passes):
+                state_pass(bank[:, at + f * P : at + (f + n) * P], h, g, f, n, i == 0, i == len(passes) - 1)
 
         def store_state(bank, h, at=0):
             result = stage.tile([P, DV], F32, name="result", bufs=H - 1)
             nc.scalar.copy(out=result[:], in_=bank[:, at : at + DV])
             nc.sync.dma_start(out=out[h], in_=result[:])
 
-        def head_pieces(h):
-            need = []
-            for g in range(G):
-                r, u = place(h, g)
-                n = len(units(r))
-                need.extend([("piece", r, u), ("piece", r, n + 2 * u), ("piece", r, n + 2 * u + 1)])
-            return need
-
-        def unit_operands(kind, r, u):
-            h, g = units(r)[u]
-            return [(kind, h), ("c", g, 0), ("c", g, 1)]
-
-        def vector_jobs(r):
-            keys = [(project_keys, keys_out, (r, u), unit_operands("wk", r, u)) for u in range(len(units(r)))]
-            pieces = [(project_piece, piece_out, (r, m), unit_operands("wv", r, m // 2)) for m in range(DIRECT[r])]
+        def pool_interleave(r):
+            pieces = POOL[r]
+            word_tile("pool_words", pieces, 1)
             if r == 0:
-                return pieces + keys
-            return keys[:2] + pieces + keys[2:]
+                src = early[:, :, 2 * DK : 4 * DK + DV]
+            elif pieces[0][0] != "v":
+                src = late[:]
+            else:
+                src = rows_of(pieces[0], len(pieces))
+            dst, src = walk(words_of(pieces[0], len(pieces)), src)
+            nc.gpsimd.tensor_scalar(out=dst, in0=src, scalar1=1.0, scalar2=0.0, op0=ALU.mult, op1=ALU.add)
 
-        def row_jobs(r):
-            jobs = []
-            if DIRECT[r] % 2:
-                jobs.append((project_piece, half_out, (r, DIRECT[r]), unit_operands("wv", r, DIRECT[r] // 2)))
-            for u in range((DIRECT[r] + 1) // 2, len(units(r))):
-                jobs.extend((project_rows, rows_out, (r, u, b), unit_operands("wv", r, u)) for b in range(2))
-            return jobs
+        def widen_factor(copy, i):
+            copy(out=factor[:, i, :, :, :], in_=factor_raw[:, i, :, :].rearrange("p g (t h) -> p g h t", t=4))
 
-        def piece_job(r, i):
-            return (weave_piece, woven_piece_out, (r, i), [("rows", r, DIRECT[r] + i)])
+        def widen_keep():
+            widen_factor(nc.scalar.copy, 0)
 
-        def copy_piece(r, i):
-            interleave(nc.scalar.copy, woven_words(r)[:, i, :, :], piece_rows(r, i))
+        def job(step):
+            kind, args = step[0], step[1:]
+            if kind in ("k", "v"):
+                return (project_piece, piece_out, (step,), [weight_of(step)] + latent_pieces(step[2]))
+            if kind == "rows":
+                return (project_rows, rows_out, args, weight_pieces("wv", args[0]) + latent_pieces(args[1]) + [("rows",)])
+            if kind == "turn":
+                return (turn, turn_out, args, [step])
+            if kind == "weave":
+                piece = args[0]
+                need = [("rows", piece[1], piece[2], 1)] if piece[0] == "v" else [("wide", piece[1], 3)] if piece[0] == "wv" else [("late",)]
+                return (weave, weave_out, args, need)
+            if kind == "state":
+                return (sum_state, store_state, args, keys(*[(args[0], g) for g in range(G)]) + values(*[(args[0], g) for g in range(G)]))
+            return (None, {"widen": widen, "copy": copy_piece}.get(kind, widen_keep), args, [])
 
-        def copy_job(r, i):
-            return (None, copy_piece, (r, i), [])
-
-        def weight_job(kind, h):
-            return (weave_weight, woven_weight_out, (kind, h), [("wide", h, j) for j in range(4)] if kind == "wv" else [("turn", 1, 1)])
-
-        def turn_job(g, b):
-            return (transpose_c, turned_out, (g, b), [("turn", g, b)])
-
-        def turned_out(bank, g, b):
-            turned_c_out(bank, g, b, nc.scalar.copy)
-
-        def state_job(h):
-            return (sum_state, store_state, (h,), head_pieces(h))
-
-        def widen_pair(h, j):
-            widen(h, j)
-            widen(h, j + 1)
-
-        def widen_jobs(h):
-            return [(None, widen_pair, (h, j), []) for j in (0, 2)]
-
-        def scalar_steps(p):
-            row = [[job] for job in row_jobs(p)]
-            wide = [[[job] for job in widen_jobs(h)] for h in range(H)]
-            if p == 0:
-                return [wide[3][0] + wide[3][1]] + wide[4] + [[turn_job(1, 0)], wide[5][0], [turn_job(1, 1)], [weight_job("wk", 4)], wide[5][1], [turn_job(2, 0)]]
-            if p == 1:
-                return wide[6][:1] + row[:2] + [[turn_job(2, 1)]] + row[2:3] + [wide[6][1] + [turn_job(3, 0)]] + row[3:4] + [[turn_job(3, 1)]] + row[4:]
-            if p == 2:
-                return row + [[weight_job("wv", 5)], [weight_job("wk", 6)]] + wide[7]
-            if p == 3:
-                return row + [[weight_job("wv", 6)], [weight_job("wk", 7)], [copy_job(p, 0)]]
-            if p == 4:
-                return row + [[weight_job("wv", 7)], [piece_job(p, 0)]]
-            if p == 5:
-                return row + [[piece_job(p, 0), state_job(0)], [state_job(1)]]
-            if p == 6:
-                return row + [[piece_job(p, 0), state_job(2)]]
-            if p == 7:
-                return row + [[piece_job(p, 0), piece_job(p, 1)], [copy_job(p, 2)], [state_job(3)]]
-            return row + [[piece_job(p, 0)], [copy_job(p, 2)], [piece_job(p, 1)]]
-
-        v_jobs = vector_jobs(0)
-        s_jobs = [job for p in range(ROUNDS) for step in scalar_steps(p) for job in step if job[0] is not None]
+        v_jobs = []
+        s_jobs = [job(s) for s in SCALAR if job(s)[0] is not None]
         v_full, s_full = [], []
 
-        def refill(jobs, full, new_bank, depth, most=VECTOR_BANKS):
+        def refill(jobs, full, new_bank, depth, most):
             for i in range(most):
-                if not (jobs and len(full) < depth and all(x in quantised or x in made for x in jobs[0][3])):
+                if not (jobs and len(full) < depth and all(x in done for x in jobs[0][3])):
                     break
                 fill, empty, args, need = jobs.pop(0)
                 bank = new_bank()
                 fill(bank, *args)
                 full.append(bank)
 
-        def refill_both(most=VECTOR_BANKS):
+        def refill_both(most):
             refill(v_jobs, v_full, vector_bank, VECTOR_BANKS, most)
-            refill(s_jobs, s_full, scalar_bank, SCALAR_BANKS)
+            refill(s_jobs, s_full, scalar_bank, SCALAR_BANKS, 2)
 
-        def run(job, full, most=1):
-            fill, empty, args, need = job
+        def run(step, full, most):
+            fill, empty, args, need = job(step)
             if fill is None:
                 empty(*args)
             else:
                 empty(full.pop(0), *args)
             refill_both(most)
 
+        steps = list(SCALAR)
+        clock = {"vector": HEAD_START, "scalar": 0}
+
+        def scalar_step(most):
+            step = steps.pop(0)
+            clock["scalar"] = clock["scalar"] + span(step)
+            if step[0] == "rows" and ("v", step[1], step[2], 0) not in rows:
+                rows_tile([p for p in range(ROUNDS) if step[1:3] in ROWS[p]][0])
+            if step[0] in ("turn", "weave", "copy"):
+                first = ("c", step[1], 0) if step[0] == "turn" else step[1]
+                if first not in slot:
+                    word_tile("scalar_words", [w for w in SCALAR_WORDS if first in w][0], 3)
+            if step[0] == "allow":
+                done.add(step[1:])
+                refill_both(0)
+            else:
+                run(step, s_full, most)
+            done.add(("step", step))
+
+        def scalar_until(length, most):
+            clock["vector"] = clock["vector"] + length
+            while steps and clock["scalar"] + span(steps[0]) <= clock["vector"] and (s_full or job(steps[0])[0] is None):
+                scalar_step(most)
+
+        def writes(step, pieces):
+            if step[0] == "turn":
+                return ("c", step[1], 2 * step[2]) in pieces
+            if step[0] == "rows":
+                return ("rows", step[1], step[2]) in pieces
+            if step[0] == "widen":
+                return ("wv", step[1], 0) in pieces
+            return step[0] in ("weave", "copy") and step[1] in pieces
+
+        def scalar_through(pieces):
+            while any(writes(step, pieces) for step in steps):
+                scalar_step(0)
+            clock["vector"] = max(clock["vector"], clock["scalar"])
+
         warm_up(4)
-        for j in range(4):
-            widen(0, j, on_vector=(j % 2 == 1))
-        for j in range(4):
-            widen(1, j, on_vector=(j % 2 == 1))
+        for h in range(2):
+            for j in range(4):
+                widen(h, 1, j, "vector" if j % 2 else "scalar")
+        word_tile("head_c", latent_pieces(0), 1)
+        word_tile("head_wv", weight_pieces("wv", 0) + weight_pieces("wv", 1), 1)
+        word_tile("pool_words", [("wk", 0), ("wk", 1)], 1)
         turned = [scalar_bank(), scalar_bank()]
         for b in range(2):
-            transpose_c(turned[b], 0, b)
+            turn(turned[b], 0, b)
         warm_up(2)
-        turned_c_out(turned[0], 0, 0, nc.scalar.copy)
-        turned_c_out(turned[1], 0, 1, nc.scalar.copy)
-        vector_interleave("wv", 0)
-        vector_interleave("wv", 1)
-        quantize_weight("wv", 0)
-        quantize_c(0, 0)
-        quantize_weight("wv", 1)
-        quantize_c(0, 1)
-        refill_both()
-        vector_interleave("wk", 0)
-        words["wk", 1] = stage.tile([P, DK, 4], BF16, name="pool_out", bufs=1, align_bytes=64)[:]
-        interleave(nc.vector.tensor_copy, words["wk", 1], wk_rows(1))
-        quantize_weight("wk", 0)
-        widen_factors()
-        quantize_weight("wk", 1)
-        refill_both()
-
-        def scalar_pieces(r):
-            at = len(units(r)) + DIRECT[r]
-            calls = quantize_calls(r, at, woven[r], 0, WOVEN[r]) if WOVEN[r] else []
-            return calls + quantize_calls(r, at + WOVEN[r], pooled[r + 1], 0, pooled[r + 1].shape[1])
-
-        def quantize_run(r):
-            n = len(units(r - 1))
-            first = []
-            if r == 1:
-                first = [(quantize_c, 1, 0), (quantize_c, 1, 1)]
-            if r == 2:
-                first = [(quantize_c, 2, 0), (quantize_c, 2, 1)]
-            if r == 3:
-                first = [(quantize_weight, "wk", 4)]
-            if r == 4:
-                first = [(quantize_weight, "wv", 5), (quantize_weight, "wk", 6)]
-            if r == 5:
-                first = [(quantize_weight, "wv", 6), (quantize_weight, "wk", 7)]
-            if r == 6:
-                first = [(quantize_weight, "wv", 7)]
-            mine = quantize_calls(r - 1, 0, own_words(r - 1), n, n + DIRECT[r - 1])
-            if r == 1:
-                release = [(quantize_weight, "wk", 2), (quantize_weight, "wv", 2), (quantize_weight, "wk", 3)]
-            elif r == 2:
-                release = [(quantize_weight, "wv", 3), (quantize_c, 3, 0), (quantize_weight, "wv", 4), (quantize_c, 3, 1), (quantize_weight, "wk", 5)]
-            else:
-                release = scalar_pieces(r - 2)
-            return first + mine + release + quantize_calls(r - 1, 0, own_words(r - 1), 0, n)
-
-        def width(step):
-            if step[0] is quantize_pieces:
-                return step[3].shape[1] * 4 * P
-            return 4 * DK if step[1] == "wk" else 4 * DV
-
-        def call(step):
-            step[0](*step[1:])
-            refill_both(1)
-
-        def scalar_step(steps, most=1):
-            for job in steps.pop(0) if steps else []:
-                run(job, s_full, most)
+        for b in range(2):
+            turn_out(turned[b], 0, b)
+        v_jobs.extend(job(s) for s in WINDOW[0])
+        for h in range(2):
+            interleave(nc.vector.tensor_copy, words_of(("wv", h, 0), 2), weight_rows("wv", h))
+        quantize(weight_pieces("wv", 0))
+        quantize(latent_pieces(0)[:2])
+        quantize(weight_pieces("wv", 1))
+        quantize(latent_pieces(0)[2:])
+        refill_both(VECTOR_BANKS)
+        interleave(nc.vector.tensor_copy, words_of(("wk", 0), 2), weight_rows("wk", 0, 2))
+        widen_factor(nc.vector.tensor_copy, 1)
+        quantize([("wk", 0), ("wk", 1)])
 
         for p in range(ROUNDS):
-            steps = scalar_steps(p)
-            if p == 0:
-                for job in widen_jobs(2):
-                    run(job, s_full)
-                made.add(("turn", 1, 0))
-                refill_both()
-                pool_weights(0, [("wv", 2), ("wk", 2), ("wk", 3)])
-            elif p == 1:
-                pool_weights(1, [("wv", 3), ("wv", 4), ("wk", 5)])
-            else:
-                pool_values(p - 1)
-            if p == H:
-                early = vector_bank()
-                sum_state(early, H - 4, DV)
-            for i, job in enumerate(vector_jobs(p)):
-                run(job, v_full)
-                if p == 0 and i == 1:
-                    made.add(("turn", 1, 1))
-                if p == 0 and i == 3:
-                    made.add(("turn", 2, 0))
-                if p == 1 and i in (2, 4):
-                    made.add(("turn", 3, i // 2 - 1))
-                refill_both(0)
-                scalar_step(steps)
-            if p == H:
+            word_tile("own_words", WINDOW[p], 2)
+            scalar_through(POOL[p] + [("wv", 4, 0)] * p if p < 2 else [("rows",) + piece[1:3] for piece in POOL[p]])
+            pool_interleave(p)
+            if p == ROUNDS - 1:
                 break
-            columns = 0
-            v_jobs.extend(vector_jobs(p + 1))
-            refill_both(1)
-            for step in quantize_run(p + 1):
-                step[0](*step[1:])
-                columns = columns + width(step)
-                if columns >= 3 * 4 * P:
-                    columns = columns - 3 * 4 * P
-                    refill_both(1)
-                    scalar_step(steps, 0)
-            refill_both()
-            while steps:
-                scalar_step(steps)
+            for step in WINDOW[p]:
+                scalar_until(16, 0)
+                run(step, v_full, 1)
+            v_jobs.extend(job(s) for s in WINDOW[p + 1])
+            run_calls = calls(SCALAR_WORDS[p]) + calls(POOL[p]) + [WINDOW[p]]
             if p == 0:
-                made.add(("turn", 2, 1))
-                refill_both()
+                run_calls = [POOL[0][:2], WINDOW[0][:4]] + calls(SCALAR_WORDS[0], (2, 4)) + [POOL[0][2:], WINDOW[0][4:]]
+            for pieces in run_calls:
+                scalar_through(pieces)
+                scalar_until(4 * len(pieces), 1)
+                quantize(pieces)
+                refill_both(1)
+            refill_both(VECTOR_BANKS)
 
         last = H - 1
-        sum_state(early, H - 3)
+        for i, step in enumerate(WINDOW[-1]):
+            scalar_until(16, 0)
+            run(step, v_full, 1)
+            if i == 0:
+                early_bank = vector_bank()
+                sum_state(early_bank, last - 2)
+            if i == 1:
+                before_last = vector_bank()
+                for g in range(G - 1):
+                    state_pass(before_last[:, :DV], last - 1, g, 0, 2, g == 0, False)
         halves = [vector_bank(), vector_bank()]
-        n = len(units(H))
-        for step in scalar_pieces(last):
-            call(step)
-        before_last = vector_bank()
-        sum_state(before_last, last - 1)
-        call(quantize_calls(H, 0, own_words(H), 0, n + DIRECT[H])[0])
-        while steps:
-            scalar_step(steps)
-        store_state(early, H - 4, DV)
-        store_state(early, H - 3)
+        late_pieces = SCALAR_WORDS[-1]
+
+        def last_passes(g):
+            for f in range(2):
+                state_pass(halves[f][:, :P], last, g, f, 1, g == 2, g == G - 1)
+
+        scalar_through(late_pieces)
+        quantize(late_pieces[:4])
+        state_pass(before_last[:, :DV], last - 1, G - 1, 0, 2, False, True)
+        quantize(WINDOW[-1])
+        last_passes(2)
+        quantize(POOL[-1])
+        last_passes(0)
+        last_passes(1)
+        store_state(early_bank, last - 2)
         store_state(before_last, last - 1)
-        for f in (0, 2, 1):
-            quantize_pieces(H, n + DIRECT[H] + f, woven[H][:, f : f + 1, :, :])
-        for g in range(G):
-            for f in (1, 0):
-                state_pass(halves[f][:, :P], last, g, f * P, (f + 1) * P)
+        quantize(late_pieces[4:])
+        last_passes(3)
         low = stage.tile([P, P], F32, name="result_half")
         nc.scalar.copy(out=low[:], in_=halves[0][:, :P])
         nc.sync.dma_start(out=out[last][:, :P], in_=low[:])

@@ -48,6 +48,7 @@ ROWS = [
     [(7, 3)],
 ]
 ROW_BUFS = 3
+PAD = 96
 POOL = [
     [("wk", 2), ("wk", 3), ("wv", 2, 0), ("wv", 2, 1)],
     [("wv", h, f) for h in (4, 5) for f in range(2)] + [("wk", h) for h in range(4, H)],
@@ -135,8 +136,8 @@ def tile_latent_kv_state_s7_kernel(tc, c, wk, wv_bytes, wv_scale, keep, write, o
         c_half = [const.tile([P, 2, L], BF16, name="c_half%d" % b, align_bytes=64) for b in range(2)]
         c_group = {g: const.tile([P, 4 * L], BF16, name="c_group%d" % g, align_bytes=64) for g in range(1, G)}
         wv_load = {first: const.tile([P, 4, (end - first) * DV], U8, name="wv_load%d" % first, align_bytes=64) for first, end in WV_LOADS}
-        early = const.tile([P, 4, 4 * DK + 2 * DV], BF16, name="early", align_bytes=64)
-        late = const.tile([P, 4, 2 * DV + 4 * DK], BF16, name="late", align_bytes=64)
+        early = const.tile([P, 4, 4 * DK + 2 * DV + PAD], BF16, name="early", align_bytes=64)
+        late = const.tile([P, 4, 2 * DV + 4 * DK + PAD], BF16, name="late", align_bytes=64)
         wv_first = [const.tile([P, 4, DV], BF16, name="wv_first%d" % h, align_bytes=64) for h in range(2)]
         wv_last = const.tile([P, 4, 2 * DV], BF16, name="wv_last", align_bytes=64)
 
@@ -296,7 +297,7 @@ def tile_latent_kv_state_s7_kernel(tc, c, wk, wv_bytes, wv_scale, keep, write, o
 
         def rows_tile(p):
             pieces = values(*ROWS[p])
-            tile = stage.tile([P, 4, len(pieces) * P], BF16, name="rows", bufs=ROW_BUFS, align_bytes=64)
+            tile = stage.tile([P, 4, len(pieces) * P + PAD], BF16, name="rows", bufs=ROW_BUFS, align_bytes=64)
             for i, piece in enumerate(pieces):
                 rows[piece] = (tile, i)
 
@@ -356,7 +357,7 @@ def tile_latent_kv_state_s7_kernel(tc, c, wk, wv_bytes, wv_scale, keep, write, o
             if r == 0:
                 src = early[:, :, 2 * DK : 4 * DK + DV]
             elif pieces[0][0] != "v":
-                src = late[:]
+                src = late[:, :, : 2 * DV + 4 * DK]
             else:
                 src = rows_of(pieces[0], len(pieces))
             dst, src = walk(words_of(pieces[0], len(pieces)), src)
@@ -484,7 +485,7 @@ def tile_latent_kv_state_s7_kernel(tc, c, wk, wv_bytes, wv_scale, keep, write, o
             v_jobs.extend(job(s) for s in WINDOW[p + 1])
             run_calls = calls(SCALAR_WORDS[p]) + calls(POOL[p]) + [WINDOW[p]]
             if p == 0:
-                run_calls = [POOL[0][:2], WINDOW[0][:4]] + calls(SCALAR_WORDS[0], (2, 4)) + [POOL[0][2:], WINDOW[0][4:]]
+                run_calls = [POOL[0][:2], SCALAR_WORDS[0][:2], WINDOW[0][4:], SCALAR_WORDS[0][2:], POOL[0][2:], WINDOW[0][:4]]
             for pieces in run_calls:
                 scalar_through(pieces)
                 scalar_until(4 * len(pieces), 1)

@@ -33,41 +33,48 @@ WINDOW = [
     values((0, 0), (1, 0)) + keys((0, 0), (1, 0)),
     keys((2, 0), (3, 0), (0, 1), (1, 1)) + values((0, 1)) + keys((2, 1), (3, 1)),
     keys((0, 2), (1, 2)) + values((0, 2), (0, 3)) + keys((0, 3), (1, 3)),
-    keys((2, 2), (2, 3), (3, 2), (3, 3)) + values((3, 2)) + keys((4, 0), (4, 1)),
+    keys((2, 2), (2, 3), (3, 2), (3, 3)) + values((1, 3)) + keys((4, 0), (4, 1)),
     keys((4, 2), (4, 3), (5, 0), (5, 1)) + values((4, 3)) + keys((5, 2), (5, 3)),
     keys((6, 0), (6, 1), (6, 2), (6, 3)) + values((6, 1), (6, 2)),
     keys((7, 0), (7, 1), (7, 2), (7, 3)),
 ]
 ROWS = [
     [],
-    [(1, 1), (2, 0), (2, 1), (3, 0)],
-    [(1, 2), (1, 3), (3, 1), (2, 2), (2, 3)],
-    [(3, 3), (4, 0), (4, 1), (4, 2)],
+    [(1, 1), (2, 0)],
+    [(2, 1), (1, 2), (2, 2), (2, 3), (3, 0)],
+    [(3, 2), (3, 3), (4, 0), (4, 1), (3, 1), (4, 2)],
     [(5, 0), (5, 1), (5, 2), (5, 3), (6, 0)],
     [(7, 0), (7, 1), (6, 3), (7, 2)],
     [(7, 3)],
 ]
-ROW_BUFS = 3
-PAD = 96
+ROW_BUFS = 2
 POOL = [
     [("wk", 2), ("wk", 3), ("wv", 2, 0), ("wv", 2, 1)],
     [("wv", h, f) for h in (4, 5) for f in range(2)] + [("wk", h) for h in range(4, H)],
-] + [values(*ROWS[r - 1])[: len(WINDOW[r])] for r in range(2, ROUNDS)]
+    [("wv", h, f) for h in (6, 7) for f in range(2)] + values(*ROWS[1]),
+] + [values(*ROWS[r - 1])[: len(WINDOW[r])] for r in range(3, ROUNDS)]
 SCALAR_WORDS = [
-    [("wv", 3, 0), ("wv", 3, 1)] + [("c", 1, t) for t in range(4)],
-    [("c", g, t) for g in (2, 3) for t in range(4)],
-    [],
-    [("wv", 6, 0), ("wv", 6, 1)] + values((2, 3)),
-    [("wv", 7, 0), ("wv", 7, 1)],
+    [("c", 1, t) for t in range(4)],
+    [("c", g, t) for g in (2, 3) for t in range(4)] + [("wv", 3, 0), ("wv", 3, 1)],
+    values((3, 0)),
+    values((3, 1)),
+    values((4, 2)),
     values((6, 0)),
     values((6, 3), (7, 2), (7, 3)),
 ]
-PACE = 4
-LEAD = 4
+
+
+A1 = 2
+A2 = 4
 
 
 def row_steps(p):
     return [("rows", h, g, b) for h, g in ROWS[p] for b in range(2)]
+
+
+def spare_first(p, n):
+    steps = row_steps(p)
+    return steps[8 : 8 + 2 * n] + steps[:8] + steps[8 + 2 * n :]
 
 
 def woven(*pieces):
@@ -82,26 +89,34 @@ def insert(steps, at, *extra):
     return steps[:at] + list(extra) + steps[at:]
 
 
-SCALAR = (
-    [("widen", h, 1, j) for h in (2, 3) for j in range(4)]
-    + [("keep",), ("widen", 4, 2, 0), ("weave", ("wv", 3, 0), 2), ("allow", "turn", 1, 0), ("allow", "turn", 1, 1), ("widen", 4, 2, 1)]
-    + [("turn", 1, 0), ("allow", "turn", 2, 0), ("allow", "turn", 2, 1), ("turn", 1, 1), ("widen", 4, 2, 2), ("widen", 4, 2, 3)]
-    + [("turn", 2, 0), ("allow", "turn", 3, 0), ("allow", "turn", 3, 1), ("turn", 2, 1), ("widen", 6, 1, 0), ("widen", 6, 1, 1)]
-    + [("turn", 3, 0), ("allow", "rows"), ("turn", 3, 1), ("widen", 6, 1, 2)]
-    + row_steps(1)
-    + insert(insert(row_steps(2), 8, ("weave", ("wv", 6, 0), 2)), 0, ("widen", 6, 1, 3))
-    + insert(row_steps(3), 6, *woven(*values((2, 3))))
-    + [("widen", 7, 1, j) for j in range(4)]
-    + [("state", 0)]
-    + insert(insert(row_steps(4), 8, ("state", 1), ("state", 2)), 6, ("weave", ("wv", 7, 0), 2))
-    + insert(insert(row_steps(5), 6, ("state", 3)), 4, *woven(*values((6, 0))))
-    + pair(6, 3)
-    + row_steps(6)
-    + pair(7, 2)
-    + [("state", 4)]
-    + pair(7, 3)
-)
-HEAD_START = 60
+def apart(steps, h, g):
+    low, high = woven(*values((h, g)))
+    return insert(insert(steps, A2, high), A1, low)
+
+
+def widening(h):
+    return [("widen", h, 1, j) for j in range(4)]
+
+
+CUT = 2
+C3 = 2
+C4 = 1
+SCALAR = [
+    widening(2)
+    + widening(3)
+    + widening(4)
+    + [("turn", 1, 0), ("widen", 5, 1, 0), ("turn", 1, 1)]
+    + widening(5)[1:]
+    + [("factors",), ("turn", 2, 0), ("turn", 2, 1)],
+    widening(6) + [("weave", ("wv", 3, 0), 2)] + insert(widening(7), 2, ("turn", 3, 0)) + [("turn", 3, 1)] + row_steps(1) + spare_first(2, 1)[:CUT],
+    apart(spare_first(2, 1)[CUT:], 3, 0) + spare_first(3, 1)[:C3],
+    apart(insert(spare_first(3, 1), 9, ("state", 0))[C3:], 3, 1) + row_steps(4)[:C4],
+    insert(insert(row_steps(4), 8, ("state", 1)), 4, *pair(4, 2))[C4:],
+    insert(insert(insert(row_steps(5), 7, ("state", 3)), 5, ("state", 2)), 3, *pair(6, 0)) + pair(6, 3)[:1],
+    pair(6, 3)[1:] + row_steps(6) + pair(7, 2)[::-1] + pair(7, 3) + [("state", 4)],
+]
+HEAD_START = 64
+LEAD = 16
 
 
 def span(step):
@@ -109,7 +124,7 @@ def span(step):
         return 8 * step[2] + 1
     if step[0] == "weave":
         return 8 * step[2]
-    return {"rows": 18, "turn": 16, "copy": 16, "state": 8, "keep": 4, "allow": 0}[step[0]]
+    return {"rows": 18, "turn": 16, "copy": 16, "state": 8, "factors": 6}[step[0]]
 
 
 def widths(n):
@@ -136,19 +151,19 @@ def tile_latent_kv_state_s7_kernel(tc, c, wk, wv_bytes, wv_scale, keep, write, o
         c_half = [const.tile([P, 2, L], BF16, name="c_half%d" % b, align_bytes=64) for b in range(2)]
         c_group = {g: const.tile([P, 4 * L], BF16, name="c_group%d" % g, align_bytes=64) for g in range(1, G)}
         wv_load = {first: const.tile([P, 4, (end - first) * DV], U8, name="wv_load%d" % first, align_bytes=64) for first, end in WV_LOADS}
-        early = const.tile([P, 4, 4 * DK + 2 * DV + PAD], BF16, name="early", align_bytes=64)
-        late = const.tile([P, 4, 2 * DV + 4 * DK + PAD], BF16, name="late", align_bytes=64)
-        wv_first = [const.tile([P, 4, DV], BF16, name="wv_first%d" % h, align_bytes=64) for h in range(2)]
-        wv_last = const.tile([P, 4, 2 * DV], BF16, name="wv_last", align_bytes=64)
+        early = const.tile([P, 4, 4 * DK + DV], BF16, name="early", align_bytes=64)
+        late = const.tile([P, 4, 2 * DV + 4 * DK], BF16, name="late", align_bytes=64)
+        first_rows = const.tile([P, 4, 4 * DV], BF16, name="first_rows", align_bytes=64)
+        wv_own = {h: const.tile([P, 4, DV], BF16, name="wv_own%d" % h, align_bytes=64) for h in (0, 1, 3)}
 
         def weight_rows(kind, h, n=1):
             if kind == "wk":
                 return early[:, :, h * DK : (h + n) * DK] if h < 4 else late[:, :, 2 * DV + (h - 4) * DK : 2 * DV + (h - 4 + n) * DK]
-            if h < 2:
-                return wv_first[h][:]
-            if h < 4:
-                return early[:, :, 4 * DK + (h - 2) * DV : 4 * DK + (h - 2 + n) * DV]
-            return late[:, :, (h - 4) * DV : (h - 4 + n) * DV] if h < 6 else wv_last[:, :, (h - 6) * DV : (h - 6 + n) * DV]
+            if h in wv_own:
+                return wv_own[h][:]
+            if h == 2:
+                return early[:, :, 4 * DK :]
+            return late[:, :, (h - 4) * DV : (h - 3) * DV] if h < 6 else first_rows[:, :, (h - 6) * DV : (h - 5) * DV]
 
         ctx.enter_context(tc.manual_schedule())
 
@@ -167,8 +182,9 @@ def tile_latent_kv_state_s7_kernel(tc, c, wk, wv_bytes, wv_scale, keep, write, o
         def load_wk(first, end):
             nc.sync.dma_start(out=weight_rows("wk", first, end - first), in_=wk_view[:, :, first * DK : end * DK])
 
-        def load_factor(i, src):
-            nc.sync.dma_start(out=factor_raw[:, i, :, :], in_=src.rearrange("(g p t) h -> p g (t h)", p=P, t=4))
+        def load_factors(first, end):
+            for i, src in enumerate((keep, write)):
+                nc.sync.dma_start(out=factor_raw[:, i, first:end, :], in_=src.rearrange("(g p t) h -> p g (t h)", p=P, t=4)[:, first:end, :])
 
         nc.scalar.dma_start(out=row_scale[:], in_=wv_scale.rearrange("(q j) o -> q (j o)", j=4))
         load_wv(*WV_LOADS[0])
@@ -176,14 +192,14 @@ def tile_latent_kv_state_s7_kernel(tc, c, wk, wv_bytes, wv_scale, keep, write, o
         load_c_half(1)
         load_wv(*WV_LOADS[1])
         load_wk(0, 4)
-        load_factor(1, write)
-        load_factor(0, keep)
-        load_wv(*WV_LOADS[2])
+        load_factors(0, 1)
         load_c(1)
+        load_wv(*WV_LOADS[2])
         load_c(2)
+        load_factors(1, G)
         load_wk(4, H)
-        load_c(3)
         load_wv(*WV_LOADS[3])
+        load_c(3)
 
         nc.vector.memset(warm[:], 0.0)
         nc.scalar.activation(out=warm[:], in_=warm[:], func=COPY)
@@ -297,13 +313,13 @@ def tile_latent_kv_state_s7_kernel(tc, c, wk, wv_bytes, wv_scale, keep, write, o
 
         def rows_tile(p):
             pieces = values(*ROWS[p])
-            tile = stage.tile([P, 4, len(pieces) * P + PAD], BF16, name="rows", bufs=ROW_BUFS, align_bytes=64)
+            tile = first_rows if p == 1 else stage.tile([P, 4, len(pieces) * P], BF16, name="rows", bufs=ROW_BUFS, align_bytes=64)
             for i, piece in enumerate(pieces):
-                rows[piece] = (tile, i)
+                rows[piece] = (tile, i + 4 * (p == 1))
 
         def rows_of(piece, n=1):
             if piece[0] != "v":
-                return weight_rows(piece[0], piece[1])[:, :, : n * P] if piece[0] == "wk" else weight_rows("wv", piece[1])[:, :, piece[2] * P : (piece[2] + n) * P]
+                return weight_rows("wk", piece[1], n) if piece[0] == "wk" else weight_rows("wv", piece[1])[:, :, piece[2] * P : (piece[2] + n) * P]
             tile, i = rows[piece]
             return tile[:, :, i * P : (i + n) * P]
 
@@ -354,85 +370,95 @@ def tile_latent_kv_state_s7_kernel(tc, c, wk, wv_bytes, wv_scale, keep, write, o
         def pool_interleave(r):
             pieces = POOL[r]
             word_tile("pool_words", pieces, 1)
-            if r == 0:
-                src = early[:, :, 2 * DK : 4 * DK + DV]
-            elif pieces[0][0] != "v":
-                src = late[:, :, : 2 * DV + 4 * DK]
-            else:
-                src = rows_of(pieces[0], len(pieces))
+            src = [early[:, :, 2 * DK :], late[:], first_rows[:]][r] if r < 3 else rows_of(pieces[0], len(pieces))
             dst, src = walk(words_of(pieces[0], len(pieces)), src)
             nc.gpsimd.tensor_scalar(out=dst, in0=src, scalar1=1.0, scalar2=0.0, op0=ALU.mult, op1=ALU.add)
 
-        def widen_factor(copy, i):
-            copy(out=factor[:, i, :, :, :], in_=factor_raw[:, i, :, :].rearrange("p g (t h) -> p g h t", t=4))
+        def widen_factors(copy, first, end):
+            copy(out=factor[:, :, first:end, :, :], in_=factor_raw[:, :, first:end, :].rearrange("p k g (t h) -> p k g h t", t=4))
 
-        def widen_keep():
-            widen_factor(nc.scalar.copy, 0)
+        def later_factors():
+            widen_factors(nc.scalar.copy, 1, G)
 
         def job(step):
             kind, args = step[0], step[1:]
             if kind in ("k", "v"):
                 return (project_piece, piece_out, (step,), [weight_of(step)] + latent_pieces(step[2]))
             if kind == "rows":
-                return (project_rows, rows_out, args, weight_pieces("wv", args[0]) + latent_pieces(args[1]) + [("rows",)])
+                return (project_rows, rows_out, args, weight_pieces("wv", args[0]) + latent_pieces(args[1]))
             if kind == "turn":
-                return (turn, turn_out, args, [step])
+                return (turn, turn_out, args, [])
             if kind == "weave":
                 piece = args[0]
-                need = [("rows", piece[1], piece[2], 1)] if piece[0] == "v" else [("wide", piece[1], 3)] if piece[0] == "wv" else [("late",)]
+                need = [("rows", piece[1], piece[2], 1)] if piece[0] == "v" else [("wide", piece[1], 3)] if piece[0] == "wv" else []
                 return (weave, weave_out, args, need)
             if kind == "state":
                 return (sum_state, store_state, args, keys(*[(args[0], g) for g in range(G)]) + values(*[(args[0], g) for g in range(G)]))
-            return (None, {"widen": widen, "copy": copy_piece}.get(kind, widen_keep), args, [])
+            return (None, {"widen": widen, "copy": copy_piece}.get(kind, later_factors), args, [])
 
-        v_jobs = []
-        s_jobs = [job(s) for s in SCALAR if job(s)[0] is not None]
-        v_full, s_full = [], []
+        def run_calls(p):
+            words = SCALAR_WORDS[p]
+            if p == 0:
+                return [POOL[0][:2], words, WINDOW[0][4:], POOL[0][2:], WINDOW[0][:4]]
+            if p == 1:
+                return [words[:4], words[8:], WINDOW[1][:4], words[4:8], POOL[1], WINDOW[1][4:]]
+            return calls(words) + [POOL[p], WINDOW[p]]
 
-        def refill(jobs, full, new_bank, depth, most):
-            for i in range(most):
-                if not (jobs and len(full) < depth and all(x in done for x in jobs[0][3])):
-                    break
-                fill, empty, args, need = jobs.pop(0)
-                bank = new_bank()
-                fill(bank, *args)
-                full.append(bank)
+        vector_steps = []
+        for p in range(ROUNDS):
+            vector_steps.extend([("window", p)] + WINDOW[p])
+            if p + 1 < ROUNDS:
+                vector_steps.extend(("call", pieces) for pieces in run_calls(p))
+        scalar_steps = [step for steps in SCALAR for step in steps]
+        full = {"vector": [], "scalar": []}
 
-        def refill_both(most):
-            refill(v_jobs, v_full, vector_bank, VECTOR_BANKS, most)
-            refill(s_jobs, s_full, scalar_bank, SCALAR_BANKS, 2)
+        reads, start = [], 0
+        for p in range(ROUNDS):
+            reads.extend((start + 16 * i - LEAD, len(reads) + i, "vector", step) for i, step in enumerate(WINDOW[p]))
+            at = start - (HEAD_START if p == 0 else 0)
+            for step in SCALAR[p]:
+                if job(step)[0] is not None:
+                    reads.append((at, len(reads), "scalar", step))
+                at = at + span(step)
+            start = max(at, start + 16 * len(WINDOW[p]) + 4 * (len(SCALAR_WORDS[p]) + len(POOL[p]) + len(WINDOW[p])))
+        fills = [read[2:] for read in sorted(reads)]
 
-        def run(step, full, most):
+        def empty_bank(step, ring):
             fill, empty, args, need = job(step)
             if fill is None:
                 empty(*args)
             else:
-                empty(full.pop(0), *args)
-            refill_both(most)
+                empty(full[ring].pop(0), *args)
 
-        steps = list(SCALAR)
-        clock = {"vector": HEAD_START, "scalar": 0}
+        def vector_step():
+            step = vector_steps.pop(0)
+            if step[0] == "window":
+                p = step[1]
+                word_tile("own_words", WINDOW[p], 2)
+                scalar_through(POOL[p] + [("rows",) + piece[1:3] for piece in POOL[p] if piece[0] == "v"])
+                pool_interleave(p)
+                done.add(step)
+            elif step[0] == "call":
+                scalar_through(step[1])
+                quantize(step[1])
+            else:
+                while step[2] and ("factors",) in scalar_steps:
+                    scalar_step()
+                empty_bank(step, "vector")
 
-        def scalar_step(most):
-            step = steps.pop(0)
-            clock["scalar"] = clock["scalar"] + span(step)
+        def scalar_step():
+            step = scalar_steps[0]
             if step[0] == "rows" and ("v", step[1], step[2], 0) not in rows:
-                rows_tile([p for p in range(ROUNDS) if step[1:3] in ROWS[p]][0])
+                p = [p for p in range(ROUNDS) if step[1:3] in ROWS[p]][0]
+                while p > 2 and ("window", p - 1) not in done:
+                    vector_step()
+                rows_tile(p)
             if step[0] in ("turn", "weave", "copy"):
                 first = ("c", step[1], 0) if step[0] == "turn" else step[1]
                 if first not in slot:
                     word_tile("scalar_words", [w for w in SCALAR_WORDS if first in w][0], 3)
-            if step[0] == "allow":
-                done.add(step[1:])
-                refill_both(0)
-            else:
-                run(step, s_full, most)
-            done.add(("step", step))
-
-        def scalar_until(length, most):
-            clock["vector"] = clock["vector"] + length
-            while steps and clock["scalar"] + span(steps[0]) <= clock["vector"] and (s_full or job(steps[0])[0] is None):
-                scalar_step(most)
+            scalar_steps.pop(0)
+            empty_bank(step, "scalar")
 
         def writes(step, pieces):
             if step[0] == "turn":
@@ -444,14 +470,24 @@ def tile_latent_kv_state_s7_kernel(tc, c, wk, wv_bytes, wv_scale, keep, write, o
             return step[0] in ("weave", "copy") and step[1] in pieces
 
         def scalar_through(pieces):
-            while any(writes(step, pieces) for step in steps):
-                scalar_step(0)
-            clock["vector"] = max(clock["vector"], clock["scalar"])
+            while any(writes(step, pieces) for step in scalar_steps):
+                scalar_step()
+
+        def fill_bank(ring, step):
+            fill, empty, args, need = job(step)
+            while len(full[ring]) == 4:
+                (vector_step if ring == "vector" else scalar_step)()
+            for x in need:
+                while x not in done:
+                    (scalar_step if x[0] in ("rows", "wide") else vector_step)()
+            bank = (vector_bank if ring == "vector" else scalar_bank)()
+            fill(bank, *args)
+            full[ring].append(bank)
 
         warm_up(4)
-        for h in range(2):
-            for j in range(4):
-                widen(h, 1, j, "vector" if j % 2 else "scalar")
+        for j in range(4):
+            widen(0, 1, j, "vector")
+            widen(1, 1, j)
         word_tile("head_c", latent_pieces(0), 1)
         word_tile("head_wv", weight_pieces("wv", 0) + weight_pieces("wv", 1), 1)
         word_tile("pool_words", [("wk", 0), ("wk", 1)], 1)
@@ -461,66 +497,51 @@ def tile_latent_kv_state_s7_kernel(tc, c, wk, wv_bytes, wv_scale, keep, write, o
         warm_up(2)
         for b in range(2):
             turn_out(turned[b], 0, b)
-        v_jobs.extend(job(s) for s in WINDOW[0])
         for h in range(2):
             interleave(nc.vector.tensor_copy, words_of(("wv", h, 0), 2), weight_rows("wv", h))
         quantize(weight_pieces("wv", 0))
         quantize(latent_pieces(0)[:2])
         quantize(weight_pieces("wv", 1))
         quantize(latent_pieces(0)[2:])
-        refill_both(VECTOR_BANKS)
-        interleave(nc.vector.tensor_copy, words_of(("wk", 0), 2), weight_rows("wk", 0, 2))
-        widen_factor(nc.vector.tensor_copy, 1)
-        quantize([("wk", 0), ("wk", 1)])
+        for h in range(2):
+            interleave(nc.vector.tensor_copy, words_of(("wk", h)), weight_rows("wk", h))
+        quantize([("wk", 0)])
+        widen_factors(nc.vector.tensor_copy, 0, 1)
+        quantize([("wk", 1)])
 
-        for p in range(ROUNDS):
-            word_tile("own_words", WINDOW[p], 2)
-            scalar_through(POOL[p] + [("wv", 4, 0)] * p if p < 2 else [("rows",) + piece[1:3] for piece in POOL[p]])
-            pool_interleave(p)
-            if p == ROUNDS - 1:
-                break
-            for step in WINDOW[p]:
-                scalar_until(16, 0)
-                run(step, v_full, 1)
-            v_jobs.extend(job(s) for s in WINDOW[p + 1])
-            run_calls = calls(SCALAR_WORDS[p]) + calls(POOL[p]) + [WINDOW[p]]
-            if p == 0:
-                run_calls = [POOL[0][:2], SCALAR_WORDS[0][:2], WINDOW[0][4:], SCALAR_WORDS[0][2:], POOL[0][2:], WINDOW[0][:4]]
-            for pieces in run_calls:
-                scalar_through(pieces)
-                scalar_until(4 * len(pieces), 1)
-                quantize(pieces)
-                refill_both(1)
-            refill_both(VECTOR_BANKS)
+        for ring, step in fills:
+            fill_bank(ring, step)
 
         last = H - 1
-        for i, step in enumerate(WINDOW[-1]):
-            scalar_until(16, 0)
-            run(step, v_full, 1)
-            if i == 0:
-                early_bank = vector_bank()
-                sum_state(early_bank, last - 2)
-            if i == 1:
-                before_last = vector_bank()
-                for g in range(G - 1):
-                    state_pass(before_last[:, :DV], last - 1, g, 0, 2, g == 0, False)
+        while len(full["vector"]) > 3:
+            vector_step()
+        early_bank = vector_bank()
+        sum_state(early_bank, last - 2)
+        vector_step()
+        before_last = vector_bank()
+        for g in range(G - 1):
+            state_pass(before_last[:, :DV], last - 1, g, 0, 2, g == 0, False)
+        while vector_steps:
+            vector_step()
         halves = [vector_bank(), vector_bank()]
         late_pieces = SCALAR_WORDS[-1]
 
         def last_passes(g):
             for f in range(2):
-                state_pass(halves[f][:, :P], last, g, f, 1, g == 2, g == G - 1)
+                state_pass(halves[f][:, :P], last, g, f, 1, g == 0, g == G - 1)
 
         scalar_through(late_pieces)
-        quantize(late_pieces[:4])
+        quantize(late_pieces[:2])
         state_pass(before_last[:, :DV], last - 1, G - 1, 0, 2, False, True)
-        quantize(WINDOW[-1])
-        last_passes(2)
         quantize(POOL[-1])
+        quantize(WINDOW[-1])
         last_passes(0)
         last_passes(1)
+        scalar_step()
         store_state(early_bank, last - 2)
         store_state(before_last, last - 1)
+        quantize(late_pieces[2:4])
+        last_passes(2)
         quantize(late_pieces[4:])
         last_passes(3)
         low = stage.tile([P, P], F32, name="result_half")

@@ -24,7 +24,7 @@ def keys(*units):
 
 
 def values(*units):
-    return [("v", h, g, f) for h, g in units for f in range(2)]
+    return [("v", unit[0], unit[1], f) for unit in units for f in (unit[2:] or range(2))]
 
 
 WV_LOADS = ((0, 2), (2, 4), (4, 6), (6, H))
@@ -33,7 +33,7 @@ WINDOW = [
     values((0, 0), (1, 0)) + keys((0, 0), (1, 0)),
     keys((2, 0), (3, 0), (0, 1), (1, 1)) + values((0, 1)) + keys((2, 1), (3, 1)),
     keys((0, 2), (1, 2)) + values((0, 2), (0, 3)) + keys((0, 3), (1, 3)),
-    keys((2, 2), (2, 3), (3, 2), (3, 3)) + values((1, 3)) + keys((4, 0), (4, 1)),
+    keys((2, 2), (2, 3), (3, 2), (3, 3)) + values((1, 3, 0)) + keys((4, 0), (4, 1)),
     keys((4, 2), (4, 3), (5, 0), (5, 1)) + values((4, 3)) + keys((5, 2), (5, 3)),
     keys((6, 0), (6, 1), (6, 2), (6, 3)) + values((6, 1), (6, 2)),
     keys((7, 0), (7, 1), (7, 2), (7, 3)),
@@ -41,7 +41,7 @@ WINDOW = [
 ROWS = [
     [],
     [(1, 1), (2, 0)],
-    [(2, 1), (1, 2), (2, 2), (2, 3), (3, 0)],
+    [(2, 1), (1, 2), (2, 2), (1, 3, 1), (3, 0), (2, 3)],
     [(3, 2), (3, 3), (4, 0), (4, 1), (3, 1), (4, 2)],
     [(5, 0), (5, 1), (5, 2), (5, 3), (6, 0)],
     [(7, 0), (7, 1), (6, 3), (7, 2)],
@@ -57,9 +57,9 @@ SCALAR_WORDS = [
     [("c", 1, t) for t in range(4)],
     [("c", g, t) for g in (2, 3) for t in range(4)] + [("wv", 3, 0), ("wv", 3, 1)],
     values((3, 0)),
+    values((2, 3)),
     values((3, 1)),
-    values((4, 2)),
-    values((6, 0)),
+    values((4, 2), (6, 0)),
     values((6, 3), (7, 2), (7, 3)),
 ]
 
@@ -69,12 +69,13 @@ A2 = 4
 
 
 def row_steps(p):
-    return [("rows", h, g, b) for h, g in ROWS[p] for b in range(2)]
+    return [step for unit in ROWS[p] for step in ([("half",) + unit] if len(unit) == 3 else [("rows",) + unit + (b,) for b in range(2)])]
 
 
 def spare_first(p, n):
     steps = row_steps(p)
-    return steps[8 : 8 + 2 * n] + steps[:8] + steps[8 + 2 * n :]
+    pooled = (len(POOL[p + 1]) + 1) // 2 + len(POOL[p + 1]) // 2
+    return steps[pooled : pooled + 2 * n] + steps[:pooled] + steps[pooled + 2 * n :]
 
 
 def woven(*pieces):
@@ -98,9 +99,34 @@ def widening(h):
     return [("widen", h, 1, j) for j in range(4)]
 
 
-CUT = 2
-C3 = 2
-C4 = 1
+def unit(h, g):
+    return [("rows", h, g, b) for b in range(2)]
+
+
+def low(h, g):
+    return woven(("v", h, g, 0))
+
+
+def high(h, g):
+    return woven(("v", h, g, 1))
+
+
+def copied(h, g):
+    return [("copy", ("v", h, g, 1))]
+
+
+def state(h):
+    return [("state", h)]
+
+
+LATER = (
+    unit(1, 1) + unit(2, 0) + unit(3, 0) + unit(2, 1) + low(3, 0) + unit(1, 2) + high(3, 0) + unit(2, 2) + [("half", 1, 3, 1)] + unit(2, 3)
+    + unit(3, 1) + low(2, 3) + copied(2, 3) + unit(3, 2) + unit(3, 3) + unit(4, 0) + low(3, 1) + unit(4, 1) + high(3, 1) + state(0)
+    + unit(5, 0) + unit(4, 2) + unit(5, 1) + low(4, 2) + unit(5, 2) + high(4, 2) + unit(5, 3) + state(1)
+    + unit(6, 0) + unit(7, 0) + low(6, 0) + copied(6, 0) + unit(7, 1) + state(2) + unit(6, 3) + state(3) + unit(7, 2) + low(6, 3)
+    + copied(6, 3) + unit(7, 3) + copied(7, 2) + low(7, 2) + low(7, 3) + copied(7, 3) + state(4)
+)
+CUTS = (0, 7, 20, 32, 45, 58, len(LATER))
 SCALAR = [
     widening(2)
     + widening(3)
@@ -108,15 +134,10 @@ SCALAR = [
     + [("turn", 1, 0), ("widen", 5, 1, 0), ("turn", 1, 1)]
     + widening(5)[1:]
     + [("factors",), ("turn", 2, 0), ("turn", 2, 1)],
-    widening(6) + [("weave", ("wv", 3, 0), 2)] + insert(widening(7), 2, ("turn", 3, 0)) + [("turn", 3, 1)] + row_steps(1) + spare_first(2, 1)[:CUT],
-    apart(spare_first(2, 1)[CUT:], 3, 0) + spare_first(3, 1)[:C3],
-    apart(insert(spare_first(3, 1), 9, ("state", 0))[C3:], 3, 1) + row_steps(4)[:C4],
-    insert(insert(row_steps(4), 8, ("state", 1)), 4, *pair(4, 2))[C4:],
-    insert(insert(insert(row_steps(5), 7, ("state", 3)), 5, ("state", 2)), 3, *pair(6, 0)) + pair(6, 3)[:1],
-    pair(6, 3)[1:] + row_steps(6) + pair(7, 2)[::-1] + pair(7, 3) + [("state", 4)],
-]
+    widening(6) + [("weave", ("wv", 3, 0), 2)] + insert(widening(7), 2, ("turn", 3, 0)) + [("turn", 3, 1)] + LATER[: CUTS[1]],
+] + [LATER[CUTS[p - 1] : CUTS[p]] for p in range(2, ROUNDS)]
 HEAD_START = 64
-LEAD = 16
+LEAD = 0
 
 
 def span(step):
@@ -124,7 +145,7 @@ def span(step):
         return 8 * step[2] + 1
     if step[0] == "weave":
         return 8 * step[2]
-    return {"rows": 18, "turn": 16, "copy": 16, "state": 8, "factors": 6}[step[0]]
+    return {"rows": 17, "half": 20, "turn": 16, "copy": 16, "state": 8, "factors": 6}[step[0]]
 
 
 def widths(n):
@@ -333,6 +354,13 @@ def tile_latent_kv_state_s7_kernel(tc, c, wk, wv_bytes, wv_scale, keep, write, o
                 nc.scalar.activation(out=rows_of(("v", h, g, 0), 2)[:, t, :], in_=bank[:, i * DV : (i + 1) * DV], func=COPY, scale=factor[:, 1, g, h, t : t + 1])
             done.add(("rows", h, g, b))
 
+        def project_half(bank, h, g, f):
+            project_piece(bank, ("v", h, g, f))
+
+        def half_out(bank, h, g, f):
+            for t in range(4):
+                nc.scalar.activation(out=rows_of(("v", h, g, f))[:, t, :], in_=bank[:, t * P : (t + 1) * P], func=COPY, scale=factor[:, 1, g, h, t : t + 1])
+
         def as_words(bank, n):
             return bank[:].bitcast(BF16)[:, : 4 * n * P].rearrange("p (n j) -> p n j", j=4)
 
@@ -386,6 +414,8 @@ def tile_latent_kv_state_s7_kernel(tc, c, wk, wv_bytes, wv_scale, keep, write, o
                 return (project_piece, piece_out, (step,), [weight_of(step)] + latent_pieces(step[2]))
             if kind == "rows":
                 return (project_rows, rows_out, args, weight_pieces("wv", args[0]) + latent_pieces(args[1]))
+            if kind == "half":
+                return (project_half, half_out, args, weight_pieces("wv", args[0]) + latent_pieces(args[1]))
             if kind == "turn":
                 return (turn, turn_out, args, [])
             if kind == "weave":
@@ -402,6 +432,8 @@ def tile_latent_kv_state_s7_kernel(tc, c, wk, wv_bytes, wv_scale, keep, write, o
                 return [POOL[0][:2], words, WINDOW[0][4:], POOL[0][2:], WINDOW[0][:4]]
             if p == 1:
                 return [words[:4], words[8:], WINDOW[1][:4], words[4:8], POOL[1], WINDOW[1][4:]]
+            if len(WINDOW[p]) == 7:
+                return calls(words) + [WINDOW[p][:4]] + calls(POOL[p]) + [WINDOW[p][4:]]
             return calls(words) + [POOL[p], WINDOW[p]]
 
         vector_steps = []
@@ -463,7 +495,7 @@ def tile_latent_kv_state_s7_kernel(tc, c, wk, wv_bytes, wv_scale, keep, write, o
         def writes(step, pieces):
             if step[0] == "turn":
                 return ("c", step[1], 2 * step[2]) in pieces
-            if step[0] == "rows":
+            if step[0] in ("rows", "half"):
                 return ("rows", step[1], step[2]) in pieces
             if step[0] == "widen":
                 return ("wv", step[1], 0) in pieces
@@ -503,10 +535,10 @@ def tile_latent_kv_state_s7_kernel(tc, c, wk, wv_bytes, wv_scale, keep, write, o
         quantize(latent_pieces(0)[:2])
         quantize(weight_pieces("wv", 1))
         quantize(latent_pieces(0)[2:])
-        for h in range(2):
-            interleave(nc.vector.tensor_copy, words_of(("wk", h)), weight_rows("wk", h))
-        quantize([("wk", 0)])
+        interleave(nc.vector.tensor_copy, words_of(("wk", 0)), weight_rows("wk", 0))
         widen_factors(nc.vector.tensor_copy, 0, 1)
+        interleave(nc.vector.tensor_copy, words_of(("wk", 1)), weight_rows("wk", 1))
+        quantize([("wk", 0)])
         quantize([("wk", 1)])
 
         for ring, step in fills:

@@ -16,7 +16,7 @@ T, L, H, DK, DV = 2048, 512, 8, 128, 256
 P = 128
 G = 4
 FLOPS = 2 * T * L * H * (DK + DV) + 2 * T * H * DK * DV
-VECTOR_BANKS, SCALAR_BANKS = 4, 4
+RING = 4
 
 
 def keys(*units):
@@ -27,7 +27,7 @@ def values(*units):
     return [("v", unit[0], unit[1], f) for unit in units for f in (unit[2:] or range(2))]
 
 
-WV_LOADS = ((0, 2), (2, 4), (4, 6), (6, H))
+WV_LOADS = ((0, 2), (2, 5), (5, H))
 ROUNDS = 7
 WINDOW = [
     values((0, 0), (1, 0)) + keys((0, 0), (1, 0)),
@@ -47,7 +47,6 @@ ROWS = [
     [(7, 0), (7, 1), (6, 3), (7, 2)],
     [(7, 3)],
 ]
-ROW_BUFS = 2
 POOL = [
     [("wk", 2), ("wk", 3), ("wv", 2, 0), ("wv", 2, 1)],
     [("wv", h, f) for h in (4, 5) for f in range(2)] + [("wk", h) for h in range(4, H)],
@@ -56,47 +55,20 @@ POOL = [
 SCALAR_WORDS = [
     [("c", 1, t) for t in range(4)],
     [("c", g, t) for g in (2, 3) for t in range(4)] + [("wv", 3, 0), ("wv", 3, 1)],
-    values((3, 0)),
-    values((2, 3)),
+    values((3, 0, 0)),
+    values((3, 0, 1), (2, 3)),
     values((3, 1)),
     values((4, 2), (6, 0)),
     values((6, 3), (7, 2), (7, 3)),
 ]
 
 
-A1 = 2
-A2 = 4
+def widening(h, n=1):
+    return [("widen", h, n, j) for j in range(4)]
 
 
-def row_steps(p):
-    return [step for unit in ROWS[p] for step in ([("half",) + unit] if len(unit) == 3 else [("rows",) + unit + (b,) for b in range(2)])]
-
-
-def spare_first(p, n):
-    steps = row_steps(p)
-    pooled = (len(POOL[p + 1]) + 1) // 2 + len(POOL[p + 1]) // 2
-    return steps[pooled : pooled + 2 * n] + steps[:pooled] + steps[pooled + 2 * n :]
-
-
-def woven(*pieces):
-    return [("weave", piece, 1) for piece in pieces]
-
-
-def pair(h, g):
-    return [("weave", ("v", h, g, 0), 1), ("copy", ("v", h, g, 1))]
-
-
-def insert(steps, at, *extra):
-    return steps[:at] + list(extra) + steps[at:]
-
-
-def apart(steps, h, g):
-    low, high = woven(*values((h, g)))
-    return insert(insert(steps, A2, high), A1, low)
-
-
-def widening(h):
-    return [("widen", h, 1, j) for j in range(4)]
+def turning(g, b):
+    return [("turn", g, b)]
 
 
 def unit(h, g):
@@ -104,11 +76,11 @@ def unit(h, g):
 
 
 def low(h, g):
-    return woven(("v", h, g, 0))
+    return [("weave", ("v", h, g, 0), 1)]
 
 
 def high(h, g):
-    return woven(("v", h, g, 1))
+    return [("weave", ("v", h, g, 1), 1)]
 
 
 def copied(h, g):
@@ -119,25 +91,25 @@ def state(h):
     return [("state", h)]
 
 
-LATER = (
-    unit(1, 1) + unit(2, 0) + unit(3, 0) + unit(2, 1) + low(3, 0) + unit(1, 2) + high(3, 0) + unit(2, 2) + [("half", 1, 3, 1)] + unit(2, 3)
-    + unit(3, 1) + low(2, 3) + copied(2, 3) + unit(3, 2) + unit(3, 3) + unit(4, 0) + low(3, 1) + unit(4, 1) + high(3, 1) + state(0)
-    + unit(5, 0) + unit(4, 2) + unit(5, 1) + low(4, 2) + unit(5, 2) + high(4, 2) + unit(5, 3) + state(1)
-    + unit(6, 0) + unit(7, 0) + low(6, 0) + copied(6, 0) + unit(7, 1) + state(2) + unit(6, 3) + state(3) + unit(7, 2) + low(6, 3)
-    + copied(6, 3) + unit(7, 3) + copied(7, 2) + low(7, 2) + low(7, 3) + copied(7, 3) + state(4)
+def between(pair, step):
+    return pair[:1] + step + pair[1:]
+
+
+SCALAR = (
+    widening(2) + widening(3, 2) + turning(1, 0) + between(widening(5), turning(1, 1))
+    + [("factors",)] + turning(2, 0) + turning(2, 1)
+    + widening(6, 2)[:2] + [("weave", ("wv", 3, 0), 2)] + widening(6, 2)[2:3] + turning(3, 0) + widening(6, 2)[3:] + turning(3, 1)
+    + unit(1, 1) + unit(2, 0) + unit(3, 0) + unit(2, 1) + low(3, 0)
+    + unit(1, 2) + unit(2, 2) + [("half", 1, 3, 1)] + between(unit(2, 3), high(3, 0))
+    + unit(3, 1) + low(2, 3) + copied(2, 3) + unit(3, 2) + state(0)
+    + unit(3, 3) + unit(4, 0) + low(3, 1) + unit(4, 1) + high(3, 1)
+    + unit(5, 0) + unit(4, 2) + unit(5, 1) + unit(5, 2) + low(4, 2) + between(unit(5, 3), state(1)) + high(4, 2)
+    + unit(6, 0) + unit(7, 0) + low(6, 0) + copied(6, 0) + unit(7, 1) + state(2)
+    + unit(6, 3) + state(3) + unit(7, 2) + low(6, 3) + copied(6, 3)
+    + unit(7, 3) + low(7, 2) + copied(7, 3) + high(7, 2) + low(7, 3) + state(4)
 )
-CUTS = (0, 7, 20, 32, 45, 58, len(LATER))
-SCALAR = [
-    widening(2)
-    + widening(3)
-    + widening(4)
-    + [("turn", 1, 0), ("widen", 5, 1, 0), ("turn", 1, 1)]
-    + widening(5)[1:]
-    + [("factors",), ("turn", 2, 0), ("turn", 2, 1)],
-    widening(6) + [("weave", ("wv", 3, 0), 2)] + insert(widening(7), 2, ("turn", 3, 0)) + [("turn", 3, 1)] + LATER[: CUTS[1]],
-] + [LATER[CUTS[p - 1] : CUTS[p]] for p in range(2, ROUNDS)]
+BANK, QUANTISED = 16, 4
 HEAD_START = 64
-LEAD = 0
 
 
 def span(step):
@@ -145,15 +117,11 @@ def span(step):
         return 8 * step[2] + 1
     if step[0] == "weave":
         return 8 * step[2]
-    return {"rows": 17, "half": 20, "turn": 16, "copy": 16, "state": 8, "factors": 6}[step[0]]
+    return {"rows": BANK + 1, "half": BANK + 2, "turn": BANK, "copy": BANK, "state": 8, "factors": 6}[step[0]]
 
 
 def widths(n):
-    if n in (8, 4, 3, 2, 1, 0):
-        return [n] if n else []
-    if n == 6:
-        return [3, 3]
-    return [8] + widths(n - 8) if n > 8 else [4] + widths(n - 4)
+    return [n] if n in (8, 4, 3, 2, 1) else [4] + widths(n - 4)
 
 
 def tile_latent_kv_state_s7_kernel(tc, c, wk, wv_bytes, wv_scale, keep, write, out):
@@ -173,18 +141,18 @@ def tile_latent_kv_state_s7_kernel(tc, c, wk, wv_bytes, wv_scale, keep, write, o
         c_group = {g: const.tile([P, 4 * L], BF16, name="c_group%d" % g, align_bytes=64) for g in range(1, G)}
         wv_load = {first: const.tile([P, 4, (end - first) * DV], U8, name="wv_load%d" % first, align_bytes=64) for first, end in WV_LOADS}
         early = const.tile([P, 4, 4 * DK + DV], BF16, name="early", align_bytes=64)
-        late = const.tile([P, 4, 2 * DV + 4 * DK], BF16, name="late", align_bytes=64)
+        late = const.tile([P, 4, 3 * DV + 4 * DK], BF16, name="late", align_bytes=64)
         first_rows = const.tile([P, 4, 4 * DV], BF16, name="first_rows", align_bytes=64)
-        wv_own = {h: const.tile([P, 4, DV], BF16, name="wv_own%d" % h, align_bytes=64) for h in (0, 1, 3)}
+        wv_own = {h: const.tile([P, 4, DV], BF16, name="wv_own%d" % h, align_bytes=64) for h in (0, 1)}
 
         def weight_rows(kind, h, n=1):
             if kind == "wk":
-                return early[:, :, h * DK : (h + n) * DK] if h < 4 else late[:, :, 2 * DV + (h - 4) * DK : 2 * DV + (h - 4 + n) * DK]
+                return early[:, :, h * DK : (h + n) * DK] if h < 4 else late[:, :, 3 * DV + (h - 4) * DK : 3 * DV + (h - 4 + n) * DK]
             if h in wv_own:
                 return wv_own[h][:]
             if h == 2:
                 return early[:, :, 4 * DK :]
-            return late[:, :, (h - 4) * DV : (h - 3) * DV] if h < 6 else first_rows[:, :, (h - 6) * DV : (h - 5) * DV]
+            return late[:, :, (h - 3) * DV : (h - 3 + n) * DV] if h < 6 else first_rows[:, :, (h - 6) * DV : (h - 6 + n) * DV]
 
         ctx.enter_context(tc.manual_schedule())
 
@@ -219,7 +187,6 @@ def tile_latent_kv_state_s7_kernel(tc, c, wk, wv_bytes, wv_scale, keep, write, o
         load_c(2)
         load_factors(1, G)
         load_wk(4, H)
-        load_wv(*WV_LOADS[3])
         load_c(3)
 
         nc.vector.memset(warm[:], 0.0)
@@ -228,10 +195,10 @@ def tile_latent_kv_state_s7_kernel(tc, c, wk, wv_bytes, wv_scale, keep, write, o
         nc.gpsimd.tensor_copy(out=ident_bf[:], in_=ident[:])
 
         def vector_bank():
-            return psum.tile([P, 512], F32, name="vector_bank", bufs=VECTOR_BANKS)
+            return psum.tile([P, 512], F32, name="vector_bank", bufs=RING)
 
         def scalar_bank():
-            return psum.tile([P, 512], F32, name="scalar_bank", bufs=SCALAR_BANKS)
+            return psum.tile([P, 512], F32, name="scalar_bank", bufs=RING)
 
         def warm_up(count):
             bank = vector_bank()
@@ -256,7 +223,6 @@ def tile_latent_kv_state_s7_kernel(tc, c, wk, wv_bytes, wv_scale, keep, write, o
             for i, piece in enumerate(pieces):
                 slot[piece] = (words, i)
                 codes[piece] = (cod, scl, i * P)
-            return words
 
         def words_of(piece, n=1):
             words, i = slot[piece]
@@ -271,15 +237,15 @@ def tile_latent_kv_state_s7_kernel(tc, c, wk, wv_bytes, wv_scale, keep, write, o
             nc.vector.quantize_mx(out=cod, scales=scl, in_=words_of(pieces[0], len(pieces)).rearrange("p n t -> p (n t)"))
             done.update(pieces)
 
-        def calls(pieces, split=None):
+        def calls(pieces):
             result, at = [], 0
-            for n in split or widths(len(pieces)):
+            for n in widths(len(pieces)):
                 result.append(pieces[at : at + n])
                 at = at + n
             return result
 
-        def weight_pieces(kind, h):
-            return [("wk", h)] if kind == "wk" else [("wv", h, 0), ("wv", h, 1)]
+        def value_weights(h):
+            return [("wv", h, 0), ("wv", h, 1)]
 
         def latent_pieces(g):
             return [("c", g, t) for t in range(4)]
@@ -334,13 +300,13 @@ def tile_latent_kv_state_s7_kernel(tc, c, wk, wv_bytes, wv_scale, keep, write, o
 
         def rows_tile(p):
             pieces = values(*ROWS[p])
-            tile = first_rows if p == 1 else stage.tile([P, 4, len(pieces) * P], BF16, name="rows", bufs=ROW_BUFS, align_bytes=64)
+            tile = first_rows if p == 1 else stage.tile([P, 4, len(pieces) * P], BF16, name="rows", bufs=2, align_bytes=64)
             for i, piece in enumerate(pieces):
                 rows[piece] = (tile, i + 4 * (p == 1))
 
         def rows_of(piece, n=1):
             if piece[0] != "v":
-                return weight_rows("wk", piece[1], n) if piece[0] == "wk" else weight_rows("wv", piece[1])[:, :, piece[2] * P : (piece[2] + n) * P]
+                return weight_rows("wv", piece[1])
             tile, i = rows[piece]
             return tile[:, :, i * P : (i + n) * P]
 
@@ -381,24 +347,24 @@ def tile_latent_kv_state_s7_kernel(tc, c, wk, wv_bytes, wv_scale, keep, write, o
             nc.tensor.matmul_mx(out=dst, lhsT=lhs, lhsT_scale=lhs_scale, rhs=rhs, rhs_scale=rhs_scale, start=start, stop=stop)
 
         def side_by_side(h, g):
-            low, high = codes["v", h, g, 0], codes["v", h, g, 1]
-            return low[0] is high[0] and high[2] == low[2] + P
+            first, second = codes["v", h, g, 0], codes["v", h, g, 1]
+            return first[0] is second[0] and second[2] == first[2] + P
 
-        def sum_state(bank, h, at=0):
+        def sum_state(bank, h):
             whole = [g for g in range(G) if side_by_side(h, g)]
             passes = [(g, 0, 2) for g in whole] + [(g, f, 1) for g in range(G) if g not in whole for f in range(2)]
             for i, (g, f, n) in enumerate(passes):
-                state_pass(bank[:, at + f * P : at + (f + n) * P], h, g, f, n, i == 0, i == len(passes) - 1)
+                state_pass(bank[:, f * P : (f + n) * P], h, g, f, n, i == 0, i == len(passes) - 1)
 
-        def store_state(bank, h, at=0):
+        def store_state(bank, h):
             result = stage.tile([P, DV], F32, name="result", bufs=H - 1)
-            nc.scalar.copy(out=result[:], in_=bank[:, at : at + DV])
+            nc.scalar.copy(out=result[:], in_=bank[:, :DV])
             nc.sync.dma_start(out=out[h], in_=result[:])
 
         def pool_interleave(r):
             pieces = POOL[r]
             word_tile("pool_words", pieces, 1)
-            src = [early[:, :, 2 * DK :], late[:], first_rows[:]][r] if r < 3 else rows_of(pieces[0], len(pieces))
+            src = [early[:, :, 2 * DK :], late[:, :, DV:], first_rows[:]][r] if r < 3 else rows_of(pieces[0], len(pieces))
             dst, src = walk(words_of(pieces[0], len(pieces)), src)
             nc.gpsimd.tensor_scalar(out=dst, in0=src, scalar1=1.0, scalar2=0.0, op0=ALU.mult, op1=ALU.add)
 
@@ -413,14 +379,14 @@ def tile_latent_kv_state_s7_kernel(tc, c, wk, wv_bytes, wv_scale, keep, write, o
             if kind in ("k", "v"):
                 return (project_piece, piece_out, (step,), [weight_of(step)] + latent_pieces(step[2]))
             if kind == "rows":
-                return (project_rows, rows_out, args, weight_pieces("wv", args[0]) + latent_pieces(args[1]))
+                return (project_rows, rows_out, args, value_weights(args[0]) + latent_pieces(args[1]))
             if kind == "half":
-                return (project_half, half_out, args, weight_pieces("wv", args[0]) + latent_pieces(args[1]))
+                return (project_half, half_out, args, value_weights(args[0]) + latent_pieces(args[1]))
             if kind == "turn":
                 return (turn, turn_out, args, [])
             if kind == "weave":
                 piece = args[0]
-                need = [("rows", piece[1], piece[2], 1)] if piece[0] == "v" else [("wide", piece[1], 3)] if piece[0] == "wv" else []
+                need = [("rows", piece[1], piece[2], 1)] if piece[0] == "v" else [("wide", piece[1], 3)]
                 return (weave, weave_out, args, need)
             if kind == "state":
                 return (sum_state, store_state, args, keys(*[(args[0], g) for g in range(G)]) + values(*[(args[0], g) for g in range(G)]))
@@ -431,7 +397,7 @@ def tile_latent_kv_state_s7_kernel(tc, c, wk, wv_bytes, wv_scale, keep, write, o
             if p == 0:
                 return [POOL[0][:2], words, WINDOW[0][4:], POOL[0][2:], WINDOW[0][:4]]
             if p == 1:
-                return [words[:4], words[8:], WINDOW[1][:4], words[4:8], POOL[1], WINDOW[1][4:]]
+                return [words[8:], words[:8], POOL[1], WINDOW[1]]
             if len(WINDOW[p]) == 7:
                 return calls(words) + [WINDOW[p][:4]] + calls(POOL[p]) + [WINDOW[p][4:]]
             return calls(words) + [POOL[p], WINDOW[p]]
@@ -441,18 +407,20 @@ def tile_latent_kv_state_s7_kernel(tc, c, wk, wv_bytes, wv_scale, keep, write, o
             vector_steps.extend([("window", p)] + WINDOW[p])
             if p + 1 < ROUNDS:
                 vector_steps.extend(("call", pieces) for pieces in run_calls(p))
-        scalar_steps = [step for steps in SCALAR for step in steps]
+        scalar_steps = list(SCALAR)
         full = {"vector": [], "scalar": []}
 
-        reads, start = [], 0
+        reads, start, ahead = [], 0, list(SCALAR)
         for p in range(ROUNDS):
-            reads.extend((start + 16 * i - LEAD, len(reads) + i, "vector", step) for i, step in enumerate(WINDOW[p]))
+            reads.extend((start + BANK * i, len(reads) + i, "vector", step) for i, step in enumerate(WINDOW[p]))
             at = start - (HEAD_START if p == 0 else 0)
-            for step in SCALAR[p]:
+            start = start + BANK * len(WINDOW[p]) + QUANTISED * (len(SCALAR_WORDS[p]) + len(POOL[p]) + len(WINDOW[p]))
+            while ahead and (2 * at + span(ahead[0]) <= 2 * start or p == ROUNDS - 1):
+                step = ahead.pop(0)
                 if job(step)[0] is not None:
                     reads.append((at, len(reads), "scalar", step))
                 at = at + span(step)
-            start = max(at, start + 16 * len(WINDOW[p]) + 4 * (len(SCALAR_WORDS[p]) + len(POOL[p]) + len(WINDOW[p])))
+            start = max(at, start)
         fills = [read[2:] for read in sorted(reads)]
 
         def empty_bank(step, ring):
@@ -498,7 +466,7 @@ def tile_latent_kv_state_s7_kernel(tc, c, wk, wv_bytes, wv_scale, keep, write, o
             if step[0] in ("rows", "half"):
                 return ("rows", step[1], step[2]) in pieces
             if step[0] == "widen":
-                return ("wv", step[1], 0) in pieces
+                return any(("wv", step[1] + i, 0) in pieces for i in range(step[2]))
             return step[0] in ("weave", "copy") and step[1] in pieces
 
         def scalar_through(pieces):
@@ -507,7 +475,7 @@ def tile_latent_kv_state_s7_kernel(tc, c, wk, wv_bytes, wv_scale, keep, write, o
 
         def fill_bank(ring, step):
             fill, empty, args, need = job(step)
-            while len(full[ring]) == 4:
+            while len(full[ring]) == RING:
                 (vector_step if ring == "vector" else scalar_step)()
             for x in need:
                 while x not in done:
@@ -521,7 +489,7 @@ def tile_latent_kv_state_s7_kernel(tc, c, wk, wv_bytes, wv_scale, keep, write, o
             widen(0, 1, j, "vector")
             widen(1, 1, j)
         word_tile("head_c", latent_pieces(0), 1)
-        word_tile("head_wv", weight_pieces("wv", 0) + weight_pieces("wv", 1), 1)
+        word_tile("head_wv", value_weights(0) + value_weights(1), 1)
         word_tile("pool_words", [("wk", 0), ("wk", 1)], 1)
         turned = [scalar_bank(), scalar_bank()]
         for b in range(2):
@@ -531,25 +499,29 @@ def tile_latent_kv_state_s7_kernel(tc, c, wk, wv_bytes, wv_scale, keep, write, o
             turn_out(turned[b], 0, b)
         for h in range(2):
             interleave(nc.vector.tensor_copy, words_of(("wv", h, 0), 2), weight_rows("wv", h))
-        quantize(weight_pieces("wv", 0))
+        quantize(value_weights(0))
         quantize(latent_pieces(0)[:2])
-        quantize(weight_pieces("wv", 1))
+        quantize(value_weights(1))
         quantize(latent_pieces(0)[2:])
-        interleave(nc.vector.tensor_copy, words_of(("wk", 0)), weight_rows("wk", 0))
+        for h in range(2):
+            interleave(nc.vector.tensor_copy, words_of(("wk", h)), weight_rows("wk", h))
         widen_factors(nc.vector.tensor_copy, 0, 1)
-        interleave(nc.vector.tensor_copy, words_of(("wk", 1)), weight_rows("wk", 1))
         quantize([("wk", 0)])
         quantize([("wk", 1)])
 
         for ring, step in fills:
-            fill_bank(ring, step)
+            if step not in SCALAR[-2:]:
+                fill_bank(ring, step)
 
         last = H - 1
-        while len(full["vector"]) > 3:
+        while len(vector_steps) > 3:
             vector_step()
         early_bank = vector_bank()
         sum_state(early_bank, last - 2)
-        vector_step()
+        for step in SCALAR[-2:]:
+            fill_bank("scalar", step)
+        while len(vector_steps) > 2:
+            vector_step()
         before_last = vector_bank()
         for g in range(G - 1):
             state_pass(before_last[:, :DV], last - 1, g, 0, 2, g == 0, False)
@@ -559,7 +531,7 @@ def tile_latent_kv_state_s7_kernel(tc, c, wk, wv_bytes, wv_scale, keep, write, o
         late_pieces = SCALAR_WORDS[-1]
 
         def last_passes(g):
-            for f in range(2):
+            for f in (1, 0):
                 state_pass(halves[f][:, :P], last, g, f, 1, g == 0, g == G - 1)
 
         scalar_through(late_pieces)
@@ -576,9 +548,9 @@ def tile_latent_kv_state_s7_kernel(tc, c, wk, wv_bytes, wv_scale, keep, write, o
         last_passes(2)
         quantize(late_pieces[4:])
         last_passes(3)
-        low = stage.tile([P, P], F32, name="result_half")
-        nc.scalar.copy(out=low[:], in_=halves[0][:, :P])
-        nc.sync.dma_start(out=out[last][:, :P], in_=low[:])
-        high = stage.tile([P, P], F32, name="result_half")
-        nc.vector.tensor_copy(out=high[:], in_=halves[1][:, :P])
-        nc.scalar.dma_start(out=out[last][:, P:], in_=high[:])
+        left = stage.tile([P, P], F32, name="result_half")
+        nc.scalar.copy(out=left[:], in_=halves[0][:, :P])
+        nc.sync.dma_start(out=out[last][:, :P], in_=left[:])
+        right = stage.tile([P, P], F32, name="result_half")
+        nc.vector.tensor_copy(out=right[:], in_=halves[1][:, :P])
+        nc.scalar.dma_start(out=out[last][:, P:], in_=right[:])

from contextlib import ExitStack

import concourse.mybir as mybir
from concourse.masks import make_identity

F32 = mybir.dt.float32
BF16 = mybir.dt.bfloat16
U32 = mybir.dt.uint32
U8 = mybir.dt.uint8
FP8 = mybir.dt.float8_e4m3fn
FP8X4 = mybir.dt.float8_e4m3fn_x4
ALU = mybir.AluOpType
COPY = mybir.ActivationFunctionType.Copy

T, L, H, DK, DV = 2048, 512, 8, 128, 256
P = 128
G = 4
FLOPS = 2 * T * L * H * (DK + DV) + 2 * T * H * DK * DV
RING = 4


def keys(*units):
    return [("k", h, g) for h, g in units]


def values(*units):
    return [("v", unit[0], unit[1], f) for unit in units for f in (unit[2:] or range(2))]


WV_LOADS = ((0, 2), (2, 5), (5, H))
ROUNDS = 7
WINDOW = [
    values((0, 0), (1, 0)) + keys((0, 0), (1, 0)),
    keys((2, 0), (3, 0), (0, 1), (1, 1)) + values((0, 1)) + keys((2, 1), (3, 1)),
    keys((0, 2), (1, 2)) + values((0, 2), (0, 3)) + keys((0, 3), (1, 3)),
    keys((2, 2), (2, 3), (3, 2), (3, 3)) + values((1, 3, 0)) + keys((4, 0), (4, 1)),
    keys((4, 2), (4, 3), (5, 0), (5, 1)) + values((4, 3)) + keys((5, 2), (5, 3)),
    keys((6, 0), (6, 1), (6, 2), (6, 3)) + values((6, 1), (6, 2)),
    keys((7, 0), (7, 1), (7, 2), (7, 3)),
]
ROWS = [
    [],
    [(1, 1), (2, 0)],
    [(2, 1), (1, 2), (2, 2), (1, 3, 1), (3, 0), (2, 3)],
    [(3, 2), (3, 3), (4, 0), (4, 1), (3, 1), (4, 2)],
    [(5, 0), (5, 1), (5, 2), (5, 3), (6, 0)],
    [(7, 0), (7, 1), (6, 3), (7, 2)],
    [(7, 3)],
]
POOL = [
    [("wk", 2), ("wk", 3), ("wv", 2, 0), ("wv", 2, 1)],
    [("wv", h, f) for h in (4, 5) for f in range(2)] + [("wk", h) for h in range(4, H)],
    [("wv", h, f) for h in (6, 7) for f in range(2)] + values(*ROWS[1]),
] + [values(*ROWS[r - 1])[: len(WINDOW[r])] for r in range(3, ROUNDS)]
SCALAR_WORDS = [
    [("c", 1, t) for t in range(4)],
    [("c", g, t) for g in (2, 3) for t in range(4)] + [("wv", 3, 0), ("wv", 3, 1)],
    values((3, 0, 0)),
    values((3, 0, 1), (2, 3)),
    values((3, 1)),
    values((4, 2), (6, 0)),
    values((6, 3), (7, 2), (7, 3)),
]


def widening(h, n=1):
    return [("widen", h, n, j) for j in range(4)]


def turning(g, b):
    return [("turn", g, b)]


def unit(h, g):
    return [("rows", h, g, b) for b in range(2)]


def low(h, g):
    return [("weave", ("v", h, g, 0), 1)]


def high(h, g):
    return [("weave", ("v", h, g, 1), 1)]


def copied(h, g):
    return [("copy", ("v", h, g, 1))]


def state(h):
    return [("state", h)]


def between(pair, step):
    return pair[:1] + step + pair[1:]


SCALAR = (
    widening(2) + widening(3, 2) + turning(1, 0) + between(widening(5), turning(1, 1))
    + [("factors",)] + turning(2, 0) + turning(2, 1)
    + widening(6, 2)[:2] + [("weave", ("wv", 3, 0), 2)] + widening(6, 2)[2:3] + turning(3, 0) + widening(6, 2)[3:] + turning(3, 1)
    + unit(1, 1) + unit(2, 0) + unit(3, 0) + unit(2, 1) + low(3, 0)
    + unit(1, 2) + unit(2, 2) + [("half", 1, 3, 1)] + between(unit(2, 3), high(3, 0))
    + unit(3, 1) + low(2, 3) + copied(2, 3) + unit(3, 2) + state(0)
    + unit(3, 3) + unit(4, 0) + low(3, 1) + unit(4, 1) + high(3, 1)
    + unit(5, 0) + unit(4, 2) + unit(5, 1) + unit(5, 2) + low(4, 2) + between(unit(5, 3), state(1)) + high(4, 2)
    + unit(6, 0) + unit(7, 0) + low(6, 0) + copied(6, 0) + unit(7, 1) + state(2)
    + unit(6, 3) + state(3) + unit(7, 2) + low(6, 3) + copied(6, 3)
    + unit(7, 3) + low(7, 2) + copied(7, 3) + high(7, 2) + low(7, 3) + state(4)
)
BANK, QUANTISED = 16, 4
HEAD_START = 64


def span(step):
    if step[0] == "widen":
        return 8 * step[2] + 1
    if step[0] == "weave":
        return 8 * step[2]
    return {"rows": BANK + 1, "half": BANK + 2, "turn": BANK, "copy": BANK, "state": 8, "factors": 6}[step[0]]


def widths(n):
    return [n] if n in (8, 4, 3, 2, 1) else [4] + widths(n - 4)


def tile_latent_kv_state_s7_kernel(tc, c, wk, wv_bytes, wv_scale, keep, write, out):
    nc = tc.nc
    with ExitStack() as ctx:
        const = ctx.enter_context(tc.tile_pool(name="const", bufs=1))
        stage = ctx.enter_context(tc.tile_pool(name="stage", bufs=2))
        psum = ctx.enter_context(tc.psum_pool(name="psum", bufs=1))

        ident = const.tile([P, P], F32, name="ident")
        ident_bf = const.tile([P, P], BF16, name="ident_bf")
        row_scale = const.tile([P, 4], F32, name="row_scale")
        warm = const.tile([P, 1], F32, name="warm")
        factor_raw = const.tile([P, 2, G, 4 * H], BF16, name="factor_raw")
        factor = const.tile([P, 2, G, H, 4], F32, name="factor")
        c_half = [const.tile([P, 2, L], BF16, name="c_half%d" % b, align_bytes=64) for b in range(2)]
        c_group = {g: const.tile([P, 4 * L], BF16, name="c_group%d" % g, align_bytes=64) for g in range(1, G)}
        wv_load = {first: const.tile([P, 4, (end - first) * DV], U8, name="wv_load%d" % first, align_bytes=64) for first, end in WV_LOADS}
        early = const.tile([P, 4, 4 * DK + DV], BF16, name="early", align_bytes=64)
        late = const.tile([P, 4, 3 * DV + 4 * DK], BF16, name="late", align_bytes=64)
        first_rows = const.tile([P, 4, 4 * DV], BF16, name="first_rows", align_bytes=64)
        wv_own = {h: const.tile([P, 4, DV], BF16, name="wv_own%d" % h, align_bytes=64) for h in (0, 1)}

        def weight_rows(kind, h, n=1):
            if kind == "wk":
                return early[:, :, h * DK : (h + n) * DK] if h < 4 else late[:, :, 3 * DV + (h - 4) * DK : 3 * DV + (h - 4 + n) * DK]
            if h in wv_own:
                return wv_own[h][:]
            if h == 2:
                return early[:, :, 4 * DK :]
            return late[:, :, (h - 3) * DV : (h - 3 + n) * DV] if h < 6 else first_rows[:, :, (h - 6) * DV : (h - 6 + n) * DV]

        ctx.enter_context(tc.manual_schedule())

        wv_view = wv_bytes.rearrange("(q j) w -> q j w", j=4)
        wk_view = wk.rearrange("(q j) w -> q j w", j=4)

        def load_c(g):
            nc.sync.dma_start(out=c_group[g][:], in_=c.rearrange("(g p t) l -> g p (t l)", p=P, t=4)[g])

        def load_c_half(b):
            nc.sync.dma_start(out=c_half[b][:], in_=c.rearrange("(g p b i) l -> g b p i l", p=P, b=2, i=2)[0, b])

        def load_wv(first, end):
            nc.sync.dma_start(out=wv_load[first][:], in_=wv_view[:, :, first * DV : end * DV])

        def load_wk(first, end):
            nc.sync.dma_start(out=weight_rows("wk", first, end - first), in_=wk_view[:, :, first * DK : end * DK])

        def load_factors(first, end):
            for i, src in enumerate((keep, write)):
                nc.sync.dma_start(out=factor_raw[:, i, first:end, :], in_=src.rearrange("(g p t) h -> p g (t h)", p=P, t=4)[:, first:end, :])

        nc.scalar.dma_start(out=row_scale[:], in_=wv_scale.rearrange("(q j) o -> q (j o)", j=4))
        load_wv(*WV_LOADS[0])
        load_c_half(0)
        load_c_half(1)
        load_wv(*WV_LOADS[1])
        load_wk(0, 4)
        load_factors(0, 1)
        load_c(1)
        load_wv(*WV_LOADS[2])
        load_c(2)
        load_factors(1, G)
        load_wk(4, H)
        load_c(3)

        nc.vector.memset(warm[:], 0.0)
        nc.scalar.activation(out=warm[:], in_=warm[:], func=COPY)
        make_identity(nc, ident[:])
        nc.gpsimd.tensor_copy(out=ident_bf[:], in_=ident[:])

        def vector_bank():
            return psum.tile([P, 512], F32, name="vector_bank", bufs=RING)

        def scalar_bank():
            return psum.tile([P, 512], F32, name="scalar_bank", bufs=RING)

        def warm_up(count):
            bank = vector_bank()
            for i in range(count):
                nc.tensor.matmul(out=bank[:, i * P : (i + 1) * P], lhsT=ident[:], rhs=ident[:], start=True, stop=True)

        def walk(dst, src):
            return dst.rearrange("p (c i) t -> p c t i", i=4), src.rearrange("p t (c i) -> p c t i", i=4)

        def interleave(copy, dst, src):
            dst, src = walk(dst, src)
            copy(out=dst, in_=src)

        done = set()
        codes = {}
        slot = {}

        def word_tile(tag, pieces, bufs):
            words = stage.tile([P, len(pieces), P, 4], BF16, name=tag, bufs=bufs, align_bytes=64)
            cod = const.tile([P, len(pieces) * P], U32, name="cod%d" % len(codes), align_bytes=64)
            scl = const.tile([P, len(pieces) * P], U8, name="scl%d" % len(codes), align_bytes=64)
            for i, piece in enumerate(pieces):
                slot[piece] = (words, i)
                codes[piece] = (cod, scl, i * P)

        def words_of(piece, n=1):
            words, i = slot[piece]
            return words[:, i : i + n, :, :].rearrange("p m n t -> p (m n) t")

        def operand(piece, n=1):
            cod, scl, at = codes[piece]
            return cod[:, at : at + n * P].bitcast(FP8X4), scl[:, at : at + n * P]

        def quantize(pieces):
            cod, scl = operand(pieces[0], len(pieces))
            nc.vector.quantize_mx(out=cod, scales=scl, in_=words_of(pieces[0], len(pieces)).rearrange("p n t -> p (n t)"))
            done.update(pieces)

        def calls(pieces):
            result, at = [], 0
            for n in widths(len(pieces)):
                result.append(pieces[at : at + n])
                at = at + n
            return result

        def value_weights(h):
            return [("wv", h, 0), ("wv", h, 1)]

        def latent_pieces(g):
            return [("c", g, t) for t in range(4)]

        def widen(h, n, j, engine="scalar"):
            first = max(f for f, e in WV_LOADS if f <= h)
            src = wv_load[first][:, j, (h - first) * DV : (h - first + n) * DV].bitcast(FP8)
            dst = weight_rows("wv", h, n)[:, j, :]
            if engine == "vector":
                nc.vector.tensor_scalar(out=dst, in0=src, scalar1=row_scale[:, j : j + 1], scalar2=None, op0=ALU.mult)
            else:
                nc.scalar.activation(out=dst, in_=src, func=COPY, scale=row_scale[:, j : j + 1])
            done.update(("wide", h + i, j) for i in range(n))

        def turn(bank, g, b):
            if g == 0:
                src = c_half[b][:].bitcast(F32)
            else:
                src = c_group[g][:].bitcast(F32).rearrange("p (t w) -> p t w", t=4)[:, 2 * b : 2 * b + 2, :]
            for i in range(2):
                for u in range(2):
                    col = (2 * i + u) * P
                    nc.tensor.transpose(bank[:, col : col + P], src[:, i, u::2], ident[:])

        def turn_out(bank, g, b):
            words, i = slot["c", g, 2 * b]
            nc.scalar.copy(out=words[:, i : i + 2, :, :].bitcast(F32), in_=bank[:].rearrange("q (i u p) -> q i p u", i=2, u=2))

        def project(dst, g, t, weight, n):
            lhs, lhs_scale = operand(("c", g, t))
            rhs, rhs_scale = operand(weight, n)
            nc.tensor.matmul_mx(out=dst, lhsT=lhs, lhsT_scale=lhs_scale, rhs=rhs, rhs_scale=rhs_scale, start=True, stop=True)

        def weight_of(piece):
            return ("wk", piece[1]) if piece[0] == "k" else ("wv", piece[1], piece[3])

        def project_piece(bank, piece):
            for t in range(4):
                project(bank[:, t * P : (t + 1) * P], piece[2], t, weight_of(piece), 1)

        def piece_out(bank, piece):
            h, g = piece[1:3]
            src = bank[:].rearrange("p (t n) -> p n t", t=4)
            if piece[0] == "k":
                by = factor[:, 0, g, h, :].unsqueeze(1).to_broadcast([P, P, 4])
                nc.vector.scalar_tensor_tensor(out=words_of(piece), in0=src, scalar=0.0, in1=by, op0=ALU.max, op1=ALU.mult)
            else:
                by = factor[:, 1, g, h, :].unsqueeze(1).to_broadcast([P, P, 4])
                nc.vector.tensor_tensor(out=words_of(piece), in0=src, in1=by, op=ALU.mult)

        rows = {}

        def rows_tile(p):
            pieces = values(*ROWS[p])
            tile = first_rows if p == 1 else stage.tile([P, 4, len(pieces) * P], BF16, name="rows", bufs=2, align_bytes=64)
            for i, piece in enumerate(pieces):
                rows[piece] = (tile, i + 4 * (p == 1))

        def rows_of(piece, n=1):
            if piece[0] != "v":
                return weight_rows("wv", piece[1])
            tile, i = rows[piece]
            return tile[:, :, i * P : (i + n) * P]

        def project_rows(bank, h, g, b):
            for i in range(2):
                project(bank[:, i * DV : (i + 1) * DV], g, 2 * b + i, ("wv", h, 0), 2)

        def rows_out(bank, h, g, b):
            for i in range(2):
                t = 2 * b + i
                nc.scalar.activation(out=rows_of(("v", h, g, 0), 2)[:, t, :], in_=bank[:, i * DV : (i + 1) * DV], func=COPY, scale=factor[:, 1, g, h, t : t + 1])
            done.add(("rows", h, g, b))

        def project_half(bank, h, g, f):
            project_piece(bank, ("v", h, g, f))

        def half_out(bank, h, g, f):
            for t in range(4):
                nc.scalar.activation(out=rows_of(("v", h, g, f))[:, t, :], in_=bank[:, t * P : (t + 1) * P], func=COPY, scale=factor[:, 1, g, h, t : t + 1])

        def as_words(bank, n):
            return bank[:].bitcast(BF16)[:, : 4 * n * P].rearrange("p (n j) -> p n j", j=4)

        def weave(bank, piece, n):
            dst = as_words(bank, n).rearrange("p n j -> p j n")
            for j in (0, 2):
                nc.tensor.matmul(out=dst[:, j : j + 2, :], lhsT=ident_bf[:], rhs=rows_of(piece, n)[:, j : j + 2, :], start=True, stop=True)

        def weave_out(bank, piece, n):
            nc.scalar.copy(out=words_of(piece, n), in_=as_words(bank, n))

        def copy_piece(piece):
            interleave(nc.scalar.copy, words_of(piece), rows_of(piece))

        def state_pass(dst, h, g, f, n, start, stop):
            lhs, lhs_scale = operand(("k", h, g))
            rhs, rhs_scale = operand(("v", h, g, f), n)
            nc.tensor.matmul_mx(out=dst, lhsT=lhs, lhsT_scale=lhs_scale, rhs=rhs, rhs_scale=rhs_scale, start=start, stop=stop)

        def side_by_side(h, g):
            first, second = codes["v", h, g, 0], codes["v", h, g, 1]
            return first[0] is second[0] and second[2] == first[2] + P

        def sum_state(bank, h):
            whole = [g for g in range(G) if side_by_side(h, g)]
            passes = [(g, 0, 2) for g in whole] + [(g, f, 1) for g in range(G) if g not in whole for f in range(2)]
            for i, (g, f, n) in enumerate(passes):
                state_pass(bank[:, f * P : (f + n) * P], h, g, f, n, i == 0, i == len(passes) - 1)

        def store_state(bank, h):
            result = stage.tile([P, DV], F32, name="result", bufs=H - 1)
            nc.scalar.copy(out=result[:], in_=bank[:, :DV])
            nc.sync.dma_start(out=out[h], in_=result[:])

        def pool_interleave(r):
            pieces = POOL[r]
            word_tile("pool_words", pieces, 1)
            src = [early[:, :, 2 * DK :], late[:, :, DV:], first_rows[:]][r] if r < 3 else rows_of(pieces[0], len(pieces))
            dst, src = walk(words_of(pieces[0], len(pieces)), src)
            nc.gpsimd.tensor_scalar(out=dst, in0=src, scalar1=1.0, scalar2=0.0, op0=ALU.mult, op1=ALU.add)

        def widen_factors(copy, first, end):
            copy(out=factor[:, :, first:end, :, :], in_=factor_raw[:, :, first:end, :].rearrange("p k g (t h) -> p k g h t", t=4))

        def later_factors():
            widen_factors(nc.scalar.copy, 1, G)

        def job(step):
            kind, args = step[0], step[1:]
            if kind in ("k", "v"):
                return (project_piece, piece_out, (step,), [weight_of(step)] + latent_pieces(step[2]))
            if kind == "rows":
                return (project_rows, rows_out, args, value_weights(args[0]) + latent_pieces(args[1]))
            if kind == "half":
                return (project_half, half_out, args, value_weights(args[0]) + latent_pieces(args[1]))
            if kind == "turn":
                return (turn, turn_out, args, [])
            if kind == "weave":
                piece = args[0]
                need = [("rows", piece[1], piece[2], 1)] if piece[0] == "v" else [("wide", piece[1], 3)]
                return (weave, weave_out, args, need)
            if kind == "state":
                return (sum_state, store_state, args, keys(*[(args[0], g) for g in range(G)]) + values(*[(args[0], g) for g in range(G)]))
            return (None, {"widen": widen, "copy": copy_piece}.get(kind, later_factors), args, [])

        def run_calls(p):
            words = SCALAR_WORDS[p]
            if p == 0:
                return [POOL[0][:2], words, WINDOW[0][4:], POOL[0][2:], WINDOW[0][:4]]
            if p == 1:
                return [words[8:], words[:8], POOL[1], WINDOW[1]]
            if len(WINDOW[p]) == 7:
                return calls(words) + [WINDOW[p][:4]] + calls(POOL[p]) + [WINDOW[p][4:]]
            return calls(words) + [POOL[p], WINDOW[p]]

        vector_steps = []
        for p in range(ROUNDS):
            vector_steps.extend([("window", p)] + WINDOW[p])
            if p + 1 < ROUNDS:
                vector_steps.extend(("call", pieces) for pieces in run_calls(p))
        scalar_steps = list(SCALAR)
        full = {"vector": [], "scalar": []}

        reads, start, ahead = [], 0, list(SCALAR)
        for p in range(ROUNDS):
            reads.extend((start + BANK * i, len(reads) + i, "vector", step) for i, step in enumerate(WINDOW[p]))
            at = start - (HEAD_START if p == 0 else 0)
            start = start + BANK * len(WINDOW[p]) + QUANTISED * (len(SCALAR_WORDS[p]) + len(POOL[p]) + len(WINDOW[p]))
            while ahead and (2 * at + span(ahead[0]) <= 2 * start or p == ROUNDS - 1):
                step = ahead.pop(0)
                if job(step)[0] is not None:
                    reads.append((at, len(reads), "scalar", step))
                at = at + span(step)
            start = max(at, start)
        fills = [read[2:] for read in sorted(reads)]

        def empty_bank(step, ring):
            fill, empty, args, need = job(step)
            if fill is None:
                empty(*args)
            else:
                empty(full[ring].pop(0), *args)

        def vector_step():
            step = vector_steps.pop(0)
            if step[0] == "window":
                p = step[1]
                word_tile("own_words", WINDOW[p], 2)
                scalar_through(POOL[p] + [("rows",) + piece[1:3] for piece in POOL[p] if piece[0] == "v"])
                pool_interleave(p)
                done.add(step)
            elif step[0] == "call":
                scalar_through(step[1])
                quantize(step[1])
            else:
                while step[2] and ("factors",) in scalar_steps:
                    scalar_step()
                empty_bank(step, "vector")

        def scalar_step():
            step = scalar_steps[0]
            if step[0] == "rows" and ("v", step[1], step[2], 0) not in rows:
                p = [p for p in range(ROUNDS) if step[1:3] in ROWS[p]][0]
                while p > 2 and ("window", p - 1) not in done:
                    vector_step()
                rows_tile(p)
            if step[0] in ("turn", "weave", "copy"):
                first = ("c", step[1], 0) if step[0] == "turn" else step[1]
                if first not in slot:
                    word_tile("scalar_words", [w for w in SCALAR_WORDS if first in w][0], 3)
            scalar_steps.pop(0)
            empty_bank(step, "scalar")

        def writes(step, pieces):
            if step[0] == "turn":
                return ("c", step[1], 2 * step[2]) in pieces
            if step[0] in ("rows", "half"):
                return ("rows", step[1], step[2]) in pieces
            if step[0] == "widen":
                return any(("wv", step[1] + i, 0) in pieces for i in range(step[2]))
            return step[0] in ("weave", "copy") and step[1] in pieces

        def scalar_through(pieces):
            while any(writes(step, pieces) for step in scalar_steps):
                scalar_step()

        def fill_bank(ring, step):
            fill, empty, args, need = job(step)
            while len(full[ring]) == RING:
                (vector_step if ring == "vector" else scalar_step)()
            for x in need:
                while x not in done:
                    (scalar_step if x[0] in ("rows", "wide") else vector_step)()
            bank = (vector_bank if ring == "vector" else scalar_bank)()
            fill(bank, *args)
            full[ring].append(bank)

        warm_up(4)
        for j in range(4):
            widen(0, 1, j, "vector")
            widen(1, 1, j)
        word_tile("head_c", latent_pieces(0), 1)
        word_tile("head_wv", value_weights(0) + value_weights(1), 1)
        word_tile("pool_words", [("wk", 0), ("wk", 1)], 1)
        turned = [scalar_bank(), scalar_bank()]
        for b in range(2):
            turn(turned[b], 0, b)
        warm_up(2)
        for b in range(2):
            turn_out(turned[b], 0, b)
        for h in range(2):
            interleave(nc.vector.tensor_copy, words_of(("wv", h, 0), 2), weight_rows("wv", h))
        quantize(value_weights(0))
        quantize(latent_pieces(0)[:2])
        quantize(value_weights(1))
        quantize(latent_pieces(0)[2:])
        for h in range(2):
            interleave(nc.vector.tensor_copy, words_of(("wk", h)), weight_rows("wk", h))
        widen_factors(nc.vector.tensor_copy, 0, 1)
        quantize([("wk", 0)])
        quantize([("wk", 1)])

        for ring, step in fills:
            if step not in SCALAR[-2:]:
                fill_bank(ring, step)

        last = H - 1
        while len(vector_steps) > 3:
            vector_step()
        early_bank = vector_bank()
        sum_state(early_bank, last - 2)
        for step in SCALAR[-2:]:
            fill_bank("scalar", step)
        while len(vector_steps) > 2:
            vector_step()
        before_last = vector_bank()
        for g in range(G - 1):
            state_pass(before_last[:, :DV], last - 1, g, 0, 2, g == 0, False)
        while vector_steps:
            vector_step()
        halves = [vector_bank(), vector_bank()]
        late_pieces = SCALAR_WORDS[-1]

        def last_passes(g):
            for f in (1, 0):
                state_pass(halves[f][:, :P], last, g, f, 1, g == 0, g == G - 1)

        scalar_through(late_pieces)
        quantize(late_pieces[:2])
        state_pass(before_last[:, :DV], last - 1, G - 1, 0, 2, False, True)
        quantize(POOL[-1])
        quantize(WINDOW[-1])
        last_passes(0)
        last_passes(1)
        scalar_step()
        store_state(early_bank, last - 2)
        store_state(before_last, last - 1)
        quantize(late_pieces[2:4])
        last_passes(2)
        quantize(late_pieces[4:])
        last_passes(3)
        left = stage.tile([P, P], F32, name="result_half")
        nc.scalar.copy(out=left[:], in_=halves[0][:, :P])
        nc.sync.dma_start(out=out[last][:, :P], in_=left[:])
        right = stage.tile([P, P], F32, name="result_half")
        nc.vector.tensor_copy(out=right[:], in_=halves[1][:, :P])
        nc.scalar.dma_start(out=out[last][:, P:], in_=right[:])
